import numpy as np
import ml_dtypes


def mxq(x, axis, fmt="e4m3"):
    dtype, down = {"e4m3": (ml_dtypes.float8_e4m3fn, 7), "e5m2": (ml_dtypes.float8_e5m2, 14)}[fmt]
    v = np.moveaxis(np.asarray(x, np.float32).astype(ml_dtypes.bfloat16).astype(np.float64), axis, -1)
    blocks = v.reshape(v.shape[:-1] + (-1, 32))
    amax = np.abs(blocks).max(-1, keepdims=True)
    byte = np.maximum(np.where(amax > 0, np.frexp(amax)[1] - 1 + 127, 0) - down, 1)
    scale = np.exp2(byte - 127.0)
    codes = (blocks / scale).astype(np.float32).astype(dtype).astype(np.float64)
    return np.moveaxis((codes * scale).reshape(v.shape), -1, axis)


WIDE = False


def mx_kscale(k):
    if not WIDE:
        return np.ones(k)
    levels = np.array([10, -10, 5, -5, 0])
    if k % 512:
        return np.exp2(np.random.permutation(np.resize(levels, k // 32))).repeat(32)
    a = np.empty((k // 512, 16))
    for p in range(k // 512):
        a[p, :8] = np.random.permutation(np.resize(levels, 8))
        for g in range(8):
            far = levels[np.abs(levels - a[p, g]) >= 10]
            a[p, g + 8] = far[np.random.randint(len(far))]
    return np.exp2(a.ravel()).repeat(32)


def f64(x):
    return np.asarray(x).astype(np.float64)


def striped(idx):
    return np.tile(np.asarray(idx).reshape(-1, 16).T, (8, 1)).astype(np.uint16)


def unstriped(offs):
    return offs[:16].T.reshape(-1).astype(np.int64)


E2M1 = np.array([0.0, 0.5, 1.0, 1.5, 2.0, 3.0, 4.0, 6.0, -0.0, -0.5, -1.0, -1.5, -2.0, -3.0, -4.0, -6.0])


def pack_weight(w, fmt):
    k, n = w.shape
    w = f64(np.asarray(w, np.float32).astype(ml_dtypes.bfloat16)).reshape(k // 32, 32, n)
    amax = np.abs(w).max(1)
    if fmt == "e4m3":
        byte = np.frexp(amax)[1] - 1 + 127 - 7
    else:
        mant, ex = np.frexp(amax / 6.0)
        byte = np.where(mant > 0.5, ex, ex - 1) + 127
    byte = np.clip(np.where(amax > 0, byte, 1), 1, 254)
    scaled = (w * np.exp2(127.0 - byte)[:, None, :]).reshape(k, n).astype(np.float32)
    by_word = np.ascontiguousarray(scaled.reshape(k // 512, 128, 4, n).transpose(0, 1, 3, 2))
    if fmt == "e4m3":
        words = by_word.astype(ml_dtypes.float8_e4m3fn).view(np.uint8)
    else:
        c = by_word.astype(ml_dtypes.float4_e2m1fn).view(np.uint8) & 0xF
        words = (c[..., 0::2] | (c[..., 1::2] << 4)).reshape(k // 512, 128, 2 * n)
    return np.ascontiguousarray(words), np.ascontiguousarray(byte.astype(np.uint8).reshape(k // 512, 16, n))


def unpack_weight(words, scales, fmt):
    g, _, n = scales.shape
    words = np.ascontiguousarray(words).reshape(g, 128, n, -1)
    if fmt == "e4m3":
        vals = words.view(ml_dtypes.float8_e4m3fn).astype(np.float64)
    else:
        nib = np.empty((g, 128, n, 4), np.uint8)
        nib[..., 0::2] = words & 0xF
        nib[..., 1::2] = words >> 4
        vals = E2M1[nib]
    vals = vals * np.repeat(np.exp2(scales.astype(np.float64) - 127.0), 8, axis=1)[..., None]
    return vals.transpose(0, 1, 3, 2).reshape(g * 512, n)


B, N, T, D, DV, NQ = 1, 1024, 4096, 1024, 128, 128
CAP = 2.0


def setup_inputs():
    n = np.random.standard_normal
    idx = np.random.permutation(T)[:B * N]
    s = mx_kscale(D)[:, None]
    u = np.ones(T)
    u[idx] = mx_kscale(B * N)
    r = np.random.uniform(0.5, 2.0, T)
    qp = [pack_weight(x, "e4m3") for x in n((B, D, NQ)) * s * (1.00 / np.sqrt(D))]
    k = n((D, T)) / s
    v = n((DV, T)) / (u * r)
    kp = pack_weight(k, "e2m1")
    return {
        "q_words": np.stack([x[0] for x in qp]),
        "q_scales": np.stack([x[1] for x in qp]),
        "k_words": np.ascontiguousarray(kp[0].reshape(D // 1024, 2, 128, T, 2).transpose(0, 2, 3, 1, 4)).reshape(D // 1024, 128, T, 4),
        "k_scales": kp[1],
        "vT": v.astype(np.float32),
        "vs": np.tile(u * r, (128, 1)).astype(np.float32),
        "og": n((B, NQ, DV)).astype(np.float32),
        "offs": striped(idx),
    }


def reference(q_words, q_scales, k_words, k_scales, vT, vs, og, offs):
    idx = unstriped(offs)
    k = unpack_weight(k_words.reshape(D // 1024, 128, T, 2, 2).transpose(0, 3, 1, 2, 4).reshape(D // 512, 128, 2 * T), k_scales, "e2m1")
    v = f64(vT)
    pick = lambda x: x[:, idx].reshape(x.shape[0], B, N).transpose(1, 0, 2)
    q = np.stack([unpack_weight(q_words[b], q_scales[b], "e4m3") for b in range(B)])
    score = q.transpose(0, 2, 1) @ pick(k)
    score = CAP * np.tanh(score / CAP)
    m = score.max(-1, keepdims=True)
    p = np.exp(score - m)
    total = p.sum(-1, keepdims=True)
    w = p * pick(f64(vs))[:, :1, :]
    y = mxq(w, 2, "e4m3") @ mxq(pick(v).transpose(0, 2, 1), 1, "e4m3")
    y = y / total
    y = y / (1.0 + np.exp(-f64(og)))
    return y

@@ -1,0 +1,191 @@
+from contextlib import ExitStack
+
+import concourse.mybir as mybir
+from concourse.masks import make_identity
+
+F32 = mybir.dt.float32
+BF16 = mybir.dt.bfloat16
+I32 = mybir.dt.int32
+U32 = mybir.dt.uint32
+U16 = mybir.dt.uint16
+U8 = mybir.dt.uint8
+FP8X4 = mybir.dt.float8_e4m3fn_x4
+FP4X4 = mybir.dt.float4_e2m1fn_x4
+ACT = mybir.ActivationFunctionType
+ALU = mybir.AluOpType
+
+P = 128
+N, T, D, DV, NQ = 1024, 4096, 1024, 128, 128
+CAP = 2.0
+PACK = 4
+HALF = P * PACK
+HALVES = N // HALF
+PASSES = D // HALF
+QUAD = 32
+SHIFT = 16
+
+FLOPS = 2 * NQ * N * (D + DV)
+BYTES = P * T * 4 + PASSES * 16 * T + DV * T * 4 + T * 4 + PASSES * (P * NQ * 4 + 16 * NQ) + 2 * NQ * DV * 4 + P * (N // 16) * 2
+
+
+def tile_attend_soft_cap_gate_topkq128n1024t4096_kernel(tc, q_words, q_scales, k_words, k_scales, vT, vs, og, offs, out):
+    nc = tc.nc
+    with ExitStack() as ctx:
+        held = ctx.enter_context(tc.tile_pool(name="held", bufs=1))
+        psum = ctx.enter_context(tc.psum_pool(name="psum", bufs=1))
+
+        def sb(name, shape, dtype):
+            return held.tile(shape, dtype, name=name, align_bytes=64)
+
+        def bank(name, shape, tag):
+            return psum.tile(shape, F32, name=name, tag=tag)
+
+        offsets = held.tile([P, N // 16], U16, name="offsets")
+        nc.sync.dma_start(offsets[:], offs)
+
+        def half_list(h):
+            return offsets[:, h * HALF // 16 : (h + 1) * HALF // 16]
+
+        key_pool = sb("key_pool", [P, T], I32)
+        nc.sync.dma_start(key_pool[:], k_words[0].rearrange("p t b -> p (t b)").bitcast(I32))
+        value_pool = sb("value_pool", [P, T], F32)
+        nc.sync.dma_start(value_pool[:], vT)
+
+        key_scale_pool = sb("key_scale_pool", [P, T], U8)
+        nc.vector.memset(key_scale_pool[:].bitcast(I32), 0)
+        for r in range(PACK):
+            nc.scalar.dma_start(
+                key_scale_pool[r:P:SHIFT, :].bitcast(I32),
+                k_scales[:, r::PACK, :].rearrange("o f t -> f o t").bitcast(I32),
+            )
+        ident = sb("ident", [P, P], F32)
+        make_identity(nc, ident[:])
+        q_codes = sb("q_codes", [P, PASSES, NQ], I32)
+        nc.gpsimd.dma_start(q_codes[:], q_words[0].rearrange("o p q r -> p o (q r)").bitcast(I32))
+        q_plane = sb("q_plane", [P, PASSES, NQ], U8)
+        nc.vector.memset(q_plane[:].rearrange("p o q -> p (o q)").bitcast(I32), 0)
+        for r in range(PACK):
+            nc.gpsimd.dma_start(
+                q_plane[r:P:QUAD, :, :].bitcast(I32),
+                q_scales[0][:, r::PACK, :].rearrange("o f q -> f o q").bitcast(I32),
+            )
+        gate_in = sb("gate_in", [P, DV], F32)
+        nc.gpsimd.dma_start(gate_in[:], og[0])
+        key_plane1 = sb("key_plane1", [P, N], U8)
+        nc.vector.memset(key_plane1[:].bitcast(I32), 0)
+
+        token_scale_pool = sb("token_scale_pool", [P, T], F32)
+        nc.vector.memset(token_scale_pool[:], 0.0)
+        nc.scalar.dma_start(token_scale_pool[0:1, :], vs[0:1, :])
+
+        gate_tanh = sb("gate_tanh", [P, DV], F32)
+        nc.scalar.activation(gate_tanh[:], gate_in[:], ACT.Tanh, scale=0.5)
+        gate = sb("gate", [P, DV], F32)
+        nc.scalar.activation(gate[:], gate_tanh[:], ACT.Copy, scale=0.5, bias=0.5)
+
+        key_plane0 = sb("key_plane0", [P, N], U8)
+        nc.vector.tensor_copy(key_plane0[:], key_scale_pool[:].indirect(offsets[:]))
+        nc.scalar.dma_start(key_plane1[0 : P - SHIFT, :].bitcast(I32), key_plane0[SHIFT:P, :].bitcast(I32))
+        key_planes = (key_plane0, key_plane1)
+
+        token_scale = sb("token_scale", [P, N], F32)
+        nc.vector.tensor_copy(token_scale[:], token_scale_pool[:].indirect(offsets[:]))
+        slot_scale = sb("slot_scale", [P, HALVES, PACK], F32)
+        for h in range(HALVES):
+            turned = bank(f"scale_turned{h}", [P, PACK, P], f"c{h}")
+            for t in range(PACK):
+                nc.tensor.transpose(turned[:, t, :], token_scale[:, h * HALF + t : (h + 1) * HALF : PACK], ident[:])
+            nc.scalar.copy(slot_scale[:, h, :], turned[:, :, 0])
+
+        capped = []
+        for h in range(HALVES):
+            cols = slice(h * HALF, (h + 1) * HALF)
+            pairs = sb(f"key_pairs{h}", [P, HALF], U32)
+            nc.vector.tensor_copy(pairs[:], key_pool[:].bitcast(U32).indirect(half_list(h)))
+            codes = sb(f"key_codes{h}", [P, PASSES, 2 * HALF], U8)
+            nc.vector.tensor_copy(codes[:].bitcast(U16), pairs[:].bitcast(U16).rearrange("p (n o) -> p o n", o=PASSES))
+            scores = bank(f"scores{h}", [P, HALF], f"a{h}")
+            for o in range(PASSES):
+                nc.tensor.matmul_mx(
+                    out=scores[:],
+                    lhsT=q_codes[:, o, :].bitcast(FP8X4),
+                    lhsT_scale=q_plane[:, o, :],
+                    rhs=codes[:, o, :].bitcast(FP4X4),
+                    rhs_scale=key_planes[o][:, cols],
+                    start=(o == 0),
+                    stop=(o == PASSES - 1),
+                )
+            tanh_h = sb(f"tanh{h}", [P, PACK, P], F32)
+            nc.scalar.activation(tanh_h[:], scores[:].rearrange("q (p t) -> q t p", t=PACK), ACT.Tanh, scale=1.0 / CAP)
+            capped.append(tanh_h)
+
+        neg_max = [sb(f"neg_max{h}", [P, 1], F32) for h in range(HALVES)]
+        neg_c = [sb(f"neg_c{h}", [P, HALF], F32) for h in range(HALVES)]
+        v_codes = sb("v_codes", [P, HALVES, DV], U32)
+        v_plane = sb("v_plane", [P, HALVES, DV], U8)
+        v_grouped = [sb(f"v_grouped{h}", [P, DV, PACK], BF16) for h in range(HALVES)]
+        for h in range(HALVES):
+            nc.vector.tensor_scalar(
+                neg_c[h][:], capped[h][:].rearrange("q t p -> q (t p)"), -CAP, neg_max[h - 1][:] if h else None,
+                ALU.mult, ALU.min, accum_out=neg_max[h][:],
+            )
+            values = sb(f"values{h}", [P, HALF], F32)
+            nc.vector.tensor_copy(values[:], value_pool[:].indirect(half_list(h)))
+            v_turned = bank(f"v_turned{h}", [P, PACK, DV], f"d{h}")
+            for t in range(PACK):
+                nc.tensor.transpose(v_turned[:, t, :], values[:, t::PACK], ident[:])
+            if h == 0:
+                nc.scalar.copy(v_grouped[h][:], v_turned[:].rearrange("p t e -> p e t"))
+            last_v_turned = v_turned
+
+        part_sum = [sb(f"part_sum{h}", [P, 1], F32) for h in range(HALVES)]
+        w_codes = sb("w_codes", [P, HALVES, NQ], U32)
+        w_plane = sb("w_plane", [P, HALVES, NQ], U8)
+        w_grouped = [sb(f"w_grouped{h}", [P, NQ, PACK], BF16) for h in range(HALVES)]
+        p_turned = []
+        for h in range(HALVES):
+            probs = sb(f"probs{h}", [P, PACK, P], F32)
+            nc.scalar.activation(
+                probs[:].rearrange("q t p -> q (t p)"), neg_c[h][:], ACT.Exp,
+                bias=neg_max[HALVES - 1][:], scale=-1.0, accum_out=part_sum[h][:],
+            )
+            turned_p = bank(f"p_turned{h}", [P, PACK, NQ], f"b{h}")
+            for t in range(PACK):
+                nc.tensor.transpose(turned_p[:, t, :], probs[:, t, :], ident[:])
+            p_turned.append(turned_p)
+        nc.scalar.copy(v_grouped[1][:], last_v_turned[:].rearrange("p t e -> p e t"))
+        total = sb("total", [P, 1], F32)
+        nc.scalar.activation(total[:], part_sum[0][:], ACT.Identity, bias=part_sum[1][:])
+
+        def weigh(h):
+            nc.vector.tensor_tensor(
+                w_grouped[h][:], p_turned[h][:].rearrange("p t q -> p q t"),
+                slot_scale[:, h, :].unsqueeze(1).to_broadcast([P, NQ, PACK]), ALU.mult,
+            )
+
+        def quantize(codes, plane, grouped, h):
+            nc.vector.quantize_mx(out=codes[:, h, :].bitcast(FP8X4), scales=plane[:, h, :], in_=grouped[h][:].rearrange("p x t -> p (x t)"))
+
+        inv_total = sb("inv_total", [P, 1], F32)
+        weigh(0)
+        quantize(v_codes, v_plane, v_grouped, 0)
+        weigh(1)
+        quantize(w_codes, w_plane, w_grouped, 0)
+        quantize(v_codes, v_plane, v_grouped, 1)
+        quantize(w_codes, w_plane, w_grouped, 1)
+        nc.vector.reciprocal(inv_total[:], total[:])
+
+        acc = bank("acc", [P, DV], "c0")
+        for h in range(HALVES):
+            nc.tensor.matmul_mx(
+                out=acc[:],
+                lhsT=w_codes[:, h, :].bitcast(FP8X4),
+                lhsT_scale=w_plane[:, h, :],
+                rhs=v_codes[:, h, :].bitcast(FP8X4),
+                rhs_scale=v_plane[:, h, :],
+                start=(h == 0),
+                stop=(h == HALVES - 1),
+            )
+        result = sb("result", [P, DV], F32)
+        nc.vector.scalar_tensor_tensor(result[:], acc[:], inv_total[:], gate[:], ALU.mult, ALU.mult)
+        nc.sync.dma_start(out[0], result[:])

@@ -1,7 +1,6 @@
 from contextlib import ExitStack
 
 import concourse.mybir as mybir
-from concourse.masks import make_identity
 
 F32 = mybir.dt.float32
 BF16 = mybir.dt.bfloat16
@@ -32,10 +31,11 @@ def tile_attend_soft_cap_gate_topkq128n1024t4096_kernel(tc, q_words, q_scales, k
     nc = tc.nc
     with ExitStack() as ctx:
         held = ctx.enter_context(tc.tile_pool(name="held", bufs=1))
+        shared = ctx.enter_context(tc.tile_pool(name="shared", bufs=1))
         psum = ctx.enter_context(tc.psum_pool(name="psum", bufs=1))
 
-        def sb(name, shape, dtype):
-            return held.tile(shape, dtype, name=name, align_bytes=64)
+        def sb(name, shape, dtype, tag=""):
+            return held.tile(shape, dtype, name=name, tag=tag or name, align_bytes=64)
 
         def bank(name, shape, tag):
             return psum.tile(shape, F32, name=name, tag=tag)
@@ -48,31 +48,40 @@ def tile_attend_soft_cap_gate_topkq128n1024t4096_kernel(tc, q_words, q_scales, k
 
         key_pool = sb("key_pool", [P, T], I32)
         nc.sync.dma_start(key_pool[:], k_words[0].rearrange("p t b -> p (t b)").bitcast(I32))
-        value_pool = sb("value_pool", [P, T], F32)
-        nc.sync.dma_start(value_pool[:], vT)
+        q_codes = sb("q_codes", [P, PASSES, NQ], I32)
+        nc.sync.dma_start(q_codes[:], q_words[0].rearrange("o p q r -> p o (q r)").bitcast(I32))
+        gate_in = sb("gate_in", [P, DV], F32)
+        nc.sync.dma_start(gate_in[:], og[0])
 
-        key_scale_pool = sb("key_scale_pool", [P, T], U8)
+        ones = sb("ones", [P, QUAD], F32)
+        nc.vector.memset(ones[:], 1.0)
+        key_scale_pool = shared.tile([P, T], U8, name="key_scale_pool", offset=2 * N)
         nc.vector.memset(key_scale_pool[:].bitcast(I32), 0)
         for r in range(PACK):
             nc.scalar.dma_start(
                 key_scale_pool[r:P:SHIFT, :].bitcast(I32),
                 k_scales[:, r::PACK, :].rearrange("o f t -> f o t").bitcast(I32),
             )
-        ident = sb("ident", [P, P], F32)
-        make_identity(nc, ident[:])
-        q_codes = sb("q_codes", [P, PASSES, NQ], I32)
-        nc.gpsimd.dma_start(q_codes[:], q_words[0].rearrange("o p q r -> p o (q r)").bitcast(I32))
+        column = sb("column", [P, QUAD], F32)
+        nc.vector.tensor_tensor_scan(column[:], ones[:], ones[:], 0.0, ALU.mult, ALU.add)
+
         q_plane = sb("q_plane", [P, PASSES, NQ], U8)
         nc.vector.memset(q_plane[:].rearrange("p o q -> p (o q)").bitcast(I32), 0)
         for r in range(PACK):
-            nc.gpsimd.dma_start(
+            nc.scalar.dma_start(
                 q_plane[r:P:QUAD, :, :].bitcast(I32),
                 q_scales[0][:, r::PACK, :].rearrange("o f q -> f o q").bitcast(I32),
             )
-        gate_in = sb("gate_in", [P, DV], F32)
-        nc.gpsimd.dma_start(gate_in[:], og[0])
+        row = sb("row", [P, QUAD], F32)
+        nc.vector.transpose(row[:], column[:])
+        ident = sb("ident", [P, P], F32)
+        nc.vector.memset(ident[:], 0.0)
         key_plane1 = sb("key_plane1", [P, N], U8)
         nc.vector.memset(key_plane1[:].bitcast(I32), 0)
+        block_ident = sb("block_ident", [P, QUAD], F32)
+        nc.vector.tensor_tensor(block_ident[:], column[:], row[:], ALU.is_equal)
+        for first in range(0, P, QUAD):
+            nc.scalar.copy(ident[first : first + QUAD, first : first + QUAD], block_ident[first : first + QUAD, :])
 
         token_scale_pool = sb("token_scale_pool", [P, T], F32)
         nc.vector.memset(token_scale_pool[:], 0.0)
@@ -85,25 +94,18 @@ def tile_attend_soft_cap_gate_topkq128n1024t4096_kernel(tc, q_words, q_scales, k
 
         key_plane0 = sb("key_plane0", [P, N], U8)
         nc.vector.tensor_copy(key_plane0[:], key_scale_pool[:].indirect(offsets[:]))
-        nc.scalar.dma_start(key_plane1[0 : P - SHIFT, :].bitcast(I32), key_plane0[SHIFT:P, :].bitcast(I32))
+        nc.sync.dma_start(key_plane1[0 : P - SHIFT, :].bitcast(I32), key_plane0[SHIFT:P, :].bitcast(I32))
+        value_pool = shared.tile([P, T], F32, name="value_pool", offset=4 * N)
+        nc.sync.dma_start(value_pool[:], vT)
         key_planes = (key_plane0, key_plane1)
 
-        token_scale = sb("token_scale", [P, N], F32)
-        nc.vector.tensor_copy(token_scale[:], token_scale_pool[:].indirect(offsets[:]))
-        slot_scale = sb("slot_scale", [P, HALVES, PACK], F32)
-        for h in range(HALVES):
-            turned = bank(f"scale_turned{h}", [P, PACK, P], f"c{h}")
-            for t in range(PACK):
-                nc.tensor.transpose(turned[:, t, :], token_scale[:, h * HALF + t : (h + 1) * HALF : PACK], ident[:])
-            nc.scalar.copy(slot_scale[:, h, :], turned[:, :, 0])
-
         capped = []
+        pairs = shared.tile([P, HALVES, HALF], U32, name="key_pairs", offset=0)
         for h in range(HALVES):
             cols = slice(h * HALF, (h + 1) * HALF)
-            pairs = sb(f"key_pairs{h}", [P, HALF], U32)
-            nc.vector.tensor_copy(pairs[:], key_pool[:].bitcast(U32).indirect(half_list(h)))
+            nc.vector.tensor_copy(pairs[:, h], key_pool[:].bitcast(U32).indirect(half_list(h)))
             codes = sb(f"key_codes{h}", [P, PASSES, 2 * HALF], U8)
-            nc.vector.tensor_copy(codes[:].bitcast(U16), pairs[:].bitcast(U16).rearrange("p (n o) -> p o n", o=PASSES))
+            nc.vector.tensor_copy(codes[:].bitcast(U16), pairs[:, h].bitcast(U16).rearrange("p (n o) -> p o n", o=PASSES))
             scores = bank(f"scores{h}", [P, HALF], f"a{h}")
             for o in range(PASSES):
                 nc.tensor.matmul_mx(
@@ -115,7 +117,7 @@ def tile_attend_soft_cap_gate_topkq128n1024t4096_kernel(tc, q_words, q_scales, k
                     start=(o == 0),
                     stop=(o == PASSES - 1),
                 )
-            tanh_h = sb(f"tanh{h}", [P, PACK, P], F32)
+            tanh_h = sb(f"tanh{h}", [P, PACK, P], F32, f"half{h}")
             nc.scalar.activation(tanh_h[:], scores[:].rearrange("q (p t) -> q t p", t=PACK), ACT.Tanh, scale=1.0 / CAP)
             capped.append(tanh_h)
 
@@ -124,19 +126,30 @@ def tile_attend_soft_cap_gate_topkq128n1024t4096_kernel(tc, q_words, q_scales, k
         v_codes = sb("v_codes", [P, HALVES, DV], U32)
         v_plane = sb("v_plane", [P, HALVES, DV], U8)
         v_grouped = [sb(f"v_grouped{h}", [P, DV, PACK], BF16) for h in range(HALVES)]
-        for h in range(HALVES):
+
+        def row_max(h):
             nc.vector.tensor_scalar(
                 neg_c[h][:], capped[h][:].rearrange("q t p -> q (t p)"), -CAP, neg_max[h - 1][:] if h else None,
                 ALU.mult, ALU.min, accum_out=neg_max[h][:],
             )
-            values = sb(f"values{h}", [P, HALF], F32)
-            nc.vector.tensor_copy(values[:], value_pool[:].indirect(half_list(h)))
-            v_turned = bank(f"v_turned{h}", [P, PACK, DV], f"d{h}")
-            for t in range(PACK):
-                nc.tensor.transpose(v_turned[:, t, :], values[:, t::PACK], ident[:])
-            if h == 0:
-                nc.scalar.copy(v_grouped[h][:], v_turned[:].rearrange("p t e -> p e t"))
-            last_v_turned = v_turned
+
+        row_max(0)
+        token_scale = sb("token_scale", [P, N], F32, "half0")
+        nc.vector.tensor_copy(token_scale[:], token_scale_pool[:].indirect(offsets[:]))
+        slot_scale = [sb(f"slot_scale{h}", [P, PACK], F32) for h in range(HALVES)]
+        for h in range(HALVES):
+            nc.scalar.dma_start(slot_scale[h][:], token_scale[0:1, h * HALF : (h + 1) * HALF].rearrange("o (p t) -> o p t", t=PACK))
+
+        row_max(1)
+        values = sb("values", [P, HALVES, 2, P, 2], BF16, "half1")
+        for h in range(HALVES):
+            nc.vector.tensor_copy(values[:, h].rearrange("e u p i -> e p u i"), value_pool[:].indirect(half_list(h)))
+
+        def turn_values(h):
+            turned_v = bank(f"v_turned{h}", [P, 2, DV], f"d{h}")
+            for u in range(2):
+                nc.tensor.transpose(turned_v[:, u, :], values[:, h, u].rearrange("e p i -> e (p i)").bitcast(F32), ident[:])
+            return turned_v
 
         part_sum = [sb(f"part_sum{h}", [P, 1], F32) for h in range(HALVES)]
         w_codes = sb("w_codes", [P, HALVES, NQ], U32)
@@ -153,14 +166,15 @@ def tile_attend_soft_cap_gate_topkq128n1024t4096_kernel(tc, q_words, q_scales, k
             for t in range(PACK):
                 nc.tensor.transpose(turned_p[:, t, :], probs[:, t, :], ident[:])
             p_turned.append(turned_p)
-        nc.scalar.copy(v_grouped[1][:], last_v_turned[:].rearrange("p t e -> p e t"))
+        for h in range(HALVES):
+            nc.scalar.copy(v_grouped[h][:].bitcast(F32), turn_values(h)[:].rearrange("p u e -> p e u"))
         total = sb("total", [P, 1], F32)
         nc.scalar.activation(total[:], part_sum[0][:], ACT.Identity, bias=part_sum[1][:])
 
         def weigh(h):
             nc.vector.tensor_tensor(
                 w_grouped[h][:], p_turned[h][:].rearrange("p t q -> p q t"),
-                slot_scale[:, h, :].unsqueeze(1).to_broadcast([P, NQ, PACK]), ALU.mult,
+                slot_scale[h][:].unsqueeze(1).to_broadcast([P, NQ, PACK]), ALU.mult,
             )
 
         def quantize(codes, plane, grouped, h):
@@ -168,8 +182,8 @@ def tile_attend_soft_cap_gate_topkq128n1024t4096_kernel(tc, q_words, q_scales, k
 
         inv_total = sb("inv_total", [P, 1], F32)
         weigh(0)
-        quantize(v_codes, v_plane, v_grouped, 0)
         weigh(1)
+        quantize(v_codes, v_plane, v_grouped, 0)
         quantize(w_codes, w_plane, w_grouped, 0)
         quantize(v_codes, v_plane, v_grouped, 1)
         quantize(w_codes, w_plane, w_grouped, 1)

@@ -46,6 +46,8 @@ def tile_attend_soft_cap_gate_topkq128n1024t4096_kernel(tc, q_words, q_scales, k
         def half_list(h):
             return offsets[:, h * HALF // 16 : (h + 1) * HALF // 16]
 
+        key_scale_pool = shared.tile([P, T], U8, name="key_scale_pool", offset=2 * N)
+        nc.sync.dma_start(key_scale_pool[0:QUAD, :].bitcast(I32), k_scales.rearrange("o f t -> f o t").bitcast(I32))
         key_pool = sb("key_pool", [P, T], I32)
         nc.sync.dma_start(key_pool[:], k_words[0].rearrange("p t b -> p (t b)").bitcast(I32))
         q_codes = sb("q_codes", [P, PASSES, NQ], I32)
@@ -55,16 +57,6 @@ def tile_attend_soft_cap_gate_topkq128n1024t4096_kernel(tc, q_words, q_scales, k
 
         ones = sb("ones", [P, QUAD], F32)
         nc.vector.memset(ones[:], 1.0)
-        key_scale_pool = shared.tile([P, T], U8, name="key_scale_pool", offset=2 * N)
-        nc.vector.memset(key_scale_pool[:].bitcast(I32), 0)
-        for r in range(PACK):
-            nc.scalar.dma_start(
-                key_scale_pool[r:P:SHIFT, :].bitcast(I32),
-                k_scales[:, r::PACK, :].rearrange("o f t -> f o t").bitcast(I32),
-            )
-        column = sb("column", [P, QUAD], F32)
-        nc.vector.tensor_tensor_scan(column[:], ones[:], ones[:], 0.0, ALU.mult, ALU.add)
-
         q_plane = sb("q_plane", [P, PASSES, NQ], U8)
         nc.vector.memset(q_plane[:].rearrange("p o q -> p (o q)").bitcast(I32), 0)
         for r in range(PACK):
@@ -72,38 +64,45 @@ def tile_attend_soft_cap_gate_topkq128n1024t4096_kernel(tc, q_words, q_scales, k
                 q_plane[r:P:QUAD, :, :].bitcast(I32),
                 q_scales[0][:, r::PACK, :].rearrange("o f q -> f o q").bitcast(I32),
             )
+        column = sb("column", [P, QUAD], F32)
+        nc.vector.tensor_tensor_scan(column[:], ones[:], ones[:], 0.0, ALU.mult, ALU.add)
+        nc.vector.memset(key_scale_pool[QUAD : 2 * QUAD, :].bitcast(I32), 0)
         row = sb("row", [P, QUAD], F32)
         nc.vector.transpose(row[:], column[:])
-        ident = sb("ident", [P, P], F32)
-        nc.vector.memset(ident[:], 0.0)
-        key_plane1 = sb("key_plane1", [P, N], U8)
-        nc.vector.memset(key_plane1[:].bitcast(I32), 0)
+        nc.vector.memset(key_scale_pool[2 * QUAD :, :].bitcast(I32), 0)
         block_ident = sb("block_ident", [P, QUAD], F32)
         nc.vector.tensor_tensor(block_ident[:], column[:], row[:], ALU.is_equal)
+        ident = sb("ident", [P, P], F32)
+        nc.vector.memset(ident[:], 0.0)
         for first in range(0, P, QUAD):
             nc.scalar.copy(ident[first : first + QUAD, first : first + QUAD], block_ident[first : first + QUAD, :])
+        key_planes = sb("key_planes", [P, PASSES, N], U8)
+        nc.vector.memset(key_planes[:].rearrange("p o n -> p (o n)").bitcast(I32), 0)
 
         token_scale_pool = sb("token_scale_pool", [P, T], F32)
-        nc.vector.memset(token_scale_pool[:], 0.0)
-        nc.scalar.dma_start(token_scale_pool[0:1, :], vs[0:1, :])
+        nc.vector.memset(token_scale_pool[:].bitcast(I32), 0)
+        nc.sync.dma_start(token_scale_pool[0:1, :], vs[0:1, :])
 
         gate_tanh = sb("gate_tanh", [P, DV], F32)
         nc.scalar.activation(gate_tanh[:], gate_in[:], ACT.Tanh, scale=0.5)
         gate = sb("gate", [P, DV], F32)
         nc.scalar.activation(gate[:], gate_tanh[:], ACT.Copy, scale=0.5, bias=0.5)
 
-        key_plane0 = sb("key_plane0", [P, N], U8)
-        nc.vector.tensor_copy(key_plane0[:], key_scale_pool[:].indirect(offsets[:]))
-        nc.sync.dma_start(key_plane1[0 : P - SHIFT, :].bitcast(I32), key_plane0[SHIFT:P, :].bitcast(I32))
+        key_scale_rows = sb("key_scale_rows", [P, N], U8)
+        nc.vector.tensor_copy(key_scale_rows[:], key_scale_pool[:].indirect(offsets[:]))
+        for quad in range(P // QUAD):
+            nc.sync.dma_start(
+                key_planes[quad * QUAD : quad * QUAD + PACK, :, :].bitcast(I32),
+                key_scale_rows[quad * PACK * PASSES : (quad + 1) * PACK * PASSES, :].bitcast(I32),
+            )
         value_pool = shared.tile([P, T], F32, name="value_pool", offset=4 * N)
         nc.sync.dma_start(value_pool[:], vT)
-        key_planes = (key_plane0, key_plane1)
 
         capped = []
         pairs = shared.tile([P, HALVES, HALF], U32, name="key_pairs", offset=0)
+        nc.vector.tensor_copy(pairs[:].rearrange("p h n -> p (h n)"), key_pool[:].bitcast(U32).indirect(offsets[:]))
         for h in range(HALVES):
             cols = slice(h * HALF, (h + 1) * HALF)
-            nc.vector.tensor_copy(pairs[:, h], key_pool[:].bitcast(U32).indirect(half_list(h)))
             codes = sb(f"key_codes{h}", [P, PASSES, 2 * HALF], U8)
             nc.vector.tensor_copy(codes[:].bitcast(U16), pairs[:, h].bitcast(U16).rearrange("p (n o) -> p o n", o=PASSES))
             scores = bank(f"scores{h}", [P, HALF], f"a{h}")
@@ -113,7 +112,7 @@ def tile_attend_soft_cap_gate_topkq128n1024t4096_kernel(tc, q_words, q_scales, k
                     lhsT=q_codes[:, o, :].bitcast(FP8X4),
                     lhsT_scale=q_plane[:, o, :],
                     rhs=codes[:, o, :].bitcast(FP4X4),
-                    rhs_scale=key_planes[o][:, cols],
+                    rhs_scale=key_planes[:, o, cols],
                     start=(o == 0),
                     stop=(o == PASSES - 1),
                 )
@@ -133,20 +132,22 @@ def tile_attend_soft_cap_gate_topkq128n1024t4096_kernel(tc, q_words, q_scales, k
                 ALU.mult, ALU.min, accum_out=neg_max[h][:],
             )
 
-        row_max(0)
-        token_scale = sb("token_scale", [P, N], F32, "half0")
+        token_scale = shared.tile([P, N], F32, name="token_scale", offset=0)
         nc.vector.tensor_copy(token_scale[:], token_scale_pool[:].indirect(offsets[:]))
         slot_scale = [sb(f"slot_scale{h}", [P, PACK], F32) for h in range(HALVES)]
         for h in range(HALVES):
-            nc.scalar.dma_start(slot_scale[h][:], token_scale[0:1, h * HALF : (h + 1) * HALF].rearrange("o (p t) -> o p t", t=PACK))
+            nc.sync.dma_start(slot_scale[h][:], token_scale[0:1, h * HALF : (h + 1) * HALF].rearrange("o (p t) -> o p t", t=PACK))
 
+        row_max(0)
         row_max(1)
         values = sb("values", [P, HALVES, 2, P, 2], BF16, "half1")
         for h in range(HALVES):
             nc.vector.tensor_copy(values[:, h].rearrange("e u p i -> e p u i"), value_pool[:].indirect(half_list(h)))
 
+        v_turned = bank("v_turned", [P, HALVES, 2, DV], "d")
+
         def turn_values(h):
-            turned_v = bank(f"v_turned{h}", [P, 2, DV], f"d{h}")
+            turned_v = v_turned[:, h]
             for u in range(2):
                 nc.tensor.transpose(turned_v[:, u, :], values[:, h, u].rearrange("e p i -> e (p i)").bitcast(F32), ident[:])
             return turned_v
@@ -167,7 +168,7 @@ def tile_attend_soft_cap_gate_topkq128n1024t4096_kernel(tc, q_words, q_scales, k
                 nc.tensor.transpose(turned_p[:, t, :], probs[:, t, :], ident[:])
             p_turned.append(turned_p)
         for h in range(HALVES):
-            nc.scalar.copy(v_grouped[h][:].bitcast(F32), turn_values(h)[:].rearrange("p u e -> p e u"))
+            nc.scalar.copy(v_grouped[h][:].bitcast(F32), turn_values(h).rearrange("p u e -> p e u"))
         total = sb("total", [P, 1], F32)
         nc.scalar.activation(total[:], part_sum[0][:], ACT.Identity, bias=part_sum[1][:])
 
@@ -182,8 +183,8 @@ def tile_attend_soft_cap_gate_topkq128n1024t4096_kernel(tc, q_words, q_scales, k
 
         inv_total = sb("inv_total", [P, 1], F32)
         weigh(0)
-        weigh(1)
         quantize(v_codes, v_plane, v_grouped, 0)
+        weigh(1)
         quantize(w_codes, w_plane, w_grouped, 0)
         quantize(v_codes, v_plane, v_grouped, 1)
         quantize(w_codes, w_plane, w_grouped, 1)

@@ -66,19 +66,19 @@ def tile_attend_soft_cap_gate_topkq128n1024t4096_kernel(tc, q_words, q_scales, k
             )
         column = sb("column", [P, QUAD], F32)
         nc.vector.tensor_tensor_scan(column[:], ones[:], ones[:], 0.0, ALU.mult, ALU.add)
-        nc.vector.memset(key_scale_pool[QUAD : 2 * QUAD, :].bitcast(I32), 0)
-        row = sb("row", [P, QUAD], F32)
-        nc.vector.transpose(row[:], column[:])
-        nc.vector.memset(key_scale_pool[2 * QUAD :, :].bitcast(I32), 0)
-        block_ident = sb("block_ident", [P, QUAD], F32)
-        nc.vector.tensor_tensor(block_ident[:], column[:], row[:], ALU.is_equal)
-        ident = sb("ident", [P, P], F32)
-        nc.vector.memset(ident[:], 0.0)
-        for first in range(0, P, QUAD):
-            nc.scalar.copy(ident[first : first + QUAD, first : first + QUAD], block_ident[first : first + QUAD, :])
         key_planes = sb("key_planes", [P, PASSES, N], U8)
         nc.vector.memset(key_planes[:].rearrange("p o n -> p (o n)").bitcast(I32), 0)
+        row = sb("row", [P, QUAD], F32)
+        nc.vector.transpose(row[:], column[:])
+        ident = sb("ident", [P, P], F32)
+        nc.vector.memset(ident[:], 0.0)
+        nc.vector.memset(key_scale_pool[QUAD : 2 * QUAD, :].bitcast(I32), 0)
+        block_ident = sb("block_ident", [P, QUAD], F32)
+        nc.vector.tensor_tensor(block_ident[:], column[:], row[:], ALU.is_equal)
+        for first in range(0, P, QUAD):
+            nc.scalar.copy(ident[first : first + QUAD, first : first + QUAD], block_ident[first : first + QUAD, :])
 
+        nc.vector.memset(key_scale_pool[2 * QUAD :, :].bitcast(I32), 0)
         token_scale_pool = sb("token_scale_pool", [P, T], F32)
         nc.vector.memset(token_scale_pool[:].bitcast(I32), 0)
         nc.sync.dma_start(token_scale_pool[0:1, :], vs[0:1, :])
@@ -122,9 +122,7 @@ def tile_attend_soft_cap_gate_topkq128n1024t4096_kernel(tc, q_words, q_scales, k
 
         neg_max = [sb(f"neg_max{h}", [P, 1], F32) for h in range(HALVES)]
         neg_c = [sb(f"neg_c{h}", [P, HALF], F32) for h in range(HALVES)]
-        v_codes = sb("v_codes", [P, HALVES, DV], U32)
-        v_plane = sb("v_plane", [P, HALVES, DV], U8)
-        v_grouped = [sb(f"v_grouped{h}", [P, DV, PACK], BF16) for h in range(HALVES)]
+        grouped = [sb(f"grouped{h}", [P, NQ + DV, PACK], BF16) for h in range(HALVES)]
 
         def row_max(h):
             nc.vector.tensor_scalar(
@@ -134,7 +132,7 @@ def tile_attend_soft_cap_gate_topkq128n1024t4096_kernel(tc, q_words, q_scales, k
 
         token_scale = shared.tile([P, N], F32, name="token_scale", offset=0)
         nc.vector.tensor_copy(token_scale[:], token_scale_pool[:].indirect(offsets[:]))
-        slot_scale = [sb(f"slot_scale{h}", [P, PACK], F32) for h in range(HALVES)]
+        slot_scale = [sb(f"slot_scale{h}", [P, PACK], F32, f"late{h}") for h in range(HALVES)]
         for h in range(HALVES):
             nc.sync.dma_start(slot_scale[h][:], token_scale[0:1, h * HALF : (h + 1) * HALF].rearrange("o (p t) -> o p t", t=PACK))
 
@@ -153,9 +151,6 @@ def tile_attend_soft_cap_gate_topkq128n1024t4096_kernel(tc, q_words, q_scales, k
             return turned_v
 
         part_sum = [sb(f"part_sum{h}", [P, 1], F32) for h in range(HALVES)]
-        w_codes = sb("w_codes", [P, HALVES, NQ], U32)
-        w_plane = sb("w_plane", [P, HALVES, NQ], U8)
-        w_grouped = [sb(f"w_grouped{h}", [P, NQ, PACK], BF16) for h in range(HALVES)]
         p_turned = []
         for h in range(HALVES):
             probs = sb(f"probs{h}", [P, PACK, P], F32)
@@ -167,37 +162,33 @@ def tile_attend_soft_cap_gate_topkq128n1024t4096_kernel(tc, q_words, q_scales, k
             for t in range(PACK):
                 nc.tensor.transpose(turned_p[:, t, :], probs[:, t, :], ident[:])
             p_turned.append(turned_p)
-        for h in range(HALVES):
-            nc.scalar.copy(v_grouped[h][:].bitcast(F32), turn_values(h).rearrange("p u e -> p e u"))
         total = sb("total", [P, 1], F32)
         nc.scalar.activation(total[:], part_sum[0][:], ACT.Identity, bias=part_sum[1][:])
+        for h in range(HALVES):
+            nc.scalar.copy(grouped[h][:, NQ:, :].bitcast(F32), turn_values(h).rearrange("p u e -> p e u"))
 
-        def weigh(h):
+        for h in range(HALVES):
             nc.vector.tensor_tensor(
-                w_grouped[h][:], p_turned[h][:].rearrange("p t q -> p q t"),
+                grouped[h][:, :NQ, :], p_turned[h][:].rearrange("p t q -> p q t"),
                 slot_scale[h][:].unsqueeze(1).to_broadcast([P, NQ, PACK]), ALU.mult,
             )
-
-        def quantize(codes, plane, grouped, h):
-            nc.vector.quantize_mx(out=codes[:, h, :].bitcast(FP8X4), scales=plane[:, h, :], in_=grouped[h][:].rearrange("p x t -> p (x t)"))
-
-        inv_total = sb("inv_total", [P, 1], F32)
-        weigh(0)
-        quantize(v_codes, v_plane, v_grouped, 0)
-        weigh(1)
-        quantize(w_codes, w_plane, w_grouped, 0)
-        quantize(v_codes, v_plane, v_grouped, 1)
-        quantize(w_codes, w_plane, w_grouped, 1)
+        slot_codes = sb("slot_codes", [P, HALVES, NQ + DV], U32)
+        slot_plane = sb("slot_plane", [P, HALVES, NQ + DV], U8)
+        for h in range(HALVES):
+            nc.vector.quantize_mx(
+                out=slot_codes[:, h, :].bitcast(FP8X4), scales=slot_plane[:, h, :], in_=grouped[h][:].rearrange("p x t -> p (x t)")
+            )
+        inv_total = sb("inv_total", [P, 1], F32, "late1")
         nc.vector.reciprocal(inv_total[:], total[:])
 
         acc = bank("acc", [P, DV], "c0")
         for h in range(HALVES):
             nc.tensor.matmul_mx(
                 out=acc[:],
-                lhsT=w_codes[:, h, :].bitcast(FP8X4),
-                lhsT_scale=w_plane[:, h, :],
-                rhs=v_codes[:, h, :].bitcast(FP8X4),
-                rhs_scale=v_plane[:, h, :],
+                lhsT=slot_codes[:, h, :NQ].bitcast(FP8X4),
+                lhsT_scale=slot_plane[:, h, :NQ],
+                rhs=slot_codes[:, h, NQ:].bitcast(FP8X4),
+                rhs_scale=slot_plane[:, h, NQ:],
                 start=(h == 0),
                 stop=(h == HALVES - 1),
             )

@@ -48,6 +48,8 @@ def tile_attend_soft_cap_gate_topkq128n1024t4096_kernel(tc, q_words, q_scales, k
 
         key_scale_pool = shared.tile([P, T], U8, name="key_scale_pool", offset=2 * N)
         nc.sync.dma_start(key_scale_pool[0:QUAD, :].bitcast(I32), k_scales.rearrange("o f t -> f o t").bitcast(I32))
+        scale_filler = sb("scale_filler", [P, QUAD], F32)
+        nc.sync.dma_start(scale_filler[:], vs[:, 0:QUAD])
         key_pool = sb("key_pool", [P, T], I32)
         nc.sync.dma_start(key_pool[:], k_words[0].rearrange("p t b -> p (t b)").bitcast(I32))
         q_codes = sb("q_codes", [P, PASSES, NQ], I32)
@@ -64,6 +66,11 @@ def tile_attend_soft_cap_gate_topkq128n1024t4096_kernel(tc, q_words, q_scales, k
                 q_plane[r:P:QUAD, :, :].bitcast(I32),
                 q_scales[0][:, r::PACK, :].rearrange("o f q -> f o q").bitcast(I32),
             )
+        token_scale_pool = sb("token_scale_pool", [P, T], F32, "scale_pool")
+        nc.scalar.activation(
+            token_scale_pool[:].rearrange("p (x j) -> p x j", j=QUAD),
+            scale_filler[:].unsqueeze(1).to_broadcast([P, T // QUAD, QUAD]), ACT.Copy,
+        )
         column = sb("column", [P, QUAD], F32)
         nc.vector.tensor_tensor_scan(column[:], ones[:], ones[:], 0.0, ALU.mult, ALU.add)
         key_planes = sb("key_planes", [P, PASSES, N], U8)
@@ -79,10 +86,6 @@ def tile_attend_soft_cap_gate_topkq128n1024t4096_kernel(tc, q_words, q_scales, k
             nc.scalar.copy(ident[first : first + QUAD, first : first + QUAD], block_ident[first : first + QUAD, :])
 
         nc.vector.memset(key_scale_pool[2 * QUAD :, :].bitcast(I32), 0)
-        token_scale_pool = sb("token_scale_pool", [P, T], F32)
-        nc.vector.memset(token_scale_pool[:].bitcast(I32), 0)
-        nc.sync.dma_start(token_scale_pool[0:1, :], vs[0:1, :])
-
         gate_tanh = sb("gate_tanh", [P, DV], F32)
         nc.scalar.activation(gate_tanh[:], gate_in[:], ACT.Tanh, scale=0.5)
         gate = sb("gate", [P, DV], F32)
@@ -95,6 +98,7 @@ def tile_attend_soft_cap_gate_topkq128n1024t4096_kernel(tc, q_words, q_scales, k
                 key_planes[quad * QUAD : quad * QUAD + PACK, :, :].bitcast(I32),
                 key_scale_rows[quad * PACK * PASSES : (quad + 1) * PACK * PASSES, :].bitcast(I32),
             )
+        nc.sync.dma_start(token_scale_pool[0:1, :], vs[0:1, :])
         value_pool = shared.tile([P, T], F32, name="value_pool", offset=4 * N)
         nc.sync.dma_start(value_pool[:], vT)
 
@@ -121,7 +125,6 @@ def tile_attend_soft_cap_gate_topkq128n1024t4096_kernel(tc, q_words, q_scales, k
             capped.append(tanh_h)
 
         neg_max = [sb(f"neg_max{h}", [P, 1], F32) for h in range(HALVES)]
-        neg_c = [sb(f"neg_c{h}", [P, HALF], F32) for h in range(HALVES)]
         grouped = [sb(f"grouped{h}", [P, NQ + DV, PACK], BF16) for h in range(HALVES)]
 
         def row_max(h):
@@ -136,6 +139,7 @@ def tile_attend_soft_cap_gate_topkq128n1024t4096_kernel(tc, q_words, q_scales, k
         for h in range(HALVES):
             nc.sync.dma_start(slot_scale[h][:], token_scale[0:1, h * HALF : (h + 1) * HALF].rearrange("o (p t) -> o p t", t=PACK))
 
+        neg_c = [sb("neg_c0", [P, HALF], F32, "scale_pool"), sb("neg_c1", [P, HALF], F32)]
         row_max(0)
         row_max(1)
         values = sb("values", [P, HALVES, 2, P, 2], BF16, "half1")

@@ -21,7 +21,10 @@ HALF = P * PACK
 HALVES = N // HALF
 PASSES = D // HALF
 QUAD = 32
-SHIFT = 16
+ROW_STEP = 4
+PIECE = HALF // 2
+LAST = 128
+BLOCK_AT = 4 * T + 2 * HALF
 
 FLOPS = 2 * NQ * N * (D + DV)
 BYTES = P * T * 4 + PASSES * 16 * T + DV * T * 4 + T * 4 + PASSES * (P * NQ * 4 + 16 * NQ) + 2 * NQ * DV * 4 + P * (N // 16) * 2
@@ -37,8 +40,11 @@ def tile_attend_soft_cap_gate_topkq128n1024t4096_kernel(tc, q_words, q_scales, k
         def sb(name, shape, dtype, tag=""):
             return held.tile(shape, dtype, name=name, tag=tag or name, align_bytes=64)
 
-        def bank(name, shape, tag):
-            return psum.tile(shape, F32, name=name, tag=tag)
+        def at(name, shape, dtype, offset):
+            return shared.tile(shape, dtype, name=name, offset=offset, align_bytes=64)
+
+        def bank(name, shape):
+            return psum.tile(shape, F32, name=name, tag=name)
 
         offsets = held.tile([P, N // 16], U16, name="offsets")
         nc.sync.dma_start(offsets[:], offs)
@@ -46,70 +52,78 @@ def tile_attend_soft_cap_gate_topkq128n1024t4096_kernel(tc, q_words, q_scales, k
         def half_list(h):
             return offsets[:, h * HALF // 16 : (h + 1) * HALF // 16]
 
-        key_scale_pool = shared.tile([P, T], U8, name="key_scale_pool", offset=2 * N)
-        nc.sync.dma_start(key_scale_pool[0:QUAD, :].bitcast(I32), k_scales.rearrange("o f t -> f o t").bitcast(I32))
-        scale_filler = sb("scale_filler", [P, QUAD], F32)
-        nc.sync.dma_start(scale_filler[:], vs[:, 0:QUAD])
+        gate_in = sb("gate_in", [P, DV], F32)
+        nc.sync.dma_start(gate_in[:], og[0])
+        q_plane = sb("q_plane", [P, PASSES, NQ], U8)
+        nc.vector.memset(q_plane[:].rearrange("p o q -> p (o q)").bitcast(I32), 0)
+        for r in range(PACK):
+            queue = nc.sync if r == PACK - 1 else nc.scalar
+            queue.dma_start(
+                q_plane[r:P:QUAD, :, :].bitcast(I32),
+                q_scales[0][:, r::PACK, :].rearrange("o f q -> f o q").bitcast(I32),
+            )
+        key_scale_pool = sb("key_scale_pool", [P, T], U8)
+        nc.vector.memset(key_scale_pool[:].bitcast(I32), 0)
+        nc.sync.dma_start(key_scale_pool[0:P:ROW_STEP, :].bitcast(I32), k_scales.rearrange("o f t -> f o t").bitcast(I32))
         key_pool = sb("key_pool", [P, T], I32)
         nc.sync.dma_start(key_pool[:], k_words[0].rearrange("p t b -> p (t b)").bitcast(I32))
         q_codes = sb("q_codes", [P, PASSES, NQ], I32)
         nc.sync.dma_start(q_codes[:], q_words[0].rearrange("o p q r -> p o (q r)").bitcast(I32))
-        gate_in = sb("gate_in", [P, DV], F32)
-        nc.sync.dma_start(gate_in[:], og[0])
-
-        ones = sb("ones", [P, QUAD], F32)
-        nc.vector.memset(ones[:], 1.0)
-        q_plane = sb("q_plane", [P, PASSES, NQ], U8)
-        nc.vector.memset(q_plane[:].rearrange("p o q -> p (o q)").bitcast(I32), 0)
-        for r in range(PACK):
-            nc.scalar.dma_start(
-                q_plane[r:P:QUAD, :, :].bitcast(I32),
-                q_scales[0][:, r::PACK, :].rearrange("o f q -> f o q").bitcast(I32),
-            )
-        token_scale_pool = sb("token_scale_pool", [P, T], F32, "scale_pool")
-        nc.scalar.activation(
-            token_scale_pool[:].rearrange("p (x j) -> p x j", j=QUAD),
-            scale_filler[:].unsqueeze(1).to_broadcast([P, T // QUAD, QUAD]), ACT.Copy,
-        )
-        column = sb("column", [P, QUAD], F32)
-        nc.vector.tensor_tensor_scan(column[:], ones[:], ones[:], 0.0, ALU.mult, ALU.add)
-        key_planes = sb("key_planes", [P, PASSES, N], U8)
-        nc.vector.memset(key_planes[:].rearrange("p o n -> p (o n)").bitcast(I32), 0)
-        row = sb("row", [P, QUAD], F32)
-        nc.vector.transpose(row[:], column[:])
-        ident = sb("ident", [P, P], F32)
-        nc.vector.memset(ident[:], 0.0)
-        nc.vector.memset(key_scale_pool[QUAD : 2 * QUAD, :].bitcast(I32), 0)
-        block_ident = sb("block_ident", [P, QUAD], F32)
-        nc.vector.tensor_tensor(block_ident[:], column[:], row[:], ALU.is_equal)
-        for first in range(0, P, QUAD):
-            nc.scalar.copy(ident[first : first + QUAD, first : first + QUAD], block_ident[first : first + QUAD, :])
-
-        nc.vector.memset(key_scale_pool[2 * QUAD :, :].bitcast(I32), 0)
+        value_pool = sb("value_pool", [P, T], F32)
+        nc.sync.dma_start(value_pool[:], vT)
+        token_scale_pool = at("token_scale_pool", [P, T], F32, 0)
+        nc.vector.memset(token_scale_pool[:], 0.0)
         gate_tanh = sb("gate_tanh", [P, DV], F32)
         nc.scalar.activation(gate_tanh[:], gate_in[:], ACT.Tanh, scale=0.5)
         gate = sb("gate", [P, DV], F32)
         nc.scalar.activation(gate[:], gate_tanh[:], ACT.Copy, scale=0.5, bias=0.5)
+        nc.scalar.dma_start(token_scale_pool[0:1, :], vs[0:1, :])
+        key_planes = sb("key_planes", [P, PASSES, N], U8)
+        nc.vector.memset(key_planes[:].rearrange("p o n -> p (o n)").bitcast(I32), 0)
+        ones = sb("ones", [P, QUAD], F32)
+        nc.vector.memset(ones[:], 1.0)
 
         key_scale_rows = sb("key_scale_rows", [P, N], U8)
         nc.vector.tensor_copy(key_scale_rows[:], key_scale_pool[:].indirect(offsets[:]))
         for quad in range(P // QUAD):
-            nc.sync.dma_start(
+            nc.scalar.dma_start(
                 key_planes[quad * QUAD : quad * QUAD + PACK, :, :].bitcast(I32),
-                key_scale_rows[quad * PACK * PASSES : (quad + 1) * PACK * PASSES, :].bitcast(I32),
+                key_scale_rows[quad * QUAD : (quad + 1) * QUAD : ROW_STEP, :].bitcast(I32),
             )
-        nc.sync.dma_start(token_scale_pool[0:1, :], vs[0:1, :])
-        value_pool = shared.tile([P, T], F32, name="value_pool", offset=4 * N)
-        nc.sync.dma_start(value_pool[:], vT)
 
+        token_scale = sb("token_scale", [P, N], F32)
+        nc.vector.tensor_copy(token_scale[:], token_scale_pool[:].indirect(offsets[:]))
+        slot_scale = [sb(f"slot_scale{h}", [P, PACK], F32, f"late{h}") for h in range(HALVES)]
+        for h in range(HALVES):
+            nc.sync.dma_start(slot_scale[h][:], token_scale[0:1, h * HALF : (h + 1) * HALF].rearrange("o (p t) -> o p t", t=PACK))
+
+        pairs = at("key_pairs", [P, HALF + PIECE], U32, 0)
         capped = []
-        pairs = shared.tile([P, HALVES, HALF], U32, name="key_pairs", offset=0)
-        nc.vector.tensor_copy(pairs[:].rearrange("p h n -> p (h n)"), key_pool[:].bitcast(U32).indirect(offsets[:]))
+        column = at("column", [P, QUAD], F32, 4096)
+        row = sb("row", [P, QUAD], F32)
+        block_ident = at("block_ident", [P, QUAD], F32, BLOCK_AT)
+        scratch = at("scratch", [P, 2 * HALF], F32, BLOCK_AT + 64)
         for h in range(HALVES):
             cols = slice(h * HALF, (h + 1) * HALF)
-            codes = sb(f"key_codes{h}", [P, PASSES, 2 * HALF], U8)
-            nc.vector.tensor_copy(codes[:].bitcast(U16), pairs[:, h].bitcast(U16).rearrange("p (n o) -> p o n", o=PASSES))
-            scores = bank(f"scores{h}", [P, HALF], f"a{h}")
+            first = (HALVES - 1 - h) * PIECE
+            nc.vector.tensor_copy(pairs[:, first : first + HALF], key_pool[:].bitcast(U32).indirect(half_list(h)))
+            if h == 0:
+                nc.vector.tensor_tensor_scan(column[:], ones[:], ones[:], 0.0, ALU.mult, ALU.add)
+            else:
+                nc.vector.transpose(row[:], column[:])
+            codes = sb(f"key_codes{h}", [P, PASSES, 2 * HALF], U8, f"codes{h}")
+            for n0 in range(0, HALF, PIECE):
+                nc.vector.tensor_copy(
+                    codes[:].bitcast(U16)[:, :, n0 : n0 + PIECE],
+                    pairs[:, first + n0 : first + n0 + PIECE].bitcast(U16).rearrange("p (n o) -> p o n", o=PASSES),
+                )
+            if h == 1:
+                nc.vector.tensor_tensor(block_ident[:], column[:], row[:], ALU.is_equal)
+                ident = sb("ident", [P, P], F32, "codes0")
+                nc.vector.memset(ident[:], 0.0)
+                for first in range(0, P, QUAD):
+                    nc.scalar.copy(ident[first : first + QUAD, first : first + QUAD], block_ident[first : first + QUAD, :])
+            scores = bank(f"scores{h}", [P, HALF])
             for o in range(PASSES):
                 nc.tensor.matmul_mx(
                     out=scores[:],
@@ -120,79 +134,88 @@ def tile_attend_soft_cap_gate_topkq128n1024t4096_kernel(tc, q_words, q_scales, k
                     start=(o == 0),
                     stop=(o == PASSES - 1),
                 )
-            tanh_h = sb(f"tanh{h}", [P, PACK, P], F32, f"half{h}")
-            nc.scalar.activation(tanh_h[:], scores[:].rearrange("q (p t) -> q t p", t=PACK), ACT.Tanh, scale=1.0 / CAP)
+            tanh_h = scratch[:, :HALF] if h else sb("tanh0", [P, HALF], F32)[:]
+            nc.scalar.activation(
+                tanh_h.rearrange("q (t p) -> q t p", t=PACK), scores[:].rearrange("q (p t) -> q t p", t=PACK), ACT.Tanh, scale=1.0 / CAP
+            )
             capped.append(tanh_h)
 
         neg_max = [sb(f"neg_max{h}", [P, 1], F32) for h in range(HALVES)]
-        grouped = [sb(f"grouped{h}", [P, NQ + DV, PACK], BF16) for h in range(HALVES)]
+        neg_c = [sb("neg_c0", [P, HALF], F32, "late_v")[:], scratch[:, HALF:]]
+        value_words = [
+            at("values0", [P, HALF // 2], F32, BLOCK_AT + 64 - 2 * HALF)[:],
+            scratch[:, HALF - (HALF - LAST) // 2 : HALF + LAST // 2],
+        ]
+        v_turned = [bank(f"v_turned{h}", [P, 2, DV]) for h in range(HALVES)]
+        v_grouped = [sb("v_grouped0", [P, DV, PACK], BF16, "late_v"), sb("v_grouped1", [P, DV, PACK], BF16)]
+        w_grouped = [sb(f"w_grouped{h}", [P, NQ, PACK], BF16) for h in range(HALVES)]
+        v_codes = [sb(f"v_codes{h}", [P, DV], U32) for h in range(HALVES)]
+        v_plane = [sb(f"v_plane{h}", [P, DV], U8) for h in range(HALVES)]
+        w_codes = [sb(f"w_codes{h}", [P, NQ], U32) for h in range(HALVES)]
+        w_plane = [sb(f"w_plane{h}", [P, NQ], U8) for h in range(HALVES)]
 
-        def row_max(h):
-            nc.vector.tensor_scalar(
-                neg_c[h][:], capped[h][:].rearrange("q t p -> q (t p)"), -CAP, neg_max[h - 1][:] if h else None,
-                ALU.mult, ALU.min, accum_out=neg_max[h][:],
-            )
-
-        token_scale = shared.tile([P, N], F32, name="token_scale", offset=0)
-        nc.vector.tensor_copy(token_scale[:], token_scale_pool[:].indirect(offsets[:]))
-        slot_scale = [sb(f"slot_scale{h}", [P, PACK], F32, f"late{h}") for h in range(HALVES)]
-        for h in range(HALVES):
-            nc.sync.dma_start(slot_scale[h][:], token_scale[0:1, h * HALF : (h + 1) * HALF].rearrange("o (p t) -> o p t", t=PACK))
-
-        neg_c = [sb("neg_c0", [P, HALF], F32, "scale_pool"), sb("neg_c1", [P, HALF], F32)]
-        row_max(0)
-        row_max(1)
-        values = sb("values", [P, HALVES, 2, P, 2], BF16, "half1")
-        for h in range(HALVES):
-            nc.vector.tensor_copy(values[:, h].rearrange("e u p i -> e p u i"), value_pool[:].indirect(half_list(h)))
-
-        v_turned = bank("v_turned", [P, HALVES, 2, DV], "d")
+        def gather_values(h, n0, n1):
+            listed = offsets[:, (h * HALF + n0) // 16 : (h * HALF + n1) // 16]
+            nc.vector.tensor_copy(value_words[h].bitcast(BF16)[:, n0:n1], value_pool[:].indirect(listed))
 
         def turn_values(h):
-            turned_v = v_turned[:, h]
+            words = value_words[h]
             for u in range(2):
-                nc.tensor.transpose(turned_v[:, u, :], values[:, h, u].rearrange("e p i -> e (p i)").bitcast(F32), ident[:])
-            return turned_v
+                nc.tensor.transpose(v_turned[h][:, u, :], words[:, u::2], ident[:])
+            nc.scalar.copy(v_grouped[h][:].bitcast(F32), v_turned[h][:].rearrange("p u e -> p e u"))
 
-        part_sum = [sb(f"part_sum{h}", [P, 1], F32) for h in range(HALVES)]
-        p_turned = []
+        def quantize(codes, plane, grouped):
+            nc.vector.quantize_mx(out=codes[:].bitcast(FP8X4), scales=plane[:], in_=grouped[:].rearrange("p x t -> p (x t)"))
+
         for h in range(HALVES):
-            probs = sb(f"probs{h}", [P, PACK, P], F32)
-            nc.scalar.activation(
-                probs[:].rearrange("q t p -> q (t p)"), neg_c[h][:], ACT.Exp,
-                bias=neg_max[HALVES - 1][:], scale=-1.0, accum_out=part_sum[h][:],
+            nc.vector.tensor_scalar(
+                neg_c[h], capped[h], -CAP, neg_max[h - 1][:] if h else None,
+                ALU.mult, ALU.min, accum_out=neg_max[h][:],
             )
-            turned_p = bank(f"p_turned{h}", [P, PACK, NQ], f"b{h}")
-            for t in range(PACK):
-                nc.tensor.transpose(turned_p[:, t, :], probs[:, t, :], ident[:])
+            gather_values(h, 0, HALF - h * LAST)
+
+        part_sum = []
+        p_turned = []
+        for h, cuts in enumerate([[0, PACK], [0, PACK // 2, PACK]]):
+            probs = sb(f"probs{h}", [P, PACK * P], F32)
+            turned_p = bank(f"p_turned{h}", [P, PACK, NQ])
+            for t0, t1 in zip(cuts, cuts[1:]):
+                part_sum.append(sb(f"part_sum{h}_{t0}", [P, 1], F32))
+                nc.scalar.activation(
+                    probs[:, t0 * P : t1 * P], neg_c[h][:, t0 * P : t1 * P], ACT.Exp,
+                    bias=neg_max[HALVES - 1][:], scale=-1.0, accum_out=part_sum[-1][:],
+                )
+                for t in range(t0, t1):
+                    nc.tensor.transpose(turned_p[:, t, :], probs[:, t * P : (t + 1) * P], ident[:])
             p_turned.append(turned_p)
+        turn_values(0)
+        gather_values(1, HALF - LAST, HALF)
+        turn_values(1)
+        subtotal = sb("subtotal", [P, 1], F32)
+        nc.scalar.activation(subtotal[:], part_sum[0][:], ACT.Identity, bias=part_sum[1][:])
         total = sb("total", [P, 1], F32)
-        nc.scalar.activation(total[:], part_sum[0][:], ACT.Identity, bias=part_sum[1][:])
-        for h in range(HALVES):
-            nc.scalar.copy(grouped[h][:, NQ:, :].bitcast(F32), turn_values(h).rearrange("p u e -> p e u"))
+        nc.scalar.activation(total[:], subtotal[:], ACT.Identity, bias=part_sum[2][:])
 
         for h in range(HALVES):
             nc.vector.tensor_tensor(
-                grouped[h][:, :NQ, :], p_turned[h][:].rearrange("p t q -> p q t"),
+                w_grouped[h][:], p_turned[h][:].rearrange("p t q -> p q t"),
                 slot_scale[h][:].unsqueeze(1).to_broadcast([P, NQ, PACK]), ALU.mult,
             )
-        slot_codes = sb("slot_codes", [P, HALVES, NQ + DV], U32)
-        slot_plane = sb("slot_plane", [P, HALVES, NQ + DV], U8)
-        for h in range(HALVES):
-            nc.vector.quantize_mx(
-                out=slot_codes[:, h, :].bitcast(FP8X4), scales=slot_plane[:, h, :], in_=grouped[h][:].rearrange("p x t -> p (x t)")
-            )
+        quantize(v_codes[0], v_plane[0], v_grouped[0])
+        quantize(w_codes[0], w_plane[0], w_grouped[0])
+        quantize(w_codes[1], w_plane[1], w_grouped[1])
+        quantize(v_codes[1], v_plane[1], v_grouped[1])
         inv_total = sb("inv_total", [P, 1], F32, "late1")
         nc.vector.reciprocal(inv_total[:], total[:])
 
-        acc = bank("acc", [P, DV], "c0")
+        acc = bank("acc", [P, DV])
         for h in range(HALVES):
             nc.tensor.matmul_mx(
                 out=acc[:],
-                lhsT=slot_codes[:, h, :NQ].bitcast(FP8X4),
-                lhsT_scale=slot_plane[:, h, :NQ],
-                rhs=slot_codes[:, h, NQ:].bitcast(FP8X4),
-                rhs_scale=slot_plane[:, h, NQ:],
+                lhsT=w_codes[h][:].bitcast(FP8X4),
+                lhsT_scale=w_plane[h][:],
+                rhs=v_codes[h][:].bitcast(FP8X4),
+                rhs_scale=v_plane[h][:],
                 start=(h == 0),
                 stop=(h == HALVES - 1),
             )

@@ -24,6 +24,8 @@ QUAD = 32
 ROW_STEP = 4
 PIECE = HALF // 2
 LAST = 128
+KEYS_FIRST = 2304
+SCALE_AT = 6 * T
 BLOCK_AT = 4 * T + 2 * HALF
 
 FLOPS = 2 * NQ * N * (D + DV)
@@ -52,44 +54,46 @@ def tile_attend_soft_cap_gate_topkq128n1024t4096_kernel(tc, q_words, q_scales, k
         def half_list(h):
             return offsets[:, h * HALF // 16 : (h + 1) * HALF // 16]
 
-        gate_in = sb("gate_in", [P, DV], F32)
-        nc.sync.dma_start(gate_in[:], og[0])
         q_plane = sb("q_plane", [P, PASSES, NQ], U8)
         nc.vector.memset(q_plane[:].rearrange("p o q -> p (o q)").bitcast(I32), 0)
         for r in range(PACK):
-            queue = nc.sync if r == PACK - 1 else nc.scalar
+            queue = nc.sync if r % 2 else nc.scalar
             queue.dma_start(
                 q_plane[r:P:QUAD, :, :].bitcast(I32),
                 q_scales[0][:, r::PACK, :].rearrange("o f q -> f o q").bitcast(I32),
             )
-        key_scale_pool = sb("key_scale_pool", [P, T], U8)
+        key_scale_pool = at("key_scale_pool", [P, T], U8, SCALE_AT)
         nc.vector.memset(key_scale_pool[:].bitcast(I32), 0)
         nc.sync.dma_start(key_scale_pool[0:P:ROW_STEP, :].bitcast(I32), k_scales.rearrange("o f t -> f o t").bitcast(I32))
         key_pool = sb("key_pool", [P, T], I32)
-        nc.sync.dma_start(key_pool[:], k_words[0].rearrange("p t b -> p (t b)").bitcast(I32))
-        q_codes = sb("q_codes", [P, PASSES, NQ], I32)
-        nc.sync.dma_start(q_codes[:], q_words[0].rearrange("o p q r -> p o (q r)").bitcast(I32))
-        value_pool = sb("value_pool", [P, T], F32)
-        nc.sync.dma_start(value_pool[:], vT)
+        key_rows = k_words[0].rearrange("p t b -> p (t b)").bitcast(I32)
+        nc.sync.dma_start(key_pool[:, :KEYS_FIRST], key_rows[:, :KEYS_FIRST])
         token_scale_pool = at("token_scale_pool", [P, T], F32, 0)
         nc.vector.memset(token_scale_pool[:], 0.0)
-        gate_tanh = sb("gate_tanh", [P, DV], F32)
-        nc.scalar.activation(gate_tanh[:], gate_in[:], ACT.Tanh, scale=0.5)
-        gate = sb("gate", [P, DV], F32)
-        nc.scalar.activation(gate[:], gate_tanh[:], ACT.Copy, scale=0.5, bias=0.5)
-        nc.scalar.dma_start(token_scale_pool[0:1, :], vs[0:1, :])
-        key_planes = sb("key_planes", [P, PASSES, N], U8)
-        nc.vector.memset(key_planes[:].rearrange("p o n -> p (o n)").bitcast(I32), 0)
+        nc.sync.dma_start(token_scale_pool[0:1, :], vs[0:1, :])
+        nc.sync.dma_start(key_pool[:, KEYS_FIRST:], key_rows[:, KEYS_FIRST:])
+        q_codes = sb("q_codes", [P, PASSES, NQ], I32)
+        nc.sync.dma_start(q_codes[:], q_words[0].rearrange("o p q r -> p o (q r)").bitcast(I32))
+        gate_in = sb("gate_in", [P, DV], F32)
+        nc.sync.dma_start(gate_in[:], og[0])
         ones = sb("ones", [P, QUAD], F32)
         nc.vector.memset(ones[:], 1.0)
 
         key_scale_rows = sb("key_scale_rows", [P, N], U8)
         nc.vector.tensor_copy(key_scale_rows[:], key_scale_pool[:].indirect(offsets[:]))
-        for quad in range(P // QUAD):
+        key_planes = at("key_planes", [P, PASSES, N], U8, SCALE_AT)
+        for quad in (0, 2, 1, 3):
             nc.scalar.dma_start(
                 key_planes[quad * QUAD : quad * QUAD + PACK, :, :].bitcast(I32),
                 key_scale_rows[quad * QUAD : (quad + 1) * QUAD : ROW_STEP, :].bitcast(I32),
             )
+
+        value_pool = at("value_pool", [P, T], F32, SCALE_AT + PASSES * N)
+        nc.scalar.dma_start(value_pool[:], vT)
+        gate_tanh = sb("gate_tanh", [P, DV], F32)
+        nc.scalar.activation(gate_tanh[:], gate_in[:], ACT.Tanh, scale=0.5)
+        gate = sb("gate", [P, DV], F32)
+        nc.scalar.activation(gate[:], gate_tanh[:], ACT.Copy, scale=0.5, bias=0.5)
 
         token_scale = sb("token_scale", [P, N], F32)
         nc.vector.tensor_copy(token_scale[:], token_scale_pool[:].indirect(offsets[:]))

@@ -21,12 +21,16 @@ HALF = P * PACK
 HALVES = N // HALF
 PASSES = D // HALF
 QUAD = 32
-ROW_STEP = 4
+ZERO_CUT = T // 2 + 32
+SCALE_CUT = 896
 PIECE = HALF // 2
 LAST = 128
-KEYS_FIRST = 2304
-SCALE_AT = 6 * T
-BLOCK_AT = 4 * T + 2 * HALF
+KEYS_FIRST = 1536
+SCALE_AT = 2 * T
+FIRST = 384
+TANH_AT = FIRST // 2
+NEG_AT = TANH_AT + PIECE + 64
+SCRATCH = NEG_AT + HALF + PIECE
 
 FLOPS = 2 * NQ * N * (D + DV)
 BYTES = P * T * 4 + PASSES * 16 * T + DV * T * 4 + T * 4 + PASSES * (P * NQ * 4 + 16 * NQ) + 2 * NQ * DV * 4 + P * (N // 16) * 2
@@ -54,46 +58,58 @@ def tile_attend_soft_cap_gate_topkq128n1024t4096_kernel(tc, q_words, q_scales, k
         def half_list(h):
             return offsets[:, h * HALF // 16 : (h + 1) * HALF // 16]
 
+        key_scale_pool = at("key_scale_pool", [P, T], U8, SCALE_AT)
+        nc.sync.dma_start(key_scale_pool[0:QUAD, :].bitcast(I32), k_scales.rearrange("o f t -> f o t").bitcast(I32))
         q_plane = sb("q_plane", [P, PASSES, NQ], U8)
-        nc.vector.memset(q_plane[:].rearrange("p o q -> p (o q)").bitcast(I32), 0)
         for r in range(PACK):
-            queue = nc.sync if r % 2 else nc.scalar
-            queue.dma_start(
+            nc.scalar.dma_start(
                 q_plane[r:P:QUAD, :, :].bitcast(I32),
                 q_scales[0][:, r::PACK, :].rearrange("o f q -> f o q").bitcast(I32),
             )
-        key_scale_pool = at("key_scale_pool", [P, T], U8, SCALE_AT)
-        nc.vector.memset(key_scale_pool[:].bitcast(I32), 0)
-        nc.sync.dma_start(key_scale_pool[0:P:ROW_STEP, :].bitcast(I32), k_scales.rearrange("o f t -> f o t").bitcast(I32))
+        gate_in = sb("gate_in", [P, DV], F32)
+        nc.sync.dma_start(gate_in[:], og[0])
         key_pool = sb("key_pool", [P, T], I32)
         key_rows = k_words[0].rearrange("p t b -> p (t b)").bitcast(I32)
         nc.sync.dma_start(key_pool[:, :KEYS_FIRST], key_rows[:, :KEYS_FIRST])
-        token_scale_pool = at("token_scale_pool", [P, T], F32, 0)
-        nc.vector.memset(token_scale_pool[:], 0.0)
+        ones = sb("ones", [P, QUAD], F32)
+        nc.vector.memset(ones[:], 1.0)
+        token_scale_pool = sb("token_scale_pool", [P, T], F32)
+        nc.vector.memset(token_scale_pool[:, : ZERO_CUT - 1], 0.0)
+        nc.vector.memset(token_scale_pool[:, ZERO_CUT - 1 : ZERO_CUT], 0.0)
+        nc.gpsimd.memset(token_scale_pool[:, ZERO_CUT:], 0.0)
         nc.sync.dma_start(token_scale_pool[0:1, :], vs[0:1, :])
         nc.sync.dma_start(key_pool[:, KEYS_FIRST:], key_rows[:, KEYS_FIRST:])
         q_codes = sb("q_codes", [P, PASSES, NQ], I32)
         nc.sync.dma_start(q_codes[:], q_words[0].rearrange("o p q r -> p o (q r)").bitcast(I32))
-        gate_in = sb("gate_in", [P, DV], F32)
-        nc.sync.dma_start(gate_in[:], og[0])
-        ones = sb("ones", [P, QUAD], F32)
-        nc.vector.memset(ones[:], 1.0)
+        scale_words = key_scale_pool[:].bitcast(I32)
+        nc.gpsimd.memset(scale_words[QUAD : 2 * QUAD, :], 0)
+        column = sb("column", [P, QUAD], F32)
+        nc.vector.tensor_tensor_scan(column[:], ones[:], ones[:], 0.0, ALU.mult, ALU.add)
+        nc.gpsimd.memset(scale_words[2 * QUAD :, SCALE_CUT:], 0)
+        ident = sb("ident", [P, P], F32)
+        nc.gpsimd.memset(ident[:], 0.0)
+        nc.vector.memset(scale_words[2 * QUAD :, : SCALE_CUT - 1], 0)
+        row = sb("row", [P, QUAD], F32)
+        nc.vector.transpose(row[:], column[:])
+        nc.vector.memset(scale_words[2 * QUAD :, SCALE_CUT - 1 : SCALE_CUT], 0)
+        gate_tanh = at("gate_tanh", [P, DV], F32, 0)
+        nc.scalar.activation(gate_tanh[:], gate_in[:], ACT.Tanh, scale=0.5)
 
         key_scale_rows = sb("key_scale_rows", [P, N], U8)
         nc.vector.tensor_copy(key_scale_rows[:], key_scale_pool[:].indirect(offsets[:]))
+        block_ident = sb("block_ident", [P, QUAD], F32)
+        nc.vector.tensor_tensor(block_ident[:], column[:], row[:], ALU.is_equal)
         key_planes = at("key_planes", [P, PASSES, N], U8, SCALE_AT)
         for quad in (0, 2, 1, 3):
             nc.scalar.dma_start(
                 key_planes[quad * QUAD : quad * QUAD + PACK, :, :].bitcast(I32),
-                key_scale_rows[quad * QUAD : (quad + 1) * QUAD : ROW_STEP, :].bitcast(I32),
+                key_scale_rows[quad * PACK * PASSES : (quad + 1) * PACK * PASSES, :].bitcast(I32),
             )
 
         value_pool = at("value_pool", [P, T], F32, SCALE_AT + PASSES * N)
         nc.scalar.dma_start(value_pool[:], vT)
-        gate_tanh = sb("gate_tanh", [P, DV], F32)
-        nc.scalar.activation(gate_tanh[:], gate_in[:], ACT.Tanh, scale=0.5)
-        gate = sb("gate", [P, DV], F32)
-        nc.scalar.activation(gate[:], gate_tanh[:], ACT.Copy, scale=0.5, bias=0.5)
+        for first in range(0, P, QUAD):
+            nc.scalar.copy(ident[first : first + QUAD, first : first + QUAD], block_ident[first : first + QUAD, :])
 
         token_scale = sb("token_scale", [P, N], F32)
         nc.vector.tensor_copy(token_scale[:], token_scale_pool[:].indirect(offsets[:]))
@@ -101,55 +117,55 @@ def tile_attend_soft_cap_gate_topkq128n1024t4096_kernel(tc, q_words, q_scales, k
         for h in range(HALVES):
             nc.sync.dma_start(slot_scale[h][:], token_scale[0:1, h * HALF : (h + 1) * HALF].rearrange("o (p t) -> o p t", t=PACK))
 
-        pairs = at("key_pairs", [P, HALF + PIECE], U32, 0)
-        capped = []
-        column = at("column", [P, QUAD], F32, 4096)
-        row = sb("row", [P, QUAD], F32)
-        block_ident = at("block_ident", [P, QUAD], F32, BLOCK_AT)
-        scratch = at("scratch", [P, 2 * HALF], F32, BLOCK_AT + 64)
-        for h in range(HALVES):
-            cols = slice(h * HALF, (h + 1) * HALF)
+        pairs = sb("key_pairs", [P, HALF + PIECE], U32)
+        scratch = at("scratch", [P, SCRATCH], F32, 0)
+        late_tanh = [scratch[:, NEG_AT + HALF :], scratch[:, TANH_AT : TANH_AT + PIECE]]
+        neg_c = [sb("neg_c0", [P, HALF], F32, "late_v")[:], scratch[:, NEG_AT : NEG_AT + HALF]]
+        value_words = [
+            scratch[:, TANH_AT - FIRST // 2 : TANH_AT - FIRST // 2 + PIECE],
+            scratch[:, NEG_AT + LAST // 2 - PIECE : NEG_AT + LAST // 2],
+        ]
+
+        def gather_keys(h):
             first = (HALVES - 1 - h) * PIECE
             nc.vector.tensor_copy(pairs[:, first : first + HALF], key_pool[:].bitcast(U32).indirect(half_list(h)))
-            if h == 0:
-                nc.vector.tensor_tensor_scan(column[:], ones[:], ones[:], 0.0, ALU.mult, ALU.add)
-            else:
-                nc.vector.transpose(row[:], column[:])
             codes = sb(f"key_codes{h}", [P, PASSES, 2 * HALF], U8, f"codes{h}")
             for n0 in range(0, HALF, PIECE):
                 nc.vector.tensor_copy(
                     codes[:].bitcast(U16)[:, :, n0 : n0 + PIECE],
                     pairs[:, first + n0 : first + n0 + PIECE].bitcast(U16).rearrange("p (n o) -> p o n", o=PASSES),
                 )
-            if h == 1:
-                nc.vector.tensor_tensor(block_ident[:], column[:], row[:], ALU.is_equal)
-                ident = sb("ident", [P, P], F32, "codes0")
-                nc.vector.memset(ident[:], 0.0)
-                for first in range(0, P, QUAD):
-                    nc.scalar.copy(ident[first : first + QUAD, first : first + QUAD], block_ident[first : first + QUAD, :])
-            scores = bank(f"scores{h}", [P, HALF])
-            for o in range(PASSES):
-                nc.tensor.matmul_mx(
-                    out=scores[:],
-                    lhsT=q_codes[:, o, :].bitcast(FP8X4),
-                    lhsT_scale=q_plane[:, o, :],
-                    rhs=codes[:, o, :].bitcast(FP4X4),
-                    rhs_scale=key_planes[:, o, cols],
-                    start=(o == 0),
-                    stop=(o == PASSES - 1),
-                )
-            tanh_h = scratch[:, :HALF] if h else sb("tanh0", [P, HALF], F32)[:]
-            nc.scalar.activation(
-                tanh_h.rearrange("q (t p) -> q t p", t=PACK), scores[:].rearrange("q (p t) -> q t p", t=PACK), ACT.Tanh, scale=1.0 / CAP
-            )
-            capped.append(tanh_h)
+            return codes
 
-        neg_max = [sb(f"neg_max{h}", [P, 1], F32) for h in range(HALVES)]
-        neg_c = [sb("neg_c0", [P, HALF], F32, "late_v")[:], scratch[:, HALF:]]
-        value_words = [
-            at("values0", [P, HALF // 2], F32, BLOCK_AT + 64 - 2 * HALF)[:],
-            scratch[:, HALF - (HALF - LAST) // 2 : HALF + LAST // 2],
-        ]
+        def score(name, codes, h, n0, width, step):
+            scores = bank(name, [P, width])
+            for c0 in range(0, width, step):
+                for o in range(PASSES):
+                    nc.tensor.matmul_mx(
+                        out=scores[:, c0 : c0 + step],
+                        lhsT=q_codes[:, o, :].bitcast(FP8X4),
+                        lhsT_scale=q_plane[:, o, :],
+                        rhs=codes[:, o, 2 * (n0 + c0) : 2 * (n0 + c0 + step)].bitcast(FP4X4),
+                        rhs_scale=key_planes[:, o, h * HALF + n0 + c0 : h * HALF + n0 + c0 + step],
+                        start=(o == 0),
+                        stop=(o == PASSES - 1),
+                    )
+            return scores
+
+        def cap(capped, scores):
+            nc.scalar.activation(
+                capped.rearrange("q (t p) -> q t p", t=PACK), scores[:].rearrange("q (p t) -> q t p", t=PACK), ACT.Tanh, scale=1.0 / CAP
+            )
+
+        early_tanh = sb("early_tanh", [P, HALF], F32)
+        cap(early_tanh[:], score("scores0", gather_keys(0), 0, 0, HALF, P))
+        gate = sb("gate", [P, DV], F32, "codes0")
+        nc.scalar.activation(gate[:], gate_tanh[:], ACT.Copy, scale=0.5, bias=0.5)
+        late_codes = gather_keys(1)
+        for j in range(2):
+            cap(late_tanh[j], score(f"scores1_{j}", late_codes, 1, j * PIECE, PIECE, P))
+
+        neg_max = [sb(f"neg_max{i}", [P, 1], F32) for i in range(3)]
         v_turned = [bank(f"v_turned{h}", [P, 2, DV]) for h in range(HALVES)]
         v_grouped = [sb("v_grouped0", [P, DV, PACK], BF16, "late_v"), sb("v_grouped1", [P, DV, PACK], BF16)]
         w_grouped = [sb(f"w_grouped{h}", [P, NQ, PACK], BF16) for h in range(HALVES)]
@@ -171,12 +187,19 @@ def tile_attend_soft_cap_gate_topkq128n1024t4096_kernel(tc, q_words, q_scales, k
         def quantize(codes, plane, grouped):
             nc.vector.quantize_mx(out=codes[:].bitcast(FP8X4), scales=plane[:], in_=grouped[:].rearrange("p x t -> p (x t)"))
 
-        for h in range(HALVES):
-            nc.vector.tensor_scalar(
-                neg_c[h], capped[h], -CAP, neg_max[h - 1][:] if h else None,
-                ALU.mult, ALU.min, accum_out=neg_max[h][:],
+        def row_max(i, negated, capped):
+            nc.vector.tensor_scalar(negated, capped, -CAP, neg_max[i - 1][:] if i else None, ALU.mult, ALU.min, accum_out=neg_max[i][:])
+
+        row_max(0, neg_c[0], early_tanh[:])
+        for j in range(2):
+            gather_values(0, j * FIRST // 2, (j + 1) * FIRST // 2)
+            row_max(
+                1 + j,
+                neg_c[1].rearrange("q (t p) -> q t p", t=PACK)[:, :, j * P // 2 : (j + 1) * P // 2],
+                late_tanh[j].rearrange("q (t p) -> q t p", t=PACK),
             )
-            gather_values(h, 0, HALF - h * LAST)
+        gather_values(0, FIRST, HALF)
+        gather_values(1, 0, HALF - LAST)
 
         part_sum = []
         p_turned = []
@@ -187,7 +210,7 @@ def tile_attend_soft_cap_gate_topkq128n1024t4096_kernel(tc, q_words, q_scales, k
                 part_sum.append(sb(f"part_sum{h}_{t0}", [P, 1], F32))
                 nc.scalar.activation(
                     probs[:, t0 * P : t1 * P], neg_c[h][:, t0 * P : t1 * P], ACT.Exp,
-                    bias=neg_max[HALVES - 1][:], scale=-1.0, accum_out=part_sum[-1][:],
+                    bias=neg_max[-1][:], scale=-1.0, accum_out=part_sum[-1][:],
                 )
                 for t in range(t0, t1):
                     nc.tensor.transpose(turned_p[:, t, :], probs[:, t * P : (t + 1) * P], ident[:])

@@ -21,11 +21,9 @@ HALF = P * PACK
 HALVES = N // HALF
 PASSES = D // HALF
 QUAD = 32
-ZERO_CUT = T // 2 + 32
-SCALE_CUT = 896
 PIECE = HALF // 2
 LAST = 128
-KEYS_FIRST = 1536
+KEYS_FIRST = 1792
 SCALE_AT = 2 * T
 FIRST = 384
 TANH_AT = FIRST // 2
@@ -74,24 +72,18 @@ def tile_attend_soft_cap_gate_topkq128n1024t4096_kernel(tc, q_words, q_scales, k
         ones = sb("ones", [P, QUAD], F32)
         nc.vector.memset(ones[:], 1.0)
         token_scale_pool = sb("token_scale_pool", [P, T], F32)
-        nc.vector.memset(token_scale_pool[:, : ZERO_CUT - 1], 0.0)
-        nc.vector.memset(token_scale_pool[:, ZERO_CUT - 1 : ZERO_CUT], 0.0)
-        nc.gpsimd.memset(token_scale_pool[:, ZERO_CUT:], 0.0)
+        nc.vector.memset(token_scale_pool[:], 0.0)
         nc.sync.dma_start(token_scale_pool[0:1, :], vs[0:1, :])
         nc.sync.dma_start(key_pool[:, KEYS_FIRST:], key_rows[:, KEYS_FIRST:])
         q_codes = sb("q_codes", [P, PASSES, NQ], I32)
         nc.sync.dma_start(q_codes[:], q_words[0].rearrange("o p q r -> p o (q r)").bitcast(I32))
         scale_words = key_scale_pool[:].bitcast(I32)
-        nc.gpsimd.memset(scale_words[QUAD : 2 * QUAD, :], 0)
         column = sb("column", [P, QUAD], F32)
         nc.vector.tensor_tensor_scan(column[:], ones[:], ones[:], 0.0, ALU.mult, ALU.add)
-        nc.gpsimd.memset(scale_words[2 * QUAD :, SCALE_CUT:], 0)
-        ident = sb("ident", [P, P], F32)
-        nc.gpsimd.memset(ident[:], 0.0)
-        nc.vector.memset(scale_words[2 * QUAD :, : SCALE_CUT - 1], 0)
+        nc.vector.memset(scale_words[QUAD : 2 * QUAD, :], 0)
         row = sb("row", [P, QUAD], F32)
         nc.vector.transpose(row[:], column[:])
-        nc.vector.memset(scale_words[2 * QUAD :, SCALE_CUT - 1 : SCALE_CUT], 0)
+        nc.vector.memset(scale_words[2 * QUAD :, :], 0)
         gate_tanh = at("gate_tanh", [P, DV], F32, 0)
         nc.scalar.activation(gate_tanh[:], gate_in[:], ACT.Tanh, scale=0.5)
 
@@ -99,6 +91,8 @@ def tile_attend_soft_cap_gate_topkq128n1024t4096_kernel(tc, q_words, q_scales, k
         nc.vector.tensor_copy(key_scale_rows[:], key_scale_pool[:].indirect(offsets[:]))
         block_ident = sb("block_ident", [P, QUAD], F32)
         nc.vector.tensor_tensor(block_ident[:], column[:], row[:], ALU.is_equal)
+        ident = sb("ident", [P, P], F32)
+        nc.vector.memset(ident[:], 0.0)
         key_planes = at("key_planes", [P, PASSES, N], U8, SCALE_AT)
         for quad in (0, 2, 1, 3):
             nc.scalar.dma_start(

@@ -23,12 +23,9 @@ PASSES = D // HALF
 QUAD = 32
 PIECE = HALF // 2
 LAST = 128
-KEYS_FIRST = 1792
-SCALE_AT = 2 * T
-FIRST = 384
-TANH_AT = FIRST // 2
-NEG_AT = TANH_AT + PIECE + 64
-SCRATCH = NEG_AT + HALF + PIECE
+ZEROED = T // 2
+SCALE_AT = 0
+SCRATCH = 2 * HALF
 
 FLOPS = 2 * NQ * N * (D + DV)
 BYTES = P * T * 4 + PASSES * 16 * T + DV * T * 4 + T * 4 + PASSES * (P * NQ * 4 + 16 * NQ) + 2 * NQ * DV * 4 + P * (N // 16) * 2
@@ -64,28 +61,35 @@ def tile_attend_soft_cap_gate_topkq128n1024t4096_kernel(tc, q_words, q_scales, k
                 q_plane[r:P:QUAD, :, :].bitcast(I32),
                 q_scales[0][:, r::PACK, :].rearrange("o f q -> f o q").bitcast(I32),
             )
-        gate_in = sb("gate_in", [P, DV], F32)
-        nc.sync.dma_start(gate_in[:], og[0])
+        scale_filler = sb("scale_filler", [P, QUAD], F32)
+        nc.sync.dma_start(scale_filler[:], vs[:, 0:QUAD])
         key_pool = sb("key_pool", [P, T], I32)
         key_rows = k_words[0].rearrange("p t b -> p (t b)").bitcast(I32)
-        nc.sync.dma_start(key_pool[:, :KEYS_FIRST], key_rows[:, :KEYS_FIRST])
+        nc.sync.dma_start(key_pool[:], key_rows)
         ones = sb("ones", [P, QUAD], F32)
         nc.vector.memset(ones[:], 1.0)
-        token_scale_pool = sb("token_scale_pool", [P, T], F32)
-        nc.vector.memset(token_scale_pool[:], 0.0)
-        nc.sync.dma_start(token_scale_pool[0:1, :], vs[0:1, :])
-        nc.sync.dma_start(key_pool[:, KEYS_FIRST:], key_rows[:, KEYS_FIRST:])
-        q_codes = sb("q_codes", [P, PASSES, NQ], I32)
-        nc.sync.dma_start(q_codes[:], q_words[0].rearrange("o p q r -> p o (q r)").bitcast(I32))
         scale_words = key_scale_pool[:].bitcast(I32)
+        nc.vector.memset(scale_words[QUAD : 2 * QUAD, :], 0)
         column = sb("column", [P, QUAD], F32)
         nc.vector.tensor_tensor_scan(column[:], ones[:], ones[:], 0.0, ALU.mult, ALU.add)
-        nc.vector.memset(scale_words[QUAD : 2 * QUAD, :], 0)
+        nc.vector.memset(scale_words[2 * QUAD :, :], 0)
         row = sb("row", [P, QUAD], F32)
         nc.vector.transpose(row[:], column[:])
-        nc.vector.memset(scale_words[2 * QUAD :, :], 0)
-        gate_tanh = at("gate_tanh", [P, DV], F32, 0)
+        token_scale_pool = sb("token_scale_pool", [P, T], F32)
+        nc.vector.memset(token_scale_pool[:, :ZEROED], 0.0)
+        nc.scalar.activation(
+            token_scale_pool[:, ZEROED:].rearrange("p (x j) -> p x j", j=QUAD),
+            scale_filler[:].unsqueeze(1).to_broadcast([P, (T - ZEROED) // QUAD, QUAD]), ACT.Copy,
+        )
+        nc.sync.dma_start(token_scale_pool[0:1, :], vs[0:1, :])
+        q_codes = sb("q_codes", [P, PASSES, NQ], I32)
+        nc.sync.dma_start(q_codes[:], q_words[0].rearrange("o p q r -> p o (q r)").bitcast(I32))
+        gate_in = sb("gate_in", [P, DV], F32)
+        nc.sync.dma_start(gate_in[:], og[0])
+        gate_tanh = sb("gate_tanh", [P, DV], F32)
         nc.scalar.activation(gate_tanh[:], gate_in[:], ACT.Tanh, scale=0.5)
+        gate = sb("gate", [P, DV], F32)
+        nc.scalar.activation(gate[:], gate_tanh[:], ACT.Copy, scale=0.5, bias=0.5)
 
         key_scale_rows = sb("key_scale_rows", [P, N], U8)
         nc.vector.tensor_copy(key_scale_rows[:], key_scale_pool[:].indirect(offsets[:]))
@@ -105,61 +109,40 @@ def tile_attend_soft_cap_gate_topkq128n1024t4096_kernel(tc, q_words, q_scales, k
         for first in range(0, P, QUAD):
             nc.scalar.copy(ident[first : first + QUAD, first : first + QUAD], block_ident[first : first + QUAD, :])
 
+        scratch = sb("scratch", [P, SCRATCH], F32)
+        capped = [sb("early_tanh", [P, HALF], F32)[:], scratch[:, :HALF]]
+        neg_late = scratch[:, HALF:]
+        value_words = [scratch[:, :PIECE], scratch[:, HALF + LAST // 2 - PIECE : HALF + LAST // 2]]
+
+        pairs = sb("key_pairs", [P, HALVES, HALF], U32)
+        for h in range(HALVES):
+            nc.vector.tensor_copy(pairs[:, h], key_pool[:].bitcast(U32).indirect(half_list(h)))
+        for h in range(HALVES):
+            codes = sb(f"key_codes{h}", [P, PASSES, 2 * HALF], U8)
+            nc.vector.tensor_copy(codes[:].bitcast(U16), pairs[:, h].bitcast(U16).rearrange("p (n o) -> p o n", o=PASSES))
+            scores = bank(f"scores{h}", [P, HALF])
+            for o in range(PASSES):
+                nc.tensor.matmul_mx(
+                    out=scores[:],
+                    lhsT=q_codes[:, o, :].bitcast(FP8X4),
+                    lhsT_scale=q_plane[:, o, :],
+                    rhs=codes[:, o, :].bitcast(FP4X4),
+                    rhs_scale=key_planes[:, o, h * HALF : (h + 1) * HALF],
+                    start=(o == 0),
+                    stop=(o == PASSES - 1),
+                )
+            nc.scalar.activation(
+                capped[h].rearrange("q (t p) -> q t p", t=PACK), scores[:].rearrange("q (p t) -> q t p", t=PACK), ACT.Tanh, scale=1.0 / CAP
+            )
+
         token_scale = sb("token_scale", [P, N], F32)
         nc.vector.tensor_copy(token_scale[:], token_scale_pool[:].indirect(offsets[:]))
         slot_scale = [sb(f"slot_scale{h}", [P, PACK], F32, f"late{h}") for h in range(HALVES)]
         for h in range(HALVES):
             nc.sync.dma_start(slot_scale[h][:], token_scale[0:1, h * HALF : (h + 1) * HALF].rearrange("o (p t) -> o p t", t=PACK))
 
-        pairs = sb("key_pairs", [P, HALF + PIECE], U32)
-        scratch = at("scratch", [P, SCRATCH], F32, 0)
-        late_tanh = [scratch[:, NEG_AT + HALF :], scratch[:, TANH_AT : TANH_AT + PIECE]]
-        neg_c = [sb("neg_c0", [P, HALF], F32, "late_v")[:], scratch[:, NEG_AT : NEG_AT + HALF]]
-        value_words = [
-            scratch[:, TANH_AT - FIRST // 2 : TANH_AT - FIRST // 2 + PIECE],
-            scratch[:, NEG_AT + LAST // 2 - PIECE : NEG_AT + LAST // 2],
-        ]
-
-        def gather_keys(h):
-            first = (HALVES - 1 - h) * PIECE
-            nc.vector.tensor_copy(pairs[:, first : first + HALF], key_pool[:].bitcast(U32).indirect(half_list(h)))
-            codes = sb(f"key_codes{h}", [P, PASSES, 2 * HALF], U8, f"codes{h}")
-            for n0 in range(0, HALF, PIECE):
-                nc.vector.tensor_copy(
-                    codes[:].bitcast(U16)[:, :, n0 : n0 + PIECE],
-                    pairs[:, first + n0 : first + n0 + PIECE].bitcast(U16).rearrange("p (n o) -> p o n", o=PASSES),
-                )
-            return codes
-
-        def score(name, codes, h, n0, width, step):
-            scores = bank(name, [P, width])
-            for c0 in range(0, width, step):
-                for o in range(PASSES):
-                    nc.tensor.matmul_mx(
-                        out=scores[:, c0 : c0 + step],
-                        lhsT=q_codes[:, o, :].bitcast(FP8X4),
-                        lhsT_scale=q_plane[:, o, :],
-                        rhs=codes[:, o, 2 * (n0 + c0) : 2 * (n0 + c0 + step)].bitcast(FP4X4),
-                        rhs_scale=key_planes[:, o, h * HALF + n0 + c0 : h * HALF + n0 + c0 + step],
-                        start=(o == 0),
-                        stop=(o == PASSES - 1),
-                    )
-            return scores
-
-        def cap(capped, scores):
-            nc.scalar.activation(
-                capped.rearrange("q (t p) -> q t p", t=PACK), scores[:].rearrange("q (p t) -> q t p", t=PACK), ACT.Tanh, scale=1.0 / CAP
-            )
-
-        early_tanh = sb("early_tanh", [P, HALF], F32)
-        cap(early_tanh[:], score("scores0", gather_keys(0), 0, 0, HALF, P))
-        gate = sb("gate", [P, DV], F32, "codes0")
-        nc.scalar.activation(gate[:], gate_tanh[:], ACT.Copy, scale=0.5, bias=0.5)
-        late_codes = gather_keys(1)
-        for j in range(2):
-            cap(late_tanh[j], score(f"scores1_{j}", late_codes, 1, j * PIECE, PIECE, P))
-
-        neg_max = [sb(f"neg_max{i}", [P, 1], F32) for i in range(3)]
+        neg_c = [sb("neg_c0", [P, HALF], F32, "late_v")[:], neg_late]
+        neg_max = [sb(f"neg_max{i}", [P, 1], F32) for i in range(HALVES)]
         v_turned = [bank(f"v_turned{h}", [P, 2, DV]) for h in range(HALVES)]
         v_grouped = [sb("v_grouped0", [P, DV, PACK], BF16, "late_v"), sb("v_grouped1", [P, DV, PACK], BF16)]
         w_grouped = [sb(f"w_grouped{h}", [P, NQ, PACK], BF16) for h in range(HALVES)]
@@ -184,15 +167,9 @@ def tile_attend_soft_cap_gate_topkq128n1024t4096_kernel(tc, q_words, q_scales, k
         def row_max(i, negated, capped):
             nc.vector.tensor_scalar(negated, capped, -CAP, neg_max[i - 1][:] if i else None, ALU.mult, ALU.min, accum_out=neg_max[i][:])
 
-        row_max(0, neg_c[0], early_tanh[:])
-        for j in range(2):
-            gather_values(0, j * FIRST // 2, (j + 1) * FIRST // 2)
-            row_max(
-                1 + j,
-                neg_c[1].rearrange("q (t p) -> q t p", t=PACK)[:, :, j * P // 2 : (j + 1) * P // 2],
-                late_tanh[j].rearrange("q (t p) -> q t p", t=PACK),
-            )
-        gather_values(0, FIRST, HALF)
+        for h in range(HALVES):
+            row_max(h, neg_c[h], capped[h])
+        gather_values(0, 0, HALF)
         gather_values(1, 0, HALF - LAST)
 
         part_sum = []

@@ -25,7 +25,6 @@ PIECE = HALF // 2
 LAST = 128
 ZEROED = T // 2
 SCALE_AT = 0
-SCRATCH = 2 * HALF
 
 FLOPS = 2 * NQ * N * (D + DV)
 BYTES = P * T * 4 + PASSES * 16 * T + DV * T * 4 + T * 4 + PASSES * (P * NQ * 4 + 16 * NQ) + 2 * NQ * DV * 4 + P * (N // 16) * 2
@@ -109,10 +108,13 @@ def tile_attend_soft_cap_gate_topkq128n1024t4096_kernel(tc, q_words, q_scales, k
         for first in range(0, P, QUAD):
             nc.scalar.copy(ident[first : first + QUAD, first : first + QUAD], block_ident[first : first + QUAD, :])
 
-        scratch = sb("scratch", [P, SCRATCH], F32)
-        capped = [sb("early_tanh", [P, HALF], F32)[:], scratch[:, :HALF]]
-        neg_late = scratch[:, HALF:]
-        value_words = [scratch[:, :PIECE], scratch[:, HALF + LAST // 2 - PIECE : HALF + LAST // 2]]
+        scratch = sb("scratch", [P, 3 * HALF], F32)
+        capped = [scratch[:, HALF + PIECE : 2 * HALF + PIECE], scratch[:, :HALF]]
+        neg_late = [scratch[:, HALF : HALF + PIECE], scratch[:, 2 * HALF + PIECE :]]
+        value_words = [
+            scratch[:, HALF + PIECE - LAST // 2 : 2 * HALF - LAST // 2],
+            scratch[:, HALF + LAST // 2 - PIECE : HALF + LAST // 2],
+        ]
 
         pairs = sb("key_pairs", [P, HALVES, HALF], U32)
         for h in range(HALVES):
@@ -137,14 +139,14 @@ def tile_attend_soft_cap_gate_topkq128n1024t4096_kernel(tc, q_words, q_scales, k
 
         token_scale = sb("token_scale", [P, N], F32)
         nc.vector.tensor_copy(token_scale[:], token_scale_pool[:].indirect(offsets[:]))
-        slot_scale = [sb(f"slot_scale{h}", [P, PACK], F32, f"late{h}") for h in range(HALVES)]
+        slot_scale = [sb(f"slot_scale{h}", [P, PACK], F32) for h in range(HALVES)]
         for h in range(HALVES):
             nc.sync.dma_start(slot_scale[h][:], token_scale[0:1, h * HALF : (h + 1) * HALF].rearrange("o (p t) -> o p t", t=PACK))
 
-        neg_c = [sb("neg_c0", [P, HALF], F32, "late_v")[:], neg_late]
+        neg_early = sb("neg_early", [P, HALF], F32)
         neg_max = [sb(f"neg_max{i}", [P, 1], F32) for i in range(HALVES)]
         v_turned = [bank(f"v_turned{h}", [P, 2, DV]) for h in range(HALVES)]
-        v_grouped = [sb("v_grouped0", [P, DV, PACK], BF16, "late_v"), sb("v_grouped1", [P, DV, PACK], BF16)]
+        v_grouped = [sb(f"v_grouped{h}", [P, DV, PACK], BF16, f"v_grouped{h}") for h in range(HALVES)]
         w_grouped = [sb(f"w_grouped{h}", [P, NQ, PACK], BF16) for h in range(HALVES)]
         v_codes = [sb(f"v_codes{h}", [P, DV], U32) for h in range(HALVES)]
         v_plane = [sb(f"v_plane{h}", [P, DV], U8) for h in range(HALVES)]
@@ -167,28 +169,34 @@ def tile_attend_soft_cap_gate_topkq128n1024t4096_kernel(tc, q_words, q_scales, k
         def row_max(i, negated, capped):
             nc.vector.tensor_scalar(negated, capped, -CAP, neg_max[i - 1][:] if i else None, ALU.mult, ALU.min, accum_out=neg_max[i][:])
 
-        for h in range(HALVES):
-            row_max(h, neg_c[h], capped[h])
-        gather_values(0, 0, HALF)
+        row_max(0, neg_early[:], capped[0])
+        row_max(
+            1,
+            scratch[:, HALF:].rearrange("q (a x) -> q a x", x=PIECE)[:, 0:PACK:3, :],
+            capped[1].rearrange("q (a x) -> q a x", x=PIECE),
+        )
+        gather_values(0, LAST, HALF)
         gather_values(1, 0, HALF - LAST)
 
         part_sum = []
         p_turned = []
-        for h, cuts in enumerate([[0, PACK], [0, PACK // 2, PACK]]):
+        for h, pieces in enumerate([[neg_early[:]], neg_late]):
             probs = sb(f"probs{h}", [P, PACK * P], F32)
             turned_p = bank(f"p_turned{h}", [P, PACK, NQ])
-            for t0, t1 in zip(cuts, cuts[1:]):
-                part_sum.append(sb(f"part_sum{h}_{t0}", [P, 1], F32))
+            width = HALF // len(pieces)
+            for i, piece in enumerate(pieces):
+                part_sum.append(sb(f"part_sum{h}_{i}", [P, 1], F32))
                 nc.scalar.activation(
-                    probs[:, t0 * P : t1 * P], neg_c[h][:, t0 * P : t1 * P], ACT.Exp,
+                    probs[:, i * width : (i + 1) * width], piece, ACT.Exp,
                     bias=neg_max[-1][:], scale=-1.0, accum_out=part_sum[-1][:],
                 )
-                for t in range(t0, t1):
+                for t in range(i * width // P, (i + 1) * width // P):
                     nc.tensor.transpose(turned_p[:, t, :], probs[:, t * P : (t + 1) * P], ident[:])
             p_turned.append(turned_p)
-        turn_values(0)
+        gather_values(0, 0, LAST)
         gather_values(1, HALF - LAST, HALF)
-        turn_values(1)
+        for h in range(HALVES):
+            turn_values(h)
         subtotal = sb("subtotal", [P, 1], F32)
         nc.scalar.activation(subtotal[:], part_sum[0][:], ACT.Identity, bias=part_sum[1][:])
         total = sb("total", [P, 1], F32)
@@ -199,11 +207,11 @@ def tile_attend_soft_cap_gate_topkq128n1024t4096_kernel(tc, q_words, q_scales, k
                 w_grouped[h][:], p_turned[h][:].rearrange("p t q -> p q t"),
                 slot_scale[h][:].unsqueeze(1).to_broadcast([P, NQ, PACK]), ALU.mult,
             )
-        quantize(v_codes[0], v_plane[0], v_grouped[0])
-        quantize(w_codes[0], w_plane[0], w_grouped[0])
-        quantize(w_codes[1], w_plane[1], w_grouped[1])
-        quantize(v_codes[1], v_plane[1], v_grouped[1])
-        inv_total = sb("inv_total", [P, 1], F32, "late1")
+        for h in range(HALVES):
+            quantize(w_codes[h], w_plane[h], w_grouped[h])
+        for h in range(HALVES):
+            quantize(v_codes[h], v_plane[h], v_grouped[h])
+        inv_total = sb("inv_total", [P, 1], F32, "v_grouped1")
         nc.vector.reciprocal(inv_total[:], total[:])
 
         acc = bank("acc", [P, DV])

@@ -23,7 +23,10 @@ PASSES = D // HALF
 QUAD = 32
 PIECE = HALF // 2
 LAST = 128
-ZEROED = T // 2
+PITCH = PIECE + HALF
+ZEROED = T // 4
+FILLER_AT = T
+SCALE_ROW = 68
 SCALE_AT = 0
 
 FLOPS = 2 * NQ * N * (D + DV)
@@ -54,14 +57,10 @@ def tile_attend_soft_cap_gate_topkq128n1024t4096_kernel(tc, q_words, q_scales, k
 
         key_scale_pool = at("key_scale_pool", [P, T], U8, SCALE_AT)
         nc.sync.dma_start(key_scale_pool[0:QUAD, :].bitcast(I32), k_scales.rearrange("o f t -> f o t").bitcast(I32))
-        q_plane = sb("q_plane", [P, PASSES, NQ], U8)
-        for r in range(PACK):
-            nc.scalar.dma_start(
-                q_plane[r:P:QUAD, :, :].bitcast(I32),
-                q_scales[0][:, r::PACK, :].rearrange("o f q -> f o q").bitcast(I32),
-            )
-        scale_filler = sb("scale_filler", [P, QUAD], F32)
-        nc.sync.dma_start(scale_filler[:], vs[:, 0:QUAD])
+        scale_filler = at("scale_filler", [P, QUAD], F32, FILLER_AT)
+        nc.scalar.dma_start(scale_filler[:], vs[:, 0:QUAD])
+        scale_rows = sb("scale_rows", [P, N + NQ], U8)
+        nc.scalar.dma_start(scale_rows[0:QUAD, N:].bitcast(I32), q_scales[0].rearrange("o f q -> f o q").bitcast(I32))
         key_pool = sb("key_pool", [P, T], I32)
         key_rows = k_words[0].rearrange("p t b -> p (t b)").bitcast(I32)
         nc.sync.dma_start(key_pool[:], key_rows)
@@ -80,78 +79,80 @@ def tile_attend_soft_cap_gate_topkq128n1024t4096_kernel(tc, q_words, q_scales, k
             token_scale_pool[:, ZEROED:].rearrange("p (x j) -> p x j", j=QUAD),
             scale_filler[:].unsqueeze(1).to_broadcast([P, (T - ZEROED) // QUAD, QUAD]), ACT.Copy,
         )
-        nc.sync.dma_start(token_scale_pool[0:1, :], vs[0:1, :])
+        nc.sync.dma_start(token_scale_pool[SCALE_ROW : SCALE_ROW + 1, :], vs[0:1, :])
         q_codes = sb("q_codes", [P, PASSES, NQ], I32)
         nc.sync.dma_start(q_codes[:], q_words[0].rearrange("o p q r -> p o (q r)").bitcast(I32))
-        gate_in = sb("gate_in", [P, DV], F32)
-        nc.sync.dma_start(gate_in[:], og[0])
-        gate_tanh = sb("gate_tanh", [P, DV], F32)
-        nc.scalar.activation(gate_tanh[:], gate_in[:], ACT.Tanh, scale=0.5)
-        gate = sb("gate", [P, DV], F32)
-        nc.scalar.activation(gate[:], gate_tanh[:], ACT.Copy, scale=0.5, bias=0.5)
 
         key_scale_rows = sb("key_scale_rows", [P, N], U8)
         nc.vector.tensor_copy(key_scale_rows[:], key_scale_pool[:].indirect(offsets[:]))
+        nc.vector.tensor_copy(scale_rows[0:QUAD, :N].bitcast(I32), key_scale_rows[0:QUAD, :].bitcast(I32))
         block_ident = sb("block_ident", [P, QUAD], F32)
         nc.vector.tensor_tensor(block_ident[:], column[:], row[:], ALU.is_equal)
         ident = sb("ident", [P, P], F32)
         nc.vector.memset(ident[:], 0.0)
-        key_planes = at("key_planes", [P, PASSES, N], U8, SCALE_AT)
+        planes = at("planes", [P, PASSES, N + NQ], U8, SCALE_AT)
         for quad in (0, 2, 1, 3):
             nc.scalar.dma_start(
-                key_planes[quad * QUAD : quad * QUAD + PACK, :, :].bitcast(I32),
-                key_scale_rows[quad * PACK * PASSES : (quad + 1) * PACK * PASSES, :].bitcast(I32),
+                planes[quad * QUAD : quad * QUAD + PACK, :, :].bitcast(I32),
+                scale_rows[quad * PACK * PASSES : (quad + 1) * PACK * PASSES, :].bitcast(I32),
             )
 
-        value_pool = at("value_pool", [P, T], F32, SCALE_AT + PASSES * N)
+        gate_in = at("gate_in", [P, DV], F32, FILLER_AT + 64 - 4 * DV)
+        nc.scalar.dma_start(gate_in[:], og[0])
+        value_pool = at("value_pool", [P, T], F32, FILLER_AT + 64)
         nc.scalar.dma_start(value_pool[:], vT)
+        scratch = sb("scratch", [P, 2 * PITCH + DV], F32)
+        gate_tanh = scratch[:, PITCH + PIECE : PITCH + PIECE + DV]
+        nc.scalar.activation(gate_tanh, gate_in[:], ACT.Tanh, scale=0.5)
         for first in range(0, P, QUAD):
             nc.scalar.copy(ident[first : first + QUAD, first : first + QUAD], block_ident[first : first + QUAD, :])
 
-        scratch = sb("scratch", [P, 3 * HALF], F32)
-        capped = [scratch[:, HALF + PIECE : 2 * HALF + PIECE], scratch[:, :HALF]]
-        neg_late = [scratch[:, HALF : HALF + PIECE], scratch[:, 2 * HALF + PIECE :]]
+        capped = [scratch[:, 2 * PITCH + DV - HALF :], scratch[:, PIECE:PITCH]]
+        neg_late = scratch[:, : 2 * PITCH].rearrange("q (a x) -> q a x", x=PITCH)[:, :, :PIECE]
         value_words = [
-            scratch[:, HALF + PIECE - LAST // 2 : 2 * HALF - LAST // 2],
-            scratch[:, HALF + LAST // 2 - PIECE : HALF + LAST // 2],
+            scratch[:, PITCH + PIECE - LAST // 2 : PITCH + HALF - LAST // 2],
+            scratch[:, PITCH + LAST // 2 - PIECE : PITCH + LAST // 2],
         ]
 
         pairs = sb("key_pairs", [P, HALVES, HALF], U32)
         for h in range(HALVES):
             nc.vector.tensor_copy(pairs[:, h], key_pool[:].bitcast(U32).indirect(half_list(h)))
         for h in range(HALVES):
-            codes = sb(f"key_codes{h}", [P, PASSES, 2 * HALF], U8)
+            codes = sb(f"key_codes{h}", [P, PASSES, 2 * HALF], U8, f"codes{h}")
             nc.vector.tensor_copy(codes[:].bitcast(U16), pairs[:, h].bitcast(U16).rearrange("p (n o) -> p o n", o=PASSES))
             scores = bank(f"scores{h}", [P, HALF])
             for o in range(PASSES):
                 nc.tensor.matmul_mx(
                     out=scores[:],
                     lhsT=q_codes[:, o, :].bitcast(FP8X4),
-                    lhsT_scale=q_plane[:, o, :],
+                    lhsT_scale=planes[:, o, N:],
                     rhs=codes[:, o, :].bitcast(FP4X4),
-                    rhs_scale=key_planes[:, o, h * HALF : (h + 1) * HALF],
+                    rhs_scale=planes[:, o, h * HALF : (h + 1) * HALF],
                     start=(o == 0),
                     stop=(o == PASSES - 1),
                 )
             nc.scalar.activation(
                 capped[h].rearrange("q (t p) -> q t p", t=PACK), scores[:].rearrange("q (p t) -> q t p", t=PACK), ACT.Tanh, scale=1.0 / CAP
             )
+            if h == 0:
+                gate = sb("gate", [P, DV], F32, "codes0")
+                nc.scalar.activation(gate[:], gate_tanh, ACT.Copy, scale=0.5, bias=0.5)
 
         token_scale = sb("token_scale", [P, N], F32)
         nc.vector.tensor_copy(token_scale[:], token_scale_pool[:].indirect(offsets[:]))
         slot_scale = [sb(f"slot_scale{h}", [P, PACK], F32) for h in range(HALVES)]
         for h in range(HALVES):
-            nc.sync.dma_start(slot_scale[h][:], token_scale[0:1, h * HALF : (h + 1) * HALF].rearrange("o (p t) -> o p t", t=PACK))
+            nc.sync.dma_start(slot_scale[h][:], token_scale[SCALE_ROW : SCALE_ROW + 1, h * HALF : (h + 1) * HALF].rearrange("o (p t) -> o p t", t=PACK))
 
         neg_early = sb("neg_early", [P, HALF], F32)
         neg_max = [sb(f"neg_max{i}", [P, 1], F32) for i in range(HALVES)]
         v_turned = [bank(f"v_turned{h}", [P, 2, DV]) for h in range(HALVES)]
         v_grouped = [sb(f"v_grouped{h}", [P, DV, PACK], BF16, f"v_grouped{h}") for h in range(HALVES)]
-        w_grouped = [sb(f"w_grouped{h}", [P, NQ, PACK], BF16) for h in range(HALVES)]
+        w_grouped = sb("w_grouped", [P, HALVES, NQ, PACK], BF16)
         v_codes = [sb(f"v_codes{h}", [P, DV], U32) for h in range(HALVES)]
         v_plane = [sb(f"v_plane{h}", [P, DV], U8) for h in range(HALVES)]
-        w_codes = [sb(f"w_codes{h}", [P, NQ], U32) for h in range(HALVES)]
-        w_plane = [sb(f"w_plane{h}", [P, NQ], U8) for h in range(HALVES)]
+        w_codes = sb("w_codes", [P, HALVES, NQ], U32)
+        w_plane = sb("w_plane", [P, HALVES, NQ], U8)
 
         def gather_values(h, n0, n1):
             listed = offsets[:, (h * HALF + n0) // 16 : (h * HALF + n1) // 16]
@@ -170,29 +171,29 @@ def tile_attend_soft_cap_gate_topkq128n1024t4096_kernel(tc, q_words, q_scales, k
             nc.vector.tensor_scalar(negated, capped, -CAP, neg_max[i - 1][:] if i else None, ALU.mult, ALU.min, accum_out=neg_max[i][:])
 
         row_max(0, neg_early[:], capped[0])
-        row_max(
-            1,
-            scratch[:, HALF:].rearrange("q (a x) -> q a x", x=PIECE)[:, 0:PACK:3, :],
-            capped[1].rearrange("q (a x) -> q a x", x=PIECE),
-        )
-        gather_values(0, LAST, HALF)
+        gather_values(0, LAST, 2 * LAST)
+        row_max(1, neg_late, capped[1].rearrange("q (a x) -> q a x", x=PIECE))
+        gather_values(0, 2 * LAST, HALF)
         gather_values(1, 0, HALF - LAST)
 
         part_sum = []
         p_turned = []
-        for h, pieces in enumerate([[neg_early[:]], neg_late]):
+        for h, pieces in enumerate([[(0, neg_early[:])], [(PIECE, neg_late[:, 1]), (0, neg_late[:, 0])]]):
             probs = sb(f"probs{h}", [P, PACK * P], F32)
             turned_p = bank(f"p_turned{h}", [P, PACK, NQ])
             width = HALF // len(pieces)
-            for i, piece in enumerate(pieces):
-                part_sum.append(sb(f"part_sum{h}_{i}", [P, 1], F32))
+            for first, piece in pieces:
+                part_sum.append(sb(f"part_sum{h}_{first}", [P, 1], F32))
                 nc.scalar.activation(
-                    probs[:, i * width : (i + 1) * width], piece, ACT.Exp,
+                    probs[:, first : first + width], piece, ACT.Exp,
                     bias=neg_max[-1][:], scale=-1.0, accum_out=part_sum[-1][:],
                 )
-                for t in range(i * width // P, (i + 1) * width // P):
+                for t in range(first // P, (first + width) // P):
                     nc.tensor.transpose(turned_p[:, t, :], probs[:, t * P : (t + 1) * P], ident[:])
             p_turned.append(turned_p)
+        early_w = sb("early_w", [P, PACK, NQ], BF16)
+        for t in range(PACK):
+            nc.scalar.activation(early_w[:, t, :], p_turned[0][:, t, :], ACT.Copy, scale=slot_scale[0][:, t : t + 1])
         gather_values(0, 0, LAST)
         gather_values(1, HALF - LAST, HALF)
         for h in range(HALVES):
@@ -202,15 +203,17 @@ def tile_attend_soft_cap_gate_topkq128n1024t4096_kernel(tc, q_words, q_scales, k
         total = sb("total", [P, 1], F32)
         nc.scalar.activation(total[:], subtotal[:], ACT.Identity, bias=part_sum[2][:])
 
-        for h in range(HALVES):
-            nc.vector.tensor_tensor(
-                w_grouped[h][:], p_turned[h][:].rearrange("p t q -> p q t"),
-                slot_scale[h][:].unsqueeze(1).to_broadcast([P, NQ, PACK]), ALU.mult,
-            )
-        for h in range(HALVES):
-            quantize(w_codes[h], w_plane[h], w_grouped[h])
-        for h in range(HALVES):
-            quantize(v_codes[h], v_plane[h], v_grouped[h])
+        nc.vector.tensor_tensor(
+            w_grouped[:, 1], p_turned[1][:].rearrange("p t q -> p q t"),
+            slot_scale[1][:].unsqueeze(1).to_broadcast([P, NQ, PACK]), ALU.mult,
+        )
+        nc.vector.tensor_copy(w_grouped[:, 0], early_w[:].rearrange("p t q -> p q t"))
+        quantize(v_codes[0], v_plane[0], v_grouped[0])
+        nc.vector.quantize_mx(
+            out=w_codes[:].rearrange("p h q -> p (h q)").bitcast(FP8X4), scales=w_plane[:].rearrange("p h q -> p (h q)"),
+            in_=w_grouped[:].rearrange("p h q t -> p (h q t)"),
+        )
+        quantize(v_codes[1], v_plane[1], v_grouped[1])
         inv_total = sb("inv_total", [P, 1], F32, "v_grouped1")
         nc.vector.reciprocal(inv_total[:], total[:])
 
@@ -218,8 +221,8 @@ def tile_attend_soft_cap_gate_topkq128n1024t4096_kernel(tc, q_words, q_scales, k
         for h in range(HALVES):
             nc.tensor.matmul_mx(
                 out=acc[:],
-                lhsT=w_codes[h][:].bitcast(FP8X4),
-                lhsT_scale=w_plane[h][:],
+                lhsT=w_codes[:, h].bitcast(FP8X4),
+                lhsT_scale=w_plane[:, h],
                 rhs=v_codes[h][:].bitcast(FP8X4),
                 rhs_scale=v_plane[h][:],
                 start=(h == 0),

@@ -12,6 +12,7 @@ FP8X4 = mybir.dt.float8_e4m3fn_x4
 FP4X4 = mybir.dt.float4_e2m1fn_x4
 ACT = mybir.ActivationFunctionType
 ALU = mybir.AluOpType
+AX = mybir.AxisListType
 
 P = 128
 N, T, D, DV, NQ = 1024, 4096, 1024, 128, 128
@@ -22,12 +23,12 @@ HALVES = N // HALF
 PASSES = D // HALF
 QUAD = 32
 PIECE = HALF // 2
-LAST = 128
-PITCH = PIECE + HALF
-ZEROED = T // 4
-FILLER_AT = T
-SCALE_ROW = 68
-SCALE_AT = 0
+PIECES = N // PIECE
+SCALE_ROW = P - 1
+ROW_STEP = P // QUAD
+EARLY_VALUES = 768
+LEAD, TRAIL = 128, 192
+PITCH = PIECE + (N - LEAD - TRAIL) // 2
 
 FLOPS = 2 * NQ * N * (D + DV)
 BYTES = P * T * 4 + PASSES * 16 * T + DV * T * 4 + T * 4 + PASSES * (P * NQ * 4 + 16 * NQ) + 2 * NQ * DV * 4 + P * (N // 16) * 2
@@ -37,183 +38,164 @@ def tile_attend_soft_cap_gate_topkq128n1024t4096_kernel(tc, q_words, q_scales, k
     nc = tc.nc
     with ExitStack() as ctx:
         held = ctx.enter_context(tc.tile_pool(name="held", bufs=1))
-        shared = ctx.enter_context(tc.tile_pool(name="shared", bufs=1))
         psum = ctx.enter_context(tc.psum_pool(name="psum", bufs=1))
 
         def sb(name, shape, dtype, tag=""):
             return held.tile(shape, dtype, name=name, tag=tag or name, align_bytes=64)
 
-        def at(name, shape, dtype, offset):
-            return shared.tile(shape, dtype, name=name, offset=offset, align_bytes=64)
-
-        def bank(name, shape):
-            return psum.tile(shape, F32, name=name, tag=name)
+        def bank(name, shape, tag=""):
+            return psum.tile(shape, F32, name=name, tag=tag or name)
 
         offsets = held.tile([P, N // 16], U16, name="offsets")
         nc.sync.dma_start(offsets[:], offs)
 
-        def half_list(h):
-            return offsets[:, h * HALF // 16 : (h + 1) * HALF // 16]
+        def listed(n0, n1):
+            return offsets[:, n0 // 16 : n1 // 16]
 
-        key_scale_pool = at("key_scale_pool", [P, T], U8, SCALE_AT)
-        nc.sync.dma_start(key_scale_pool[0:QUAD, :].bitcast(I32), k_scales.rearrange("o f t -> f o t").bitcast(I32))
-        scale_filler = at("scale_filler", [P, QUAD], F32, FILLER_AT)
-        nc.scalar.dma_start(scale_filler[:], vs[:, 0:QUAD])
-        scale_rows = sb("scale_rows", [P, N + NQ], U8)
-        nc.scalar.dma_start(scale_rows[0:QUAD, N:].bitcast(I32), q_scales[0].rearrange("o f q -> f o q").bitcast(I32))
-        key_pool = sb("key_pool", [P, T], I32)
-        key_rows = k_words[0].rearrange("p t b -> p (t b)").bitcast(I32)
-        nc.sync.dma_start(key_pool[:], key_rows)
-        ones = sb("ones", [P, QUAD], F32)
-        nc.vector.memset(ones[:], 1.0)
-        scale_words = key_scale_pool[:].bitcast(I32)
-        nc.vector.memset(scale_words[QUAD : 2 * QUAD, :], 0)
-        column = sb("column", [P, QUAD], F32)
-        nc.vector.tensor_tensor_scan(column[:], ones[:], ones[:], 0.0, ALU.mult, ALU.add)
-        nc.vector.memset(scale_words[2 * QUAD :, :], 0)
-        row = sb("row", [P, QUAD], F32)
-        nc.vector.transpose(row[:], column[:])
         token_scale_pool = sb("token_scale_pool", [P, T], F32)
-        nc.vector.memset(token_scale_pool[:, :ZEROED], 0.0)
-        nc.scalar.activation(
-            token_scale_pool[:, ZEROED:].rearrange("p (x j) -> p x j", j=QUAD),
-            scale_filler[:].unsqueeze(1).to_broadcast([P, (T - ZEROED) // QUAD, QUAD]), ACT.Copy,
-        )
-        nc.sync.dma_start(token_scale_pool[SCALE_ROW : SCALE_ROW + 1, :], vs[0:1, :])
+        nc.scalar.dma_start(token_scale_pool[SCALE_ROW:, :], vs[0:1, :])
+        scale_rows = sb("scale_rows", [P, N + NQ], U8)
+        nc.scalar.dma_start(scale_rows[::ROW_STEP, N:].bitcast(I32), q_scales[0].rearrange("o f q -> f o q").bitcast(I32))
         q_codes = sb("q_codes", [P, PASSES, NQ], I32)
         nc.sync.dma_start(q_codes[:], q_words[0].rearrange("o p q r -> p o (q r)").bitcast(I32))
+        gate_in = sb("gate_in", [P, DV], F32)
+        nc.sync.dma_start(gate_in[:], og[0])
+
+        key_scale_pool = sb("key_scale_pool", [P, T], U8)
+        nc.vector.memset(key_scale_pool[:].bitcast(I32), 0)
+        nc.sync.dma_start(key_scale_pool[::ROW_STEP, :].bitcast(I32), k_scales.rearrange("o f t -> f o t").bitcast(I32))
+        key_pool = sb("key_pool", [P, T], I32)
+        nc.sync.dma_start(key_pool[:], k_words[0].rearrange("p t b -> p (t b)").bitcast(I32))
+        value_pool = sb("value_pool", [P, T], F32)
+        nc.sync.dma_start(value_pool[:, :EARLY_VALUES], vT[:, :EARLY_VALUES])
+        nc.vector.memset(token_scale_pool[:SCALE_ROW, :], 0.0)
 
         key_scale_rows = sb("key_scale_rows", [P, N], U8)
         nc.vector.tensor_copy(key_scale_rows[:], key_scale_pool[:].indirect(offsets[:]))
-        nc.vector.tensor_copy(scale_rows[0:QUAD, :N].bitcast(I32), key_scale_rows[0:QUAD, :].bitcast(I32))
-        block_ident = sb("block_ident", [P, QUAD], F32)
-        nc.vector.tensor_tensor(block_ident[:], column[:], row[:], ALU.is_equal)
+        ones = sb("ones", [P, QUAD], F32)
+        nc.vector.memset(ones[:], 1.0)
+        nc.vector.tensor_copy(scale_rows[:, :N].bitcast(I32), key_scale_rows[:].bitcast(I32))
+        column = sb("column", [P, QUAD], F32)
+        nc.vector.tensor_tensor_scan(column[:], ones[:], ones[:], 0.0, ALU.mult, ALU.add)
         ident = sb("ident", [P, P], F32)
         nc.vector.memset(ident[:], 0.0)
-        planes = at("planes", [P, PASSES, N + NQ], U8, SCALE_AT)
-        for quad in (0, 2, 1, 3):
-            nc.scalar.dma_start(
-                planes[quad * QUAD : quad * QUAD + PACK, :, :].bitcast(I32),
-                scale_rows[quad * PACK * PASSES : (quad + 1) * PACK * PASSES, :].bitcast(I32),
-            )
-
-        gate_in = at("gate_in", [P, DV], F32, FILLER_AT + 64 - 4 * DV)
-        nc.scalar.dma_start(gate_in[:], og[0])
-        value_pool = at("value_pool", [P, T], F32, FILLER_AT + 64)
-        nc.scalar.dma_start(value_pool[:], vT)
-        scratch = sb("scratch", [P, 2 * PITCH + DV], F32)
-        gate_tanh = scratch[:, PITCH + PIECE : PITCH + PIECE + DV]
-        nc.scalar.activation(gate_tanh, gate_in[:], ACT.Tanh, scale=0.5)
+        row = sb("row", [P, QUAD], F32)
+        nc.vector.transpose(row[:], column[:])
         for first in range(0, P, QUAD):
-            nc.scalar.copy(ident[first : first + QUAD, first : first + QUAD], block_ident[first : first + QUAD, :])
+            rows = slice(first, first + QUAD)
+            nc.vector.tensor_tensor(ident[rows, rows], column[rows, :], row[rows, :], ALU.is_equal)
+        planes = sb("planes", [P, PASSES, N + NQ], U8)
+        for quad in (0, 2, 1, 3):
+            nc.sync.dma_start(
+                planes[quad * QUAD : quad * QUAD + PACK, :, :].bitcast(I32),
+                scale_rows[quad * QUAD : (quad + 1) * QUAD : ROW_STEP, :].bitcast(I32),
+            )
+        nc.sync.dma_start(value_pool[:, EARLY_VALUES:], vT[:, EARLY_VALUES:])
 
-        capped = [scratch[:, 2 * PITCH + DV - HALF :], scratch[:, PIECE:PITCH]]
-        neg_late = scratch[:, : 2 * PITCH].rearrange("q (a x) -> q a x", x=PITCH)[:, :, :PIECE]
-        value_words = [
-            scratch[:, PITCH + PIECE - LAST // 2 : PITCH + HALF - LAST // 2],
-            scratch[:, PITCH + LAST // 2 - PIECE : PITCH + LAST // 2],
-        ]
+        token_scale = sb("token_scale", [P, N], F32)
+        slot_scale = [sb(f"slot_scale{h}", [P, PACK], F32) for h in range(HALVES)]
+        for h in range(HALVES):
+            nc.scalar.activation(token_scale[:, h * HALF : (h + 1) * HALF], token_scale_pool[:].indirect(listed(h * HALF, (h + 1) * HALF)), ACT.Copy)
+        for h in range(HALVES):
+            scale_turned = bank(f"scale_turned{h}", [P, PACK, P], f"turned{h}")
+            for t in range(PACK):
+                nc.tensor.transpose(scale_turned[:, t, :], token_scale[:, h * HALF + t : (h + 1) * HALF : PACK], ident[:])
+            nc.scalar.copy(slot_scale[h][:], scale_turned[:, :, SCALE_ROW])
+        gate_tanh = sb("gate_tanh", [P, DV], F32)
+        nc.scalar.activation(gate_tanh[:], gate_in[:], ACT.Tanh, scale=0.5)
+        gate = sb("gate", [P, DV], F32)
+        nc.scalar.activation(gate[:], gate_tanh[:], ACT.Copy, scale=0.5, bias=0.5)
 
-        pairs = sb("key_pairs", [P, HALVES, HALF], U32)
-        for h in range(HALVES):
-            nc.vector.tensor_copy(pairs[:, h], key_pool[:].bitcast(U32).indirect(half_list(h)))
-        for h in range(HALVES):
-            codes = sb(f"key_codes{h}", [P, PASSES, 2 * HALF], U8, f"codes{h}")
-            nc.vector.tensor_copy(codes[:].bitcast(U16), pairs[:, h].bitcast(U16).rearrange("p (n o) -> p o n", o=PASSES))
-            scores = bank(f"scores{h}", [P, HALF])
+        pairs = [sb(f"key_pairs{i}", [P, PIECE], U32) for i in range(PIECES)]
+        width = PIECE // PACK
+        capped_early = sb("capped_early", [P, PACK, P], F32)
+        capped_third = sb("capped_third", [P, PACK, width], F32)
+        neg_early = sb("neg_early", [P, 2, PIECE], F32)
+        scratch = sb("scratch", [P, 2, PITCH], F32)
+        capped_last = scratch[:, 0, PIECE : 2 * PIECE].rearrange("q (t p) -> q t p", t=PACK)
+        capped = [capped_early[:, :, :width], capped_early[:, :, width:], capped_third[:], capped_last]
+        negated = [neg_early[:], scratch[:, :, :PIECE]]
+        values = scratch[:].rearrange("e a x -> e (a x)").bitcast(BF16)[:, 2 * PIECE - LEAD : 2 * PIECE - LEAD + N]
+        neg_max = [sb(f"neg_max{i}", [P, 1], F32) for i in range(3)]
+
+        def gather_keys(i):
+            nc.vector.tensor_copy(pairs[i][:], key_pool[:].bitcast(U32).indirect(listed(i * PIECE, (i + 1) * PIECE)))
+
+        def score(i):
+            codes = sb(f"key_codes{i}", [P, PASSES, 2 * PIECE], U8)
+            nc.vector.tensor_copy(codes[:].bitcast(U16), pairs[i][:].bitcast(U16).rearrange("p (n o) -> p o n", o=PASSES))
+            scores = bank(f"scores{i}", [P, PIECE])
             for o in range(PASSES):
                 nc.tensor.matmul_mx(
                     out=scores[:],
                     lhsT=q_codes[:, o, :].bitcast(FP8X4),
                     lhsT_scale=planes[:, o, N:],
                     rhs=codes[:, o, :].bitcast(FP4X4),
-                    rhs_scale=planes[:, o, h * HALF : (h + 1) * HALF],
+                    rhs_scale=planes[:, o, i * PIECE : (i + 1) * PIECE],
                     start=(o == 0),
                     stop=(o == PASSES - 1),
                 )
-            nc.scalar.activation(
-                capped[h].rearrange("q (t p) -> q t p", t=PACK), scores[:].rearrange("q (p t) -> q t p", t=PACK), ACT.Tanh, scale=1.0 / CAP
+            nc.scalar.activation(capped[i], scores[:].rearrange("q (p t) -> q t p", t=PACK), ACT.Tanh, scale=1.0 / CAP)
+
+        def row_max(i, target, source):
+            nc.vector.tensor_scalar(target, source, -CAP, neg_max[i - 1][:] if i else None, ALU.mult, ALU.min, accum_out=neg_max[i][:])
+
+        gather_keys(0)
+        for i in range(PIECES):
+            if i + 1 < PIECES:
+                gather_keys(i + 1)
+            score(i)
+        row_max(0, neg_early[:].rearrange("q a x -> q (a x)"), capped_early[:].rearrange("q t p -> q (t p)"))
+        for part in range(2):
+            row_max(
+                1 + part, negated[1].rearrange("q a (t p) -> q a t p", p=P)[:, :, :, part * width : (part + 1) * width],
+                capped[2 + part].rearrange("q (a t) p -> q a t p", a=2),
             )
-            if h == 0:
-                gate = sb("gate", [P, DV], F32, "codes0")
-                nc.scalar.activation(gate[:], gate_tanh, ACT.Copy, scale=0.5, bias=0.5)
 
-        token_scale = sb("token_scale", [P, N], F32)
-        nc.vector.tensor_copy(token_scale[:], token_scale_pool[:].indirect(offsets[:]))
-        slot_scale = [sb(f"slot_scale{h}", [P, PACK], F32) for h in range(HALVES)]
+        nc.vector.tensor_copy(values[:, LEAD : N - TRAIL], value_pool[:].indirect(listed(LEAD, N - TRAIL)))
+
+        part_sum = sb("part_sum", [P, PIECES], F32)
+        p_turned = []
         for h in range(HALVES):
-            nc.sync.dma_start(slot_scale[h][:], token_scale[SCALE_ROW : SCALE_ROW + 1, h * HALF : (h + 1) * HALF].rearrange("o (p t) -> o p t", t=PACK))
+            probs = sb(f"probs{h}", [P, PACK, P], F32)
+            turned_p = bank(f"p_turned{h}", [P, PACK, NQ], f"turned{h}")
+            for first in range(0, PACK, 2):
+                i = h * 2 + first // 2
+                nc.scalar.activation(
+                    probs[:, first : first + 2].rearrange("q t p -> q (t p)"), negated[h][:, first // 2], ACT.Exp,
+                    bias=neg_max[-1][:], scale=-1.0, accum_out=part_sum[:, i : i + 1],
+                )
+                for t in range(first, first + 2):
+                    nc.tensor.transpose(turned_p[:, t, :], probs[:, t], ident[:])
+            p_turned.append(turned_p)
 
-        neg_early = sb("neg_early", [P, HALF], F32)
-        neg_max = [sb(f"neg_max{i}", [P, 1], F32) for i in range(HALVES)]
-        v_turned = [bank(f"v_turned{h}", [P, 2, DV]) for h in range(HALVES)]
-        v_grouped = [sb(f"v_grouped{h}", [P, DV, PACK], BF16, f"v_grouped{h}") for h in range(HALVES)]
+        for n0, n1 in ((0, LEAD), (N - TRAIL, N)):
+            nc.scalar.activation(values[:, n0:n1], value_pool[:].indirect(listed(n0, n1)), ACT.Copy)
+
+        v_grouped = [sb(f"v_grouped{h}", [P, DV, PACK], BF16) for h in range(HALVES)]
         w_grouped = sb("w_grouped", [P, HALVES, NQ, PACK], BF16)
         v_codes = [sb(f"v_codes{h}", [P, DV], U32) for h in range(HALVES)]
         v_plane = [sb(f"v_plane{h}", [P, DV], U8) for h in range(HALVES)]
         w_codes = sb("w_codes", [P, HALVES, NQ], U32)
         w_plane = sb("w_plane", [P, HALVES, NQ], U8)
 
-        def gather_values(h, n0, n1):
-            listed = offsets[:, (h * HALF + n0) // 16 : (h * HALF + n1) // 16]
-            nc.vector.tensor_copy(value_words[h].bitcast(BF16)[:, n0:n1], value_pool[:].indirect(listed))
-
-        def turn_values(h):
-            words = value_words[h]
-            for u in range(2):
-                nc.tensor.transpose(v_turned[h][:, u, :], words[:, u::2], ident[:])
-            nc.scalar.copy(v_grouped[h][:].bitcast(F32), v_turned[h][:].rearrange("p u e -> p e u"))
-
-        def quantize(codes, plane, grouped):
-            nc.vector.quantize_mx(out=codes[:].bitcast(FP8X4), scales=plane[:], in_=grouped[:].rearrange("p x t -> p (x t)"))
-
-        def row_max(i, negated, capped):
-            nc.vector.tensor_scalar(negated, capped, -CAP, neg_max[i - 1][:] if i else None, ALU.mult, ALU.min, accum_out=neg_max[i][:])
-
-        row_max(0, neg_early[:], capped[0])
-        gather_values(0, LAST, 2 * LAST)
-        row_max(1, neg_late, capped[1].rearrange("q (a x) -> q a x", x=PIECE))
-        gather_values(0, 2 * LAST, HALF)
-        gather_values(1, 0, HALF - LAST)
-
-        part_sum = []
-        p_turned = []
-        for h, pieces in enumerate([[(0, neg_early[:])], [(PIECE, neg_late[:, 1]), (0, neg_late[:, 0])]]):
-            probs = sb(f"probs{h}", [P, PACK * P], F32)
-            turned_p = bank(f"p_turned{h}", [P, PACK, NQ])
-            width = HALF // len(pieces)
-            for first, piece in pieces:
-                part_sum.append(sb(f"part_sum{h}_{first}", [P, 1], F32))
-                nc.scalar.activation(
-                    probs[:, first : first + width], piece, ACT.Exp,
-                    bias=neg_max[-1][:], scale=-1.0, accum_out=part_sum[-1][:],
-                )
-                for t in range(first // P, (first + width) // P):
-                    nc.tensor.transpose(turned_p[:, t, :], probs[:, t * P : (t + 1) * P], ident[:])
-            p_turned.append(turned_p)
-        early_w = sb("early_w", [P, PACK, NQ], BF16)
-        for t in range(PACK):
-            nc.scalar.activation(early_w[:, t, :], p_turned[0][:, t, :], ACT.Copy, scale=slot_scale[0][:, t : t + 1])
-        gather_values(0, 0, LAST)
-        gather_values(1, HALF - LAST, HALF)
         for h in range(HALVES):
-            turn_values(h)
-        subtotal = sb("subtotal", [P, 1], F32)
-        nc.scalar.activation(subtotal[:], part_sum[0][:], ACT.Identity, bias=part_sum[1][:])
-        total = sb("total", [P, 1], F32)
-        nc.scalar.activation(total[:], subtotal[:], ACT.Identity, bias=part_sum[2][:])
+            words = values[:, h * HALF : (h + 1) * HALF].bitcast(F32)
+            v_turned = bank(f"v_turned{h}", [P, 2, DV], f"scores{h}")
+            for u in range(2):
+                nc.tensor.transpose(v_turned[:, u, :], words[:, u::2], ident[:])
+            nc.scalar.copy(v_grouped[h][:].bitcast(F32), v_turned[:].rearrange("p u e -> p e u"))
 
-        nc.vector.tensor_tensor(
-            w_grouped[:, 1], p_turned[1][:].rearrange("p t q -> p q t"),
-            slot_scale[1][:].unsqueeze(1).to_broadcast([P, NQ, PACK]), ALU.mult,
-        )
-        nc.vector.tensor_copy(w_grouped[:, 0], early_w[:].rearrange("p t q -> p q t"))
-        quantize(v_codes[0], v_plane[0], v_grouped[0])
-        nc.vector.quantize_mx(
-            out=w_codes[:].rearrange("p h q -> p (h q)").bitcast(FP8X4), scales=w_plane[:].rearrange("p h q -> p (h q)"),
-            in_=w_grouped[:].rearrange("p h q t -> p (h q t)"),
-        )
-        quantize(v_codes[1], v_plane[1], v_grouped[1])
+        for h in range(HALVES):
+            nc.vector.tensor_tensor(
+                w_grouped[:, h], p_turned[h][:].rearrange("p t q -> p q t"),
+                slot_scale[h][:].unsqueeze(1).to_broadcast([P, NQ, PACK]), ALU.mult,
+            )
+        total = sb("total", [P, 1], F32)
+        nc.vector.tensor_reduce(total[:], part_sum[:], AX.X, ALU.add)
+        for h in range(HALVES):
+            nc.vector.quantize_mx(out=w_codes[:, h].bitcast(FP8X4), scales=w_plane[:, h], in_=w_grouped[:, h].rearrange("p q t -> p (q t)"))
+            nc.vector.quantize_mx(out=v_codes[h][:].bitcast(FP8X4), scales=v_plane[h][:], in_=v_grouped[h][:].rearrange("p x t -> p (x t)"))
         inv_total = sb("inv_total", [P, 1], F32, "v_grouped1")
         nc.vector.reciprocal(inv_total[:], total[:])
 

@@ -25,8 +25,8 @@ QUAD = 32
 PIECE = HALF // 2
 PIECES = N // PIECE
 SCALE_ROW = P - 1
-ROW_STEP = P // QUAD
-EARLY_VALUES = 768
+ZERO_PIECE = T // 4
+ODD_CUT = T // 8 + 1
 LEAD, TRAIL = 128, 192
 PITCH = PIECE + (N - LEAD - TRAIL) // 2
 
@@ -46,6 +46,8 @@ def tile_attend_soft_cap_gate_topkq128n1024t4096_kernel(tc, q_words, q_scales, k
         def bank(name, shape, tag=""):
             return psum.tile(shape, F32, name=name, tag=tag or name)
 
+        key_scale_pool = sb("key_scale_pool", [P, T], U8)
+        nc.sync.dma_start(key_scale_pool[0:QUAD, :].bitcast(I32), k_scales.rearrange("o f t -> f o t").bitcast(I32))
         offsets = held.tile([P, N // 16], U16, name="offsets")
         nc.sync.dma_start(offsets[:], offs)
 
@@ -55,75 +57,72 @@ def tile_attend_soft_cap_gate_topkq128n1024t4096_kernel(tc, q_words, q_scales, k
         token_scale_pool = sb("token_scale_pool", [P, T], F32)
         nc.scalar.dma_start(token_scale_pool[SCALE_ROW:, :], vs[0:1, :])
         scale_rows = sb("scale_rows", [P, N + NQ], U8)
-        nc.scalar.dma_start(scale_rows[::ROW_STEP, N:].bitcast(I32), q_scales[0].rearrange("o f q -> f o q").bitcast(I32))
+        nc.scalar.dma_start(scale_rows[0:QUAD, N:].bitcast(I32), q_scales[0].rearrange("o f q -> f o q").bitcast(I32))
+        key_pool = sb("key_pool", [P, T], I32)
+        nc.sync.dma_start(key_pool[:], k_words[0].rearrange("p t b -> p (t b)").bitcast(I32))
         q_codes = sb("q_codes", [P, PASSES, NQ], I32)
         nc.sync.dma_start(q_codes[:], q_words[0].rearrange("o p q r -> p o (q r)").bitcast(I32))
         gate_in = sb("gate_in", [P, DV], F32)
         nc.sync.dma_start(gate_in[:], og[0])
 
-        key_scale_pool = sb("key_scale_pool", [P, T], U8)
-        nc.vector.memset(key_scale_pool[:].bitcast(I32), 0)
-        nc.sync.dma_start(key_scale_pool[::ROW_STEP, :].bitcast(I32), k_scales.rearrange("o f t -> f o t").bitcast(I32))
-        key_pool = sb("key_pool", [P, T], I32)
-        nc.sync.dma_start(key_pool[:], k_words[0].rearrange("p t b -> p (t b)").bitcast(I32))
-        value_pool = sb("value_pool", [P, T], F32)
-        nc.sync.dma_start(value_pool[:, :EARLY_VALUES], vT[:, :EARLY_VALUES])
-        nc.vector.memset(token_scale_pool[:SCALE_ROW, :], 0.0)
+        ones = sb("ones", [P, QUAD], F32)
+        nc.gpsimd.memset(ones[:], 1.0)
+        scale_words = key_scale_pool[:].bitcast(I32)
+        nc.gpsimd.memset(scale_words[QUAD : 2 * QUAD, :], 0)
+        for first in range(ZERO_PIECE, T, ZERO_PIECE):
+            nc.gpsimd.memset(token_scale_pool[:SCALE_ROW, first : first + ZERO_PIECE], 0.0)
+        ident = sb("ident", [P, P], F32)
+        nc.gpsimd.memset(ident[:], 0.0)
+        for window in (scale_words[2 * QUAD :, :], token_scale_pool[:SCALE_ROW, :ZERO_PIECE]):
+            for columns in (slice(0, ODD_CUT), slice(ODD_CUT, ZERO_PIECE)):
+                nc.vector.memset(window[:, columns], 0)
 
         key_scale_rows = sb("key_scale_rows", [P, N], U8)
         nc.vector.tensor_copy(key_scale_rows[:], key_scale_pool[:].indirect(offsets[:]))
-        ones = sb("ones", [P, QUAD], F32)
-        nc.vector.memset(ones[:], 1.0)
-        nc.vector.tensor_copy(scale_rows[:, :N].bitcast(I32), key_scale_rows[:].bitcast(I32))
-        column = sb("column", [P, QUAD], F32)
+        column = sb("column", [P, QUAD], F32, "column")
         nc.vector.tensor_tensor_scan(column[:], ones[:], ones[:], 0.0, ALU.mult, ALU.add)
-        ident = sb("ident", [P, P], F32)
-        nc.vector.memset(ident[:], 0.0)
+        nc.vector.tensor_copy(scale_rows[0:QUAD, :N].bitcast(I32), key_scale_rows[0:QUAD, :].bitcast(I32))
         row = sb("row", [P, QUAD], F32)
         nc.vector.transpose(row[:], column[:])
-        for first in range(0, P, QUAD):
-            rows = slice(first, first + QUAD)
-            nc.vector.tensor_tensor(ident[rows, rows], column[rows, :], row[rows, :], ALU.is_equal)
         planes = sb("planes", [P, PASSES, N + NQ], U8)
         for quad in (0, 2, 1, 3):
             nc.sync.dma_start(
                 planes[quad * QUAD : quad * QUAD + PACK, :, :].bitcast(I32),
-                scale_rows[quad * QUAD : (quad + 1) * QUAD : ROW_STEP, :].bitcast(I32),
+                scale_rows[quad * PACK * PASSES : (quad + 1) * PACK * PASSES, :].bitcast(I32),
             )
-        nc.sync.dma_start(value_pool[:, EARLY_VALUES:], vT[:, EARLY_VALUES:])
+        value_pool = sb("value_pool", [P, T], F32)
+        nc.sync.dma_start(value_pool[:], vT)
 
         token_scale = sb("token_scale", [P, N], F32)
         slot_scale = [sb(f"slot_scale{h}", [P, PACK], F32) for h in range(HALVES)]
+        nc.scalar.activation(token_scale[:], token_scale_pool[:].indirect(offsets[:]), ACT.Copy)
         for h in range(HALVES):
-            nc.scalar.activation(token_scale[:, h * HALF : (h + 1) * HALF], token_scale_pool[:].indirect(listed(h * HALF, (h + 1) * HALF)), ACT.Copy)
-        for h in range(HALVES):
-            scale_turned = bank(f"scale_turned{h}", [P, PACK, P], f"turned{h}")
-            for t in range(PACK):
-                nc.tensor.transpose(scale_turned[:, t, :], token_scale[:, h * HALF + t : (h + 1) * HALF : PACK], ident[:])
-            nc.scalar.copy(slot_scale[h][:], scale_turned[:, :, SCALE_ROW])
-        gate_tanh = sb("gate_tanh", [P, DV], F32)
-        nc.scalar.activation(gate_tanh[:], gate_in[:], ACT.Tanh, scale=0.5)
-        gate = sb("gate", [P, DV], F32)
-        nc.scalar.activation(gate[:], gate_tanh[:], ACT.Copy, scale=0.5, bias=0.5)
+            nc.sync.dma_start(slot_scale[h][:], token_scale[SCALE_ROW:, h * HALF : (h + 1) * HALF].rearrange("o (p t) -> o p t", t=PACK))
+        distance = sb("distance", [P, QUAD], F32)
+        nc.scalar.activation(distance[:], column[:], ACT.Abs, scale=-1.0, bias=row[:, 0:1])
+        for first in range(0, P, QUAD):
+            rows = slice(first, first + QUAD)
+            nc.scalar.activation(ident[rows, rows], distance[rows, :], ACT.Relu, scale=-1.0, bias=1.0)
 
-        pairs = [sb(f"key_pairs{i}", [P, PIECE], U32) for i in range(PIECES)]
         width = PIECE // PACK
         capped_early = sb("capped_early", [P, PACK, P], F32)
         capped_third = sb("capped_third", [P, PACK, width], F32)
         neg_early = sb("neg_early", [P, 2, PIECE], F32)
-        scratch = sb("scratch", [P, 2, PITCH], F32)
-        capped_last = scratch[:, 0, PIECE : 2 * PIECE].rearrange("q (t p) -> q t p", t=PACK)
+        scratch = sb("scratch", [P, 2 * PITCH], F32)
+        capped_last = scratch[:, PIECE : 2 * PIECE].rearrange("q (t p) -> q t p", t=PACK)
         capped = [capped_early[:, :, :width], capped_early[:, :, width:], capped_third[:], capped_last]
-        negated = [neg_early[:], scratch[:, :, :PIECE]]
-        values = scratch[:].rearrange("e a x -> e (a x)").bitcast(BF16)[:, 2 * PIECE - LEAD : 2 * PIECE - LEAD + N]
+        negated = [neg_early[:], scratch[:].rearrange("q (a x) -> q a x", a=2)[:, :, :PIECE]]
+        values = scratch[:].bitcast(BF16)[:, 2 * PIECE - LEAD : 2 * PIECE - LEAD + N]
         neg_max = [sb(f"neg_max{i}", [P, 1], F32) for i in range(3)]
 
         def gather_keys(i):
-            nc.vector.tensor_copy(pairs[i][:], key_pool[:].bitcast(U32).indirect(listed(i * PIECE, (i + 1) * PIECE)))
+            pairs = sb(f"key_pairs{i}", [P, PIECE], U32, f"key_pairs{i % 2}")
+            nc.vector.tensor_copy(pairs[:], key_pool[:].bitcast(U32).indirect(listed(i * PIECE, (i + 1) * PIECE)))
+            return pairs
 
-        def score(i):
+        def score(i, pairs):
             codes = sb(f"key_codes{i}", [P, PASSES, 2 * PIECE], U8)
-            nc.vector.tensor_copy(codes[:].bitcast(U16), pairs[i][:].bitcast(U16).rearrange("p (n o) -> p o n", o=PASSES))
+            nc.vector.tensor_copy(codes[:].bitcast(U16), pairs[:].bitcast(U16).rearrange("p (n o) -> p o n", o=PASSES))
             scores = bank(f"scores{i}", [P, PIECE])
             for o in range(PASSES):
                 nc.tensor.matmul_mx(
@@ -140,11 +139,14 @@ def tile_attend_soft_cap_gate_topkq128n1024t4096_kernel(tc, q_words, q_scales, k
         def row_max(i, target, source):
             nc.vector.tensor_scalar(target, source, -CAP, neg_max[i - 1][:] if i else None, ALU.mult, ALU.min, accum_out=neg_max[i][:])
 
-        gather_keys(0)
-        for i in range(PIECES):
-            if i + 1 < PIECES:
-                gather_keys(i + 1)
-            score(i)
+        for h in range(HALVES):
+            gathered = [gather_keys(2 * h + part) for part in range(2)]
+            for part in range(2):
+                score(2 * h + part, gathered[part])
+        gate_tanh = sb("gate_tanh", [P, DV], F32, f"key_codes{PIECES - 1}")
+        nc.scalar.activation(gate_tanh[:], gate_in[:], ACT.Tanh, scale=0.5)
+        gate = sb("gate", [P, DV], F32)
+        nc.scalar.activation(gate[:], gate_tanh[:], ACT.Copy, scale=0.5, bias=0.5)
         row_max(0, neg_early[:].rearrange("q a x -> q (a x)"), capped_early[:].rearrange("q t p -> q (t p)"))
         for part in range(2):
             row_max(
@@ -191,7 +193,7 @@ def tile_attend_soft_cap_gate_topkq128n1024t4096_kernel(tc, q_words, q_scales, k
                 w_grouped[:, h], p_turned[h][:].rearrange("p t q -> p q t"),
                 slot_scale[h][:].unsqueeze(1).to_broadcast([P, NQ, PACK]), ALU.mult,
             )
-        total = sb("total", [P, 1], F32)
+        total = sb("total", [P, 1], F32, "slot_scale0")
         nc.vector.tensor_reduce(total[:], part_sum[:], AX.X, ALU.add)
         for h in range(HALVES):
             nc.vector.quantize_mx(out=w_codes[:, h].bitcast(FP8X4), scales=w_plane[:, h], in_=w_grouped[:, h].rearrange("p q t -> p (q t)"))

@@ -12,7 +12,6 @@ FP8X4 = mybir.dt.float8_e4m3fn_x4
 FP4X4 = mybir.dt.float4_e2m1fn_x4
 ACT = mybir.ActivationFunctionType
 ALU = mybir.AluOpType
-AX = mybir.AxisListType
 
 P = 128
 N, T, D, DV, NQ = 1024, 4096, 1024, 128, 128
@@ -27,8 +26,8 @@ PIECES = N // PIECE
 SCALE_ROW = P - 1
 ZERO_PIECE = T // 4
 ODD_CUT = T // 8 + 1
-LEAD, TRAIL = 128, 192
-PITCH = PIECE + (N - LEAD - TRAIL) // 2
+EARLY_VALUES = 640
+LEAD, TRAIL = 128, 160
 
 FLOPS = 2 * NQ * N * (D + DV)
 BYTES = P * T * 4 + PASSES * 16 * T + DV * T * 4 + T * 4 + PASSES * (P * NQ * 4 + 16 * NQ) + 2 * NQ * DV * 4 + P * (N // 16) * 2
@@ -62,8 +61,8 @@ def tile_attend_soft_cap_gate_topkq128n1024t4096_kernel(tc, q_words, q_scales, k
         nc.sync.dma_start(key_pool[:], k_words[0].rearrange("p t b -> p (t b)").bitcast(I32))
         q_codes = sb("q_codes", [P, PASSES, NQ], I32)
         nc.sync.dma_start(q_codes[:], q_words[0].rearrange("o p q r -> p o (q r)").bitcast(I32))
-        gate_in = sb("gate_in", [P, DV], F32)
-        nc.sync.dma_start(gate_in[:], og[0])
+        value_pool = sb("value_pool", [P, T], F32)
+        nc.sync.dma_start(value_pool[:, :EARLY_VALUES], vT[:, :EARLY_VALUES])
 
         ones = sb("ones", [P, QUAD], F32)
         nc.gpsimd.memset(ones[:], 1.0)
@@ -90,14 +89,15 @@ def tile_attend_soft_cap_gate_topkq128n1024t4096_kernel(tc, q_words, q_scales, k
                 planes[quad * QUAD : quad * QUAD + PACK, :, :].bitcast(I32),
                 scale_rows[quad * PACK * PASSES : (quad + 1) * PACK * PASSES, :].bitcast(I32),
             )
-        value_pool = sb("value_pool", [P, T], F32)
-        nc.sync.dma_start(value_pool[:], vT)
+        nc.sync.dma_start(value_pool[:, EARLY_VALUES:], vT[:, EARLY_VALUES:])
 
         token_scale = sb("token_scale", [P, N], F32)
         slot_scale = [sb(f"slot_scale{h}", [P, PACK], F32) for h in range(HALVES)]
         nc.scalar.activation(token_scale[:], token_scale_pool[:].indirect(offsets[:]), ACT.Copy)
         for h in range(HALVES):
             nc.sync.dma_start(slot_scale[h][:], token_scale[SCALE_ROW:, h * HALF : (h + 1) * HALF].rearrange("o (p t) -> o p t", t=PACK))
+        gate_in = sb("gate_in", [P, DV], F32)
+        nc.sync.dma_start(gate_in[:], og[0])
         distance = sb("distance", [P, QUAD], F32)
         nc.scalar.activation(distance[:], column[:], ACT.Abs, scale=-1.0, bias=row[:, 0:1])
         for first in range(0, P, QUAD):
@@ -106,13 +106,11 @@ def tile_attend_soft_cap_gate_topkq128n1024t4096_kernel(tc, q_words, q_scales, k
 
         width = PIECE // PACK
         capped_early = sb("capped_early", [P, PACK, P], F32)
-        capped_third = sb("capped_third", [P, PACK, width], F32)
-        neg_early = sb("neg_early", [P, 2, PIECE], F32)
-        scratch = sb("scratch", [P, 2 * PITCH], F32)
-        capped_last = scratch[:, PIECE : 2 * PIECE].rearrange("q (t p) -> q t p", t=PACK)
-        capped = [capped_early[:, :, :width], capped_early[:, :, width:], capped_third[:], capped_last]
-        negated = [neg_early[:], scratch[:].rearrange("q (a x) -> q a x", a=2)[:, :, :PIECE]]
-        values = scratch[:].bitcast(BF16)[:, 2 * PIECE - LEAD : 2 * PIECE - LEAD + N]
+        capped_late = [sb(f"capped_late{part}", [P, PACK, width], F32) for part in range(2)]
+        capped = [capped_early[:, :, :width], capped_early[:, :, width:], capped_late[0][:], capped_late[1][:]]
+        negated = sb("negated", [P, N], F32)
+        value_words = sb("value_words", [P, N // 2], F32)
+        values = value_words[:].bitcast(BF16)
         neg_max = [sb(f"neg_max{i}", [P, 1], F32) for i in range(3)]
 
         def gather_keys(i):
@@ -143,37 +141,26 @@ def tile_attend_soft_cap_gate_topkq128n1024t4096_kernel(tc, q_words, q_scales, k
             gathered = [gather_keys(2 * h + part) for part in range(2)]
             for part in range(2):
                 score(2 * h + part, gathered[part])
-        gate_tanh = sb("gate_tanh", [P, DV], F32, f"key_codes{PIECES - 1}")
-        nc.scalar.activation(gate_tanh[:], gate_in[:], ACT.Tanh, scale=0.5)
-        gate = sb("gate", [P, DV], F32)
-        nc.scalar.activation(gate[:], gate_tanh[:], ACT.Copy, scale=0.5, bias=0.5)
-        row_max(0, neg_early[:].rearrange("q a x -> q (a x)"), capped_early[:].rearrange("q t p -> q (t p)"))
+        row_max(0, negated[:, :HALF], capped_early[:].rearrange("q t p -> q (t p)"))
         for part in range(2):
-            row_max(
-                1 + part, negated[1].rearrange("q a (t p) -> q a t p", p=P)[:, :, :, part * width : (part + 1) * width],
-                capped[2 + part].rearrange("q (a t) p -> q a t p", a=2),
-            )
+            row_max(1 + part, negated[:, HALF:].rearrange("q (t p) -> q t p", p=P)[:, :, part * width : (part + 1) * width], capped[2 + part])
 
         nc.vector.tensor_copy(values[:, LEAD : N - TRAIL], value_pool[:].indirect(listed(LEAD, N - TRAIL)))
 
-        part_sum = sb("part_sum", [P, PIECES], F32)
-        p_turned = []
-        for h in range(HALVES):
-            probs = sb(f"probs{h}", [P, PACK, P], F32)
-            turned_p = bank(f"p_turned{h}", [P, PACK, NQ], f"turned{h}")
-            for first in range(0, PACK, 2):
-                i = h * 2 + first // 2
-                nc.scalar.activation(
-                    probs[:, first : first + 2].rearrange("q t p -> q (t p)"), negated[h][:, first // 2], ACT.Exp,
-                    bias=neg_max[-1][:], scale=-1.0, accum_out=part_sum[:, i : i + 1],
-                )
-                for t in range(first, first + 2):
-                    nc.tensor.transpose(turned_p[:, t, :], probs[:, t], ident[:])
-            p_turned.append(turned_p)
+        part_sum = sb("part_sum", [P, 3], F32)
+        probs = sb("probs", [P, N], F32)
+        p_turned = [bank(f"p_turned{h}", [P, PACK, NQ]) for h in range(HALVES)]
+        for i, (first, last) in enumerate([(0, HALF), (HALF, HALF + PIECE), (HALF + PIECE, N)]):
+            nc.scalar.activation(probs[:, first:last], negated[:, first:last], ACT.Exp, bias=neg_max[-1][:], scale=-1.0, accum_out=part_sum[:, i : i + 1])
+            for block in range(first // P, last // P):
+                nc.tensor.transpose(p_turned[block // PACK][:, block % PACK, :], probs[:, block * P : (block + 1) * P], ident[:])
 
         for n0, n1 in ((0, LEAD), (N - TRAIL, N)):
             nc.scalar.activation(values[:, n0:n1], value_pool[:].indirect(listed(n0, n1)), ACT.Copy)
 
+        part_copy = sb("part_copy", [P, 3], F32)
+        total = sb("total", [P, 1], F32)
+        nc.scalar.activation(part_copy[:], part_sum[:], ACT.Copy, accum_out=total[:])
         v_grouped = [sb(f"v_grouped{h}", [P, DV, PACK], BF16) for h in range(HALVES)]
         w_grouped = sb("w_grouped", [P, HALVES, NQ, PACK], BF16)
         v_codes = [sb(f"v_codes{h}", [P, DV], U32) for h in range(HALVES)]
@@ -187,14 +174,16 @@ def tile_attend_soft_cap_gate_topkq128n1024t4096_kernel(tc, q_words, q_scales, k
             for u in range(2):
                 nc.tensor.transpose(v_turned[:, u, :], words[:, u::2], ident[:])
             nc.scalar.copy(v_grouped[h][:].bitcast(F32), v_turned[:].rearrange("p u e -> p e u"))
+        gate_tanh = values[:, N - 2 * DV :].bitcast(F32)
+        nc.scalar.activation(gate_tanh, gate_in[:], ACT.Tanh, scale=0.5)
+        gate = sb("gate", [P, DV], F32)
+        nc.scalar.activation(gate[:], gate_tanh, ACT.Copy, scale=0.5, bias=0.5)
 
         for h in range(HALVES):
             nc.vector.tensor_tensor(
                 w_grouped[:, h], p_turned[h][:].rearrange("p t q -> p q t"),
                 slot_scale[h][:].unsqueeze(1).to_broadcast([P, NQ, PACK]), ALU.mult,
             )
-        total = sb("total", [P, 1], F32, "slot_scale0")
-        nc.vector.tensor_reduce(total[:], part_sum[:], AX.X, ALU.add)
         for h in range(HALVES):
             nc.vector.quantize_mx(out=w_codes[:, h].bitcast(FP8X4), scales=w_plane[:, h], in_=w_grouped[:, h].rearrange("p q t -> p (q t)"))
             nc.vector.quantize_mx(out=v_codes[h][:].bitcast(FP8X4), scales=v_plane[h][:], in_=v_grouped[h][:].rearrange("p x t -> p (x t)"))

@@ -26,8 +26,7 @@ PIECES = N // PIECE
 SCALE_ROW = P - 1
 ZERO_PIECE = T // 4
 ODD_CUT = T // 8 + 1
-EARLY_VALUES = 640
-LEAD, TRAIL = 128, 160
+LEAD, TRAIL = 128, 192
 
 FLOPS = 2 * NQ * N * (D + DV)
 BYTES = P * T * 4 + PASSES * 16 * T + DV * T * 4 + T * 4 + PASSES * (P * NQ * 4 + 16 * NQ) + 2 * NQ * DV * 4 + P * (N // 16) * 2
@@ -53,16 +52,14 @@ def tile_attend_soft_cap_gate_topkq128n1024t4096_kernel(tc, q_words, q_scales, k
         def listed(n0, n1):
             return offsets[:, n0 // 16 : n1 // 16]
 
-        token_scale_pool = sb("token_scale_pool", [P, T], F32)
-        nc.scalar.dma_start(token_scale_pool[SCALE_ROW:, :], vs[0:1, :])
         scale_rows = sb("scale_rows", [P, N + NQ], U8)
         nc.scalar.dma_start(scale_rows[0:QUAD, N:].bitcast(I32), q_scales[0].rearrange("o f q -> f o q").bitcast(I32))
+        token_scale_pool = sb("token_scale_pool", [P, T], F32)
+        nc.scalar.dma_start(token_scale_pool[SCALE_ROW:, :], vs[0:1, :])
         key_pool = sb("key_pool", [P, T], I32)
         nc.sync.dma_start(key_pool[:], k_words[0].rearrange("p t b -> p (t b)").bitcast(I32))
         q_codes = sb("q_codes", [P, PASSES, NQ], I32)
         nc.sync.dma_start(q_codes[:], q_words[0].rearrange("o p q r -> p o (q r)").bitcast(I32))
-        value_pool = sb("value_pool", [P, T], F32)
-        nc.sync.dma_start(value_pool[:, :EARLY_VALUES], vT[:, :EARLY_VALUES])
 
         ones = sb("ones", [P, QUAD], F32)
         nc.gpsimd.memset(ones[:], 1.0)
@@ -89,7 +86,8 @@ def tile_attend_soft_cap_gate_topkq128n1024t4096_kernel(tc, q_words, q_scales, k
                 planes[quad * QUAD : quad * QUAD + PACK, :, :].bitcast(I32),
                 scale_rows[quad * PACK * PASSES : (quad + 1) * PACK * PASSES, :].bitcast(I32),
             )
-        nc.sync.dma_start(value_pool[:, EARLY_VALUES:], vT[:, EARLY_VALUES:])
+        value_pool = sb("value_pool", [P, T], F32)
+        nc.sync.dma_start(value_pool[:], vT)
 
         token_scale = sb("token_scale", [P, N], F32)
         slot_scale = [sb(f"slot_scale{h}", [P, PACK], F32) for h in range(HALVES)]
@@ -147,10 +145,11 @@ def tile_attend_soft_cap_gate_topkq128n1024t4096_kernel(tc, q_words, q_scales, k
 
         nc.vector.tensor_copy(values[:, LEAD : N - TRAIL], value_pool[:].indirect(listed(LEAD, N - TRAIL)))
 
-        part_sum = sb("part_sum", [P, 3], F32)
+        part_sum = sb("part_sum", [P, PIECES], F32)
         probs = sb("probs", [P, N], F32)
         p_turned = [bank(f"p_turned{h}", [P, PACK, NQ]) for h in range(HALVES)]
-        for i, (first, last) in enumerate([(0, HALF), (HALF, HALF + PIECE), (HALF + PIECE, N)]):
+        for i in range(PIECES):
+            first, last = i * PIECE, (i + 1) * PIECE
             nc.scalar.activation(probs[:, first:last], negated[:, first:last], ACT.Exp, bias=neg_max[-1][:], scale=-1.0, accum_out=part_sum[:, i : i + 1])
             for block in range(first // P, last // P):
                 nc.tensor.transpose(p_turned[block // PACK][:, block % PACK, :], probs[:, block * P : (block + 1) * P], ident[:])
@@ -158,7 +157,7 @@ def tile_attend_soft_cap_gate_topkq128n1024t4096_kernel(tc, q_words, q_scales, k
         for n0, n1 in ((0, LEAD), (N - TRAIL, N)):
             nc.scalar.activation(values[:, n0:n1], value_pool[:].indirect(listed(n0, n1)), ACT.Copy)
 
-        part_copy = sb("part_copy", [P, 3], F32)
+        part_copy = sb("part_copy", [P, PIECES], F32)
         total = sb("total", [P, 1], F32)
         nc.scalar.activation(part_copy[:], part_sum[:], ACT.Copy, accum_out=total[:])
         v_grouped = [sb(f"v_grouped{h}", [P, DV, PACK], BF16) for h in range(HALVES)]

@@ -24,8 +24,8 @@ QUAD = 32
 PIECE = HALF // 2
 PIECES = N // PIECE
 SCALE_ROW = P - 1
-ZERO_PIECE = T // 4
-ODD_CUT = T // 8 + 1
+VECTOR_ZEROES = T // 8
+ZERO_PIECE = (T - VECTOR_ZEROES) // 4
 LEAD, TRAIL = 128, 192
 
 FLOPS = 2 * NQ * N * (D + DV)
@@ -65,27 +65,30 @@ def tile_attend_soft_cap_gate_topkq128n1024t4096_kernel(tc, q_words, q_scales, k
         nc.gpsimd.memset(ones[:], 1.0)
         scale_words = key_scale_pool[:].bitcast(I32)
         nc.gpsimd.memset(scale_words[QUAD : 2 * QUAD, :], 0)
-        for first in range(ZERO_PIECE, T, ZERO_PIECE):
+        for first in range(VECTOR_ZEROES, T, ZERO_PIECE):
             nc.gpsimd.memset(token_scale_pool[:SCALE_ROW, first : first + ZERO_PIECE], 0.0)
         ident = sb("ident", [P, P], F32)
         nc.gpsimd.memset(ident[:], 0.0)
-        for window in (scale_words[2 * QUAD :, :], token_scale_pool[:SCALE_ROW, :ZERO_PIECE]):
-            for columns in (slice(0, ODD_CUT), slice(ODD_CUT, ZERO_PIECE)):
+        for window in (scale_words[2 * QUAD :, :], token_scale_pool[:SCALE_ROW, :VECTOR_ZEROES]):
+            odd_cut = window.shape[1] // 2 + 1
+            for columns in (slice(0, odd_cut), slice(odd_cut, window.shape[1])):
                 nc.vector.memset(window[:, columns], 0)
+        column = sb("column", [P, QUAD], F32)
+        nc.vector.tensor_tensor_scan(column[:], ones[:], ones[:], 0.0, ALU.mult, ALU.add)
+        row = sb("row", [P, QUAD], F32)
+        nc.vector.transpose(row[:], column[:])
 
         key_scale_rows = sb("key_scale_rows", [P, N], U8)
         nc.vector.tensor_copy(key_scale_rows[:], key_scale_pool[:].indirect(offsets[:]))
-        column = sb("column", [P, QUAD], F32, "column")
-        nc.vector.tensor_tensor_scan(column[:], ones[:], ones[:], 0.0, ALU.mult, ALU.add)
         nc.vector.tensor_copy(scale_rows[0:QUAD, :N].bitcast(I32), key_scale_rows[0:QUAD, :].bitcast(I32))
-        row = sb("row", [P, QUAD], F32)
-        nc.vector.transpose(row[:], column[:])
         planes = sb("planes", [P, PASSES, N + NQ], U8)
         for quad in (0, 2, 1, 3):
             nc.sync.dma_start(
                 planes[quad * QUAD : quad * QUAD + PACK, :, :].bitcast(I32),
                 scale_rows[quad * PACK * PASSES : (quad + 1) * PACK * PASSES, :].bitcast(I32),
             )
+        gate_in = sb("gate_in", [P, DV], F32)
+        nc.sync.dma_start(gate_in[:], og[0])
         value_pool = sb("value_pool", [P, T], F32)
         nc.sync.dma_start(value_pool[:], vT)
 
@@ -94,13 +97,6 @@ def tile_attend_soft_cap_gate_topkq128n1024t4096_kernel(tc, q_words, q_scales, k
         nc.scalar.activation(token_scale[:], token_scale_pool[:].indirect(offsets[:]), ACT.Copy)
         for h in range(HALVES):
             nc.sync.dma_start(slot_scale[h][:], token_scale[SCALE_ROW:, h * HALF : (h + 1) * HALF].rearrange("o (p t) -> o p t", t=PACK))
-        gate_in = sb("gate_in", [P, DV], F32)
-        nc.sync.dma_start(gate_in[:], og[0])
-        distance = sb("distance", [P, QUAD], F32)
-        nc.scalar.activation(distance[:], column[:], ACT.Abs, scale=-1.0, bias=row[:, 0:1])
-        for first in range(0, P, QUAD):
-            rows = slice(first, first + QUAD)
-            nc.scalar.activation(ident[rows, rows], distance[rows, :], ACT.Relu, scale=-1.0, bias=1.0)
 
         width = PIECE // PACK
         capped_early = sb("capped_early", [P, PACK, P], F32)
@@ -139,6 +135,15 @@ def tile_attend_soft_cap_gate_topkq128n1024t4096_kernel(tc, q_words, q_scales, k
             gathered = [gather_keys(2 * h + part) for part in range(2)]
             for part in range(2):
                 score(2 * h + part, gathered[part])
+        distance = sb("distance", [P, QUAD], F32, "key_codes1")
+        nc.scalar.activation(distance[:], column[:], ACT.Abs, scale=-1.0, bias=row[:, 0:1])
+        for first in range(0, P, QUAD):
+            rows = slice(first, first + QUAD)
+            nc.scalar.activation(ident[rows, rows], distance[rows, :], ACT.Relu, scale=-1.0, bias=1.0)
+        gate_tanh = sb("gate_tanh", [P, DV], F32, "key_codes3")
+        nc.scalar.activation(gate_tanh[:], gate_in[:], ACT.Tanh, scale=0.5)
+        gate = sb("gate", [P, DV], F32)
+        nc.scalar.activation(gate[:], gate_tanh[:], ACT.Copy, scale=0.5, bias=0.5)
         row_max(0, negated[:, :HALF], capped_early[:].rearrange("q t p -> q (t p)"))
         for part in range(2):
             row_max(1 + part, negated[:, HALF:].rearrange("q (t p) -> q t p", p=P)[:, :, part * width : (part + 1) * width], capped[2 + part])
@@ -157,7 +162,7 @@ def tile_attend_soft_cap_gate_topkq128n1024t4096_kernel(tc, q_words, q_scales, k
         for n0, n1 in ((0, LEAD), (N - TRAIL, N)):
             nc.scalar.activation(values[:, n0:n1], value_pool[:].indirect(listed(n0, n1)), ACT.Copy)
 
-        part_copy = sb("part_copy", [P, PIECES], F32)
+        part_copy = sb("part_copy", [P, PIECES], F32, "value_pool")
         total = sb("total", [P, 1], F32)
         nc.scalar.activation(part_copy[:], part_sum[:], ACT.Copy, accum_out=total[:])
         v_grouped = [sb(f"v_grouped{h}", [P, DV, PACK], BF16) for h in range(HALVES)]
@@ -173,10 +178,6 @@ def tile_attend_soft_cap_gate_topkq128n1024t4096_kernel(tc, q_words, q_scales, k
             for u in range(2):
                 nc.tensor.transpose(v_turned[:, u, :], words[:, u::2], ident[:])
             nc.scalar.copy(v_grouped[h][:].bitcast(F32), v_turned[:].rearrange("p u e -> p e u"))
-        gate_tanh = values[:, N - 2 * DV :].bitcast(F32)
-        nc.scalar.activation(gate_tanh, gate_in[:], ACT.Tanh, scale=0.5)
-        gate = sb("gate", [P, DV], F32)
-        nc.scalar.activation(gate[:], gate_tanh, ACT.Copy, scale=0.5, bias=0.5)
 
         for h in range(HALVES):
             nc.vector.tensor_tensor(

@@ -24,7 +24,7 @@ QUAD = 32
 PIECE = HALF // 2
 PIECES = N // PIECE
 SCALE_ROW = P - 1
-VECTOR_ZEROES = T // 8
+VECTOR_ZEROES = 3 * T // 16
 ZERO_PIECE = (T - VECTOR_ZEROES) // 4
 LEAD, TRAIL = 128, 192
 
@@ -55,7 +55,7 @@ def tile_attend_soft_cap_gate_topkq128n1024t4096_kernel(tc, q_words, q_scales, k
         scale_rows = sb("scale_rows", [P, N + NQ], U8)
         nc.scalar.dma_start(scale_rows[0:QUAD, N:].bitcast(I32), q_scales[0].rearrange("o f q -> f o q").bitcast(I32))
         token_scale_pool = sb("token_scale_pool", [P, T], F32)
-        nc.scalar.dma_start(token_scale_pool[SCALE_ROW:, :], vs[0:1, :])
+        nc.sync.dma_start(token_scale_pool[SCALE_ROW:, :], vs[0:1, :])
         key_pool = sb("key_pool", [P, T], I32)
         nc.sync.dma_start(key_pool[:], k_words[0].rearrange("p t b -> p (t b)").bitcast(I32))
         q_codes = sb("q_codes", [P, PASSES, NQ], I32)
@@ -63,12 +63,12 @@ def tile_attend_soft_cap_gate_topkq128n1024t4096_kernel(tc, q_words, q_scales, k
 
         ones = sb("ones", [P, QUAD], F32)
         nc.gpsimd.memset(ones[:], 1.0)
+        ident = sb("ident", [P, P], F32)
+        nc.gpsimd.memset(ident[:], 0.0)
         scale_words = key_scale_pool[:].bitcast(I32)
         nc.gpsimd.memset(scale_words[QUAD : 2 * QUAD, :], 0)
         for first in range(VECTOR_ZEROES, T, ZERO_PIECE):
             nc.gpsimd.memset(token_scale_pool[:SCALE_ROW, first : first + ZERO_PIECE], 0.0)
-        ident = sb("ident", [P, P], F32)
-        nc.gpsimd.memset(ident[:], 0.0)
         for window in (scale_words[2 * QUAD :, :], token_scale_pool[:SCALE_ROW, :VECTOR_ZEROES]):
             odd_cut = window.shape[1] // 2 + 1
             for columns in (slice(0, odd_cut), slice(odd_cut, window.shape[1])):
@@ -77,6 +77,11 @@ def tile_attend_soft_cap_gate_topkq128n1024t4096_kernel(tc, q_words, q_scales, k
         nc.vector.tensor_tensor_scan(column[:], ones[:], ones[:], 0.0, ALU.mult, ALU.add)
         row = sb("row", [P, QUAD], F32)
         nc.vector.transpose(row[:], column[:])
+        distance = sb("distance", [P, QUAD], F32)
+        nc.scalar.activation(distance[:], column[:], ACT.Abs, scale=-1.0, bias=row[:, 0:1])
+        for first in range(0, P, QUAD):
+            rows = slice(first, first + QUAD)
+            nc.scalar.activation(ident[rows, rows], distance[rows, :], ACT.Relu, scale=-1.0, bias=1.0)
 
         key_scale_rows = sb("key_scale_rows", [P, N], U8)
         nc.vector.tensor_copy(key_scale_rows[:], key_scale_pool[:].indirect(offsets[:]))
@@ -135,11 +140,6 @@ def tile_attend_soft_cap_gate_topkq128n1024t4096_kernel(tc, q_words, q_scales, k
             gathered = [gather_keys(2 * h + part) for part in range(2)]
             for part in range(2):
                 score(2 * h + part, gathered[part])
-        distance = sb("distance", [P, QUAD], F32, "key_codes1")
-        nc.scalar.activation(distance[:], column[:], ACT.Abs, scale=-1.0, bias=row[:, 0:1])
-        for first in range(0, P, QUAD):
-            rows = slice(first, first + QUAD)
-            nc.scalar.activation(ident[rows, rows], distance[rows, :], ACT.Relu, scale=-1.0, bias=1.0)
         gate_tanh = sb("gate_tanh", [P, DV], F32, "key_codes3")
         nc.scalar.activation(gate_tanh[:], gate_in[:], ACT.Tanh, scale=0.5)
         gate = sb("gate", [P, DV], F32)

@@ -26,7 +26,7 @@ PIECES = N // PIECE
 SCALE_ROW = P - 1
 VECTOR_ZEROES = 3 * T // 16
 ZERO_PIECE = (T - VECTOR_ZEROES) // 4
-LEAD, TRAIL = 128, 192
+SCALAR_SHARE = 320
 
 FLOPS = 2 * NQ * N * (D + DV)
 BYTES = P * T * 4 + PASSES * 16 * T + DV * T * 4 + T * 4 + PASSES * (P * NQ * 4 + 16 * NQ) + 2 * NQ * DV * 4 + P * (N // 16) * 2
@@ -53,9 +53,9 @@ def tile_attend_soft_cap_gate_topkq128n1024t4096_kernel(tc, q_words, q_scales, k
             return offsets[:, n0 // 16 : n1 // 16]
 
         scale_rows = sb("scale_rows", [P, N + NQ], U8)
-        nc.scalar.dma_start(scale_rows[0:QUAD, N:].bitcast(I32), q_scales[0].rearrange("o f q -> f o q").bitcast(I32))
+        nc.sync.dma_start(scale_rows[0:QUAD, N:].bitcast(I32), q_scales[0].rearrange("o f q -> f o q").bitcast(I32))
         token_scale_pool = sb("token_scale_pool", [P, T], F32)
-        nc.sync.dma_start(token_scale_pool[SCALE_ROW:, :], vs[0:1, :])
+        nc.scalar.dma_start(token_scale_pool[SCALE_ROW:, :], vs[0:1, :])
         key_pool = sb("key_pool", [P, T], I32)
         nc.sync.dma_start(key_pool[:], k_words[0].rearrange("p t b -> p (t b)").bitcast(I32))
         q_codes = sb("q_codes", [P, PASSES, NQ], I32)
@@ -100,7 +100,7 @@ def tile_attend_soft_cap_gate_topkq128n1024t4096_kernel(tc, q_words, q_scales, k
         token_scale = sb("token_scale", [P, N], F32)
         slot_scale = [sb(f"slot_scale{h}", [P, PACK], F32) for h in range(HALVES)]
         nc.scalar.activation(token_scale[:], token_scale_pool[:].indirect(offsets[:]), ACT.Copy)
-        for h in range(HALVES):
+        for h in reversed(range(HALVES)):
             nc.sync.dma_start(slot_scale[h][:], token_scale[SCALE_ROW:, h * HALF : (h + 1) * HALF].rearrange("o (p t) -> o p t", t=PACK))
 
         width = PIECE // PACK
@@ -148,7 +148,7 @@ def tile_attend_soft_cap_gate_topkq128n1024t4096_kernel(tc, q_words, q_scales, k
         for part in range(2):
             row_max(1 + part, negated[:, HALF:].rearrange("q (t p) -> q t p", p=P)[:, :, part * width : (part + 1) * width], capped[2 + part])
 
-        nc.vector.tensor_copy(values[:, LEAD : N - TRAIL], value_pool[:].indirect(listed(LEAD, N - TRAIL)))
+        nc.vector.tensor_copy(values[:, : N - SCALAR_SHARE], value_pool[:].indirect(listed(0, N - SCALAR_SHARE)))
 
         part_sum = sb("part_sum", [P, PIECES], F32)
         probs = sb("probs", [P, N], F32)
@@ -159,8 +159,7 @@ def tile_attend_soft_cap_gate_topkq128n1024t4096_kernel(tc, q_words, q_scales, k
             for block in range(first // P, last // P):
                 nc.tensor.transpose(p_turned[block // PACK][:, block % PACK, :], probs[:, block * P : (block + 1) * P], ident[:])
 
-        for n0, n1 in ((0, LEAD), (N - TRAIL, N)):
-            nc.scalar.activation(values[:, n0:n1], value_pool[:].indirect(listed(n0, n1)), ACT.Copy)
+        nc.scalar.activation(values[:, N - SCALAR_SHARE :], value_pool[:].indirect(listed(N - SCALAR_SHARE, N)), ACT.Copy)
 
         part_copy = sb("part_copy", [P, PIECES], F32, "value_pool")
         total = sb("total", [P, 1], F32)

@@ -26,7 +26,7 @@ PIECES = N // PIECE
 SCALE_ROW = P - 1
 VECTOR_ZEROES = 3 * T // 16
 ZERO_PIECE = (T - VECTOR_ZEROES) // 4
-SCALAR_SHARE = 320
+SCALAR_SHARE = 192
 
 FLOPS = 2 * NQ * N * (D + DV)
 BYTES = P * T * 4 + PASSES * 16 * T + DV * T * 4 + T * 4 + PASSES * (P * NQ * 4 + 16 * NQ) + 2 * NQ * DV * 4 + P * (N // 16) * 2
@@ -148,12 +148,13 @@ def tile_attend_soft_cap_gate_topkq128n1024t4096_kernel(tc, q_words, q_scales, k
         for part in range(2):
             row_max(1 + part, negated[:, HALF:].rearrange("q (t p) -> q t p", p=P)[:, :, part * width : (part + 1) * width], capped[2 + part])
 
-        nc.vector.tensor_copy(values[:, : N - SCALAR_SHARE], value_pool[:].indirect(listed(0, N - SCALAR_SHARE)))
+        for first, last in ((0, HALF), (HALF, N - SCALAR_SHARE)):
+            nc.vector.tensor_copy(values[:, first:last], value_pool[:].indirect(listed(first, last)))
 
         part_sum = sb("part_sum", [P, PIECES], F32)
         probs = sb("probs", [P, N], F32)
         p_turned = [bank(f"p_turned{h}", [P, PACK, NQ]) for h in range(HALVES)]
-        for i in range(PIECES):
+        for i in reversed(range(PIECES)):
             first, last = i * PIECE, (i + 1) * PIECE
             nc.scalar.activation(probs[:, first:last], negated[:, first:last], ACT.Exp, bias=neg_max[-1][:], scale=-1.0, accum_out=part_sum[:, i : i + 1])
             for block in range(first // P, last // P):

@@ -60,6 +60,8 @@ def tile_attend_soft_cap_gate_topkq128n1024t4096_kernel(tc, q_words, q_scales, k
         nc.sync.dma_start(key_pool[:], k_words[0].rearrange("p t b -> p (t b)").bitcast(I32))
         q_codes = sb("q_codes", [P, PASSES, NQ], I32)
         nc.sync.dma_start(q_codes[:], q_words[0].rearrange("o p q r -> p o (q r)").bitcast(I32))
+        gate_in = sb("gate_in", [P, DV], F32)
+        nc.sync.dma_start(gate_in[:], og[0])
 
         ones = sb("ones", [P, QUAD], F32)
         nc.gpsimd.memset(ones[:], 1.0)
@@ -92,8 +94,6 @@ def tile_attend_soft_cap_gate_topkq128n1024t4096_kernel(tc, q_words, q_scales, k
                 planes[quad * QUAD : quad * QUAD + PACK, :, :].bitcast(I32),
                 scale_rows[quad * PACK * PASSES : (quad + 1) * PACK * PASSES, :].bitcast(I32),
             )
-        gate_in = sb("gate_in", [P, DV], F32)
-        nc.sync.dma_start(gate_in[:], og[0])
         value_pool = sb("value_pool", [P, T], F32)
         nc.sync.dma_start(value_pool[:], vT)
 
@@ -103,52 +103,64 @@ def tile_attend_soft_cap_gate_topkq128n1024t4096_kernel(tc, q_words, q_scales, k
         for h in reversed(range(HALVES)):
             nc.sync.dma_start(slot_scale[h][:], token_scale[SCALE_ROW:, h * HALF : (h + 1) * HALF].rearrange("o (p t) -> o p t", t=PACK))
 
-        width = PIECE // PACK
-        capped_early = sb("capped_early", [P, PACK, P], F32)
-        capped_late = [sb(f"capped_late{part}", [P, PACK, width], F32) for part in range(2)]
-        capped = [capped_early[:, :, :width], capped_early[:, :, width:], capped_late[0][:], capped_late[1][:]]
+        capped = [sb(f"capped{h}", [P, PACK, P], F32) for h in range(HALVES)]
         negated = sb("negated", [P, N], F32)
         value_words = sb("value_words", [P, N // 2], F32)
         values = value_words[:].bitcast(BF16)
-        neg_max = [sb(f"neg_max{i}", [P, 1], F32) for i in range(3)]
+        neg_max = [sb(f"neg_max{i}", [P, 1], F32) for i in range(HALVES)]
 
         def gather_keys(i):
             pairs = sb(f"key_pairs{i}", [P, PIECE], U32, f"key_pairs{i % 2}")
             nc.vector.tensor_copy(pairs[:], key_pool[:].bitcast(U32).indirect(listed(i * PIECE, (i + 1) * PIECE)))
             return pairs
 
-        def score(i, pairs):
-            codes = sb(f"key_codes{i}", [P, PASSES, 2 * PIECE], U8)
-            nc.vector.tensor_copy(codes[:].bitcast(U16), pairs[:].bitcast(U16).rearrange("p (n o) -> p o n", o=PASSES))
-            scores = bank(f"scores{i}", [P, PIECE])
+        def part_keys(pairs, first, last):
+            codes = sb(f"key_codes{first}", [P, PASSES, 2 * (last - first)], U8)
+            words = pairs[:, first % PIECE : first % PIECE + last - first]
+            nc.vector.tensor_copy(codes[:].bitcast(U16), words.bitcast(U16).rearrange("p (n o) -> p o n", o=PASSES))
+            return codes
+
+        def multiply(scores, codes, first, last):
             for o in range(PASSES):
                 nc.tensor.matmul_mx(
-                    out=scores[:],
+                    out=scores,
                     lhsT=q_codes[:, o, :].bitcast(FP8X4),
                     lhsT_scale=planes[:, o, N:],
                     rhs=codes[:, o, :].bitcast(FP4X4),
-                    rhs_scale=planes[:, o, i * PIECE : (i + 1) * PIECE],
+                    rhs_scale=planes[:, o, first:last],
                     start=(o == 0),
                     stop=(o == PASSES - 1),
                 )
-            nc.scalar.activation(capped[i], scores[:].rearrange("q (p t) -> q t p", t=PACK), ACT.Tanh, scale=1.0 / CAP)
 
-        def row_max(i, target, source):
-            nc.vector.tensor_scalar(target, source, -CAP, neg_max[i - 1][:] if i else None, ALU.mult, ALU.min, accum_out=neg_max[i][:])
+        def cap(scores, first, last):
+            places = capped[first // HALF][:, :, first % HALF // PACK : (last - 1) % HALF // PACK + 1]
+            nc.scalar.activation(places, scores.rearrange("q (p t) -> q t p", t=PACK), ACT.Tanh, scale=1.0 / CAP)
 
         for h in range(HALVES):
             gathered = [gather_keys(2 * h + part) for part in range(2)]
-            for part in range(2):
-                score(2 * h + part, gathered[part])
-        gate_tanh = sb("gate_tanh", [P, DV], F32, "key_codes3")
+            first = h * HALF
+            scores = bank(f"scores{2 * h}", [P, PIECE])
+            for group in range(0, PIECE, P):
+                multiply(scores[:, group : group + P], part_keys(gathered[0], first + group, first + group + P), first + group, first + group + P)
+            cap(scores[:], first, first + PIECE)
+            first = first + PIECE
+            codes = part_keys(gathered[1], first, first + PIECE)
+            width = PIECE if h == 0 else P
+            for group in range(0, PIECE, width):
+                scores = bank(f"scores{2 * h + 1}_{group}", [P, width])
+                multiply(scores[:], codes[:, :, 2 * group : 2 * (group + width)], first + group, first + group + width)
+                cap(scores[:], first + group, first + group + width)
+        gate_tanh = sb("gate_tanh", [P, DV], F32, f"key_codes{N - PIECE}")
         nc.scalar.activation(gate_tanh[:], gate_in[:], ACT.Tanh, scale=0.5)
         gate = sb("gate", [P, DV], F32)
         nc.scalar.activation(gate[:], gate_tanh[:], ACT.Copy, scale=0.5, bias=0.5)
-        row_max(0, negated[:, :HALF], capped_early[:].rearrange("q t p -> q (t p)"))
-        for part in range(2):
-            row_max(1 + part, negated[:, HALF:].rearrange("q (t p) -> q t p", p=P)[:, :, part * width : (part + 1) * width], capped[2 + part])
+        for h in range(HALVES):
+            nc.vector.tensor_scalar(
+                negated[:, h * HALF : (h + 1) * HALF], capped[h][:].rearrange("q t p -> q (t p)"), -CAP, neg_max[h - 1][:] if h else None,
+                ALU.mult, ALU.min, accum_out=neg_max[h][:],
+            )
 
-        for first, last in ((0, HALF), (HALF, N - SCALAR_SHARE)):
+        for first, last in ((HALF, N), (SCALAR_SHARE, HALF)):
             nc.vector.tensor_copy(values[:, first:last], value_pool[:].indirect(listed(first, last)))
 
         part_sum = sb("part_sum", [P, PIECES], F32)
@@ -160,46 +172,45 @@ def tile_attend_soft_cap_gate_topkq128n1024t4096_kernel(tc, q_words, q_scales, k
             for block in range(first // P, last // P):
                 nc.tensor.transpose(p_turned[block // PACK][:, block % PACK, :], probs[:, block * P : (block + 1) * P], ident[:])
 
-        nc.scalar.activation(values[:, N - SCALAR_SHARE :], value_pool[:].indirect(listed(N - SCALAR_SHARE, N)), ACT.Copy)
+        nc.scalar.activation(values[:, :SCALAR_SHARE], value_pool[:].indirect(listed(0, SCALAR_SHARE)), ACT.Copy)
 
         part_copy = sb("part_copy", [P, PIECES], F32, "value_pool")
         total = sb("total", [P, 1], F32)
         nc.scalar.activation(part_copy[:], part_sum[:], ACT.Copy, accum_out=total[:])
-        v_grouped = [sb(f"v_grouped{h}", [P, DV, PACK], BF16) for h in range(HALVES)]
-        w_grouped = sb("w_grouped", [P, HALVES, NQ, PACK], BF16)
-        v_codes = [sb(f"v_codes{h}", [P, DV], U32) for h in range(HALVES)]
-        v_plane = [sb(f"v_plane{h}", [P, DV], U8) for h in range(HALVES)]
-        w_codes = sb("w_codes", [P, HALVES, NQ], U32)
-        w_plane = sb("w_plane", [P, HALVES, NQ], U8)
+        grouped = [sb(f"grouped{i}", [P, NQ + DV, PACK], BF16) for i in range(HALVES)]
+        slot_codes = [sb(f"slot_codes{i}", [P, NQ + DV], U32) for i in range(HALVES)]
+        slot_plane = [sb(f"slot_plane{i}", [P, NQ + DV], U8) for i in range(HALVES)]
 
-        for h in range(HALVES):
+        for h in reversed(range(HALVES)):
             words = values[:, h * HALF : (h + 1) * HALF].bitcast(F32)
-            v_turned = bank(f"v_turned{h}", [P, 2, DV], f"scores{h}")
+            v_turned = bank(f"v_turned{h}", [P, 2, DV], f"scores{2 * h}")
             for u in range(2):
                 nc.tensor.transpose(v_turned[:, u, :], words[:, u::2], ident[:])
-            nc.scalar.copy(v_grouped[h][:].bitcast(F32), v_turned[:].rearrange("p u e -> p e u"))
+            nc.scalar.copy(grouped[h][:, NQ:].bitcast(F32), v_turned[:].rearrange("p u e -> p e u"))
 
-        for h in range(HALVES):
+        for h in reversed(range(HALVES)):
             nc.vector.tensor_tensor(
-                w_grouped[:, h], p_turned[h][:].rearrange("p t q -> p q t"),
+                grouped[h][:, :NQ], p_turned[h][:].rearrange("p t q -> p q t"),
                 slot_scale[h][:].unsqueeze(1).to_broadcast([P, NQ, PACK]), ALU.mult,
             )
-        for h in range(HALVES):
-            nc.vector.quantize_mx(out=w_codes[:, h].bitcast(FP8X4), scales=w_plane[:, h], in_=w_grouped[:, h].rearrange("p q t -> p (q t)"))
-            nc.vector.quantize_mx(out=v_codes[h][:].bitcast(FP8X4), scales=v_plane[h][:], in_=v_grouped[h][:].rearrange("p x t -> p (x t)"))
-        inv_total = sb("inv_total", [P, 1], F32, "v_grouped1")
+        for i in reversed(range(HALVES)):
+            for columns in (slice(0, NQ), slice(NQ, NQ + DV)):
+                nc.vector.quantize_mx(
+                    out=slot_codes[i][:, columns].bitcast(FP8X4), scales=slot_plane[i][:, columns], in_=grouped[i][:, columns].rearrange("p x t -> p (x t)")
+                )
+        inv_total = sb("inv_total", [P, 1], F32, "grouped0")
         nc.vector.reciprocal(inv_total[:], total[:])
 
         acc = bank("acc", [P, DV])
-        for h in range(HALVES):
+        for h in reversed(range(HALVES)):
             nc.tensor.matmul_mx(
                 out=acc[:],
-                lhsT=w_codes[:, h].bitcast(FP8X4),
-                lhsT_scale=w_plane[:, h],
-                rhs=v_codes[h][:].bitcast(FP8X4),
-                rhs_scale=v_plane[h][:],
-                start=(h == 0),
-                stop=(h == HALVES - 1),
+                lhsT=slot_codes[h][:, :NQ].bitcast(FP8X4),
+                lhsT_scale=slot_plane[h][:, :NQ],
+                rhs=slot_codes[h][:, NQ:].bitcast(FP8X4),
+                rhs_scale=slot_plane[h][:, NQ:],
+                start=(h == HALVES - 1),
+                stop=(h == 0),
             )
         result = sb("result", [P, DV], F32)
         nc.vector.scalar_tensor_tensor(result[:], acc[:], inv_total[:], gate[:], ALU.mult, ALU.mult)

@@ -160,8 +160,8 @@ def tile_attend_soft_cap_gate_topkq128n1024t4096_kernel(tc, q_words, q_scales, k
                 ALU.mult, ALU.min, accum_out=neg_max[h][:],
             )
 
-        for first, last in ((HALF, N), (SCALAR_SHARE, HALF)):
-            nc.vector.tensor_copy(values[:, first:last], value_pool[:].indirect(listed(first, last)))
+        nc.vector.tensor_copy(values[:, HALF:].rearrange("f (u p e) -> f p u e", u=2, e=2), value_pool[:].indirect(listed(HALF, N)))
+        nc.vector.tensor_copy(values[:, SCALAR_SHARE:HALF], value_pool[:].indirect(listed(SCALAR_SHARE, HALF)))
 
         part_sum = sb("part_sum", [P, PIECES], F32)
         probs = sb("probs", [P, N], F32)
@@ -185,7 +185,7 @@ def tile_attend_soft_cap_gate_topkq128n1024t4096_kernel(tc, q_words, q_scales, k
             words = values[:, h * HALF : (h + 1) * HALF].bitcast(F32)
             v_turned = bank(f"v_turned{h}", [P, 2, DV], f"scores{2 * h}")
             for u in range(2):
-                nc.tensor.transpose(v_turned[:, u, :], words[:, u::2], ident[:])
+                nc.tensor.transpose(v_turned[:, u, :], words[:, u * P : (u + 1) * P] if h else words[:, u::2], ident[:])
             nc.scalar.copy(grouped[h][:, NQ:].bitcast(F32), v_turned[:].rearrange("p u e -> p e u"))
 
         for h in reversed(range(HALVES)):

@@ -136,21 +136,20 @@ def tile_attend_soft_cap_gate_topkq128n1024t4096_kernel(tc, q_words, q_scales, k
             places = capped[first // HALF][:, :, first % HALF // PACK : (last - 1) % HALF // PACK + 1]
             nc.scalar.activation(places, scores.rearrange("q (p t) -> q t p", t=PACK), ACT.Tanh, scale=1.0 / CAP)
 
-        for h in range(HALVES):
-            gathered = [gather_keys(2 * h + part) for part in range(2)]
-            first = h * HALF
-            scores = bank(f"scores{2 * h}", [P, PIECE])
-            for group in range(0, PIECE, P):
-                multiply(scores[:, group : group + P], part_keys(gathered[0], first + group, first + group + P), first + group, first + group + P)
-            cap(scores[:], first, first + PIECE)
-            first = first + PIECE
-            codes = part_keys(gathered[1], first, first + PIECE)
-            width = PIECE if h == 0 else P
-            for group in range(0, PIECE, width):
-                scores = bank(f"scores{2 * h + 1}_{group}", [P, width])
-                multiply(scores[:], codes[:, :, 2 * group : 2 * (group + width)], first + group, first + group + width)
-                cap(scores[:], first + group, first + group + width)
-        gate_tanh = sb("gate_tanh", [P, DV], F32, f"key_codes{N - PIECE}")
+        gathered = [gather_keys(part) for part in range(2)]
+        scores = bank("scores0", [P, PIECE])
+        for first in range(0, PIECE, P):
+            multiply(scores[:, first : first + P], part_keys(gathered[0], first, first + P), first, first + P)
+        cap(scores[:], 0, PIECE)
+        scores = bank("scores1", [P, PIECE])
+        multiply(scores[:], part_keys(gathered[1], PIECE, HALF), PIECE, HALF)
+        cap(scores[:], PIECE, HALF)
+        gathered = [gather_keys(2 + part) for part in range(2)]
+        for first in range(HALF, N, P):
+            scores = bank(f"scores_from{first}", [P, P], f"scores{(first // P - 2) % 5}")
+            multiply(scores[:], part_keys(gathered[first // PIECE - 2], first, first + P), first, first + P)
+            cap(scores[:], first, first + P)
+        gate_tanh = sb("gate_tanh", [P, DV], F32, f"key_codes{N - P}")
         nc.scalar.activation(gate_tanh[:], gate_in[:], ACT.Tanh, scale=0.5)
         gate = sb("gate", [P, DV], F32)
         nc.scalar.activation(gate[:], gate_tanh[:], ACT.Copy, scale=0.5, bias=0.5)

@@ -26,7 +26,7 @@ PIECES = N // PIECE
 SCALE_ROW = P - 1
 VECTOR_ZEROES = 3 * T // 16
 ZERO_PIECE = (T - VECTOR_ZEROES) // 4
-SCALAR_SHARE = 192
+SCALAR_SHARE = 224
 
 FLOPS = 2 * NQ * N * (D + DV)
 BYTES = P * T * 4 + PASSES * 16 * T + DV * T * 4 + T * 4 + PASSES * (P * NQ * 4 + 16 * NQ) + 2 * NQ * DV * 4 + P * (N // 16) * 2
@@ -117,7 +117,9 @@ def tile_attend_soft_cap_gate_topkq128n1024t4096_kernel(tc, q_words, q_scales, k
         def part_keys(pairs, first, last):
             codes = sb(f"key_codes{first}", [P, PASSES, 2 * (last - first)], U8)
             words = pairs[:, first % PIECE : first % PIECE + last - first]
-            nc.vector.tensor_copy(codes[:].bitcast(U16), words.bitcast(U16).rearrange("p (n o) -> p o n", o=PASSES))
+            nc.vector.tensor_copy(
+                codes[:].bitcast(U16).rearrange("p o (h n) -> p h o n", h=2), words.bitcast(U16).rearrange("p (h n o) -> p h o n", h=2, o=PASSES)
+            )
             return codes
 
         def multiply(scores, codes, first, last):
@@ -162,20 +164,19 @@ def tile_attend_soft_cap_gate_topkq128n1024t4096_kernel(tc, q_words, q_scales, k
         nc.vector.tensor_copy(values[:, HALF:].rearrange("f (u p e) -> f p u e", u=2, e=2), value_pool[:].indirect(listed(HALF, N)))
         nc.vector.tensor_copy(values[:, SCALAR_SHARE:HALF], value_pool[:].indirect(listed(SCALAR_SHARE, HALF)))
 
-        part_sum = sb("part_sum", [P, PIECES], F32)
+        part_sum = [sb(f"part_sum{h}", [P, 1], F32) for h in range(HALVES)]
         probs = sb("probs", [P, N], F32)
         p_turned = [bank(f"p_turned{h}", [P, PACK, NQ]) for h in range(HALVES)]
-        for i in reversed(range(PIECES)):
-            first, last = i * PIECE, (i + 1) * PIECE
-            nc.scalar.activation(probs[:, first:last], negated[:, first:last], ACT.Exp, bias=neg_max[-1][:], scale=-1.0, accum_out=part_sum[:, i : i + 1])
-            for block in range(first // P, last // P):
-                nc.tensor.transpose(p_turned[block // PACK][:, block % PACK, :], probs[:, block * P : (block + 1) * P], ident[:])
+        for h in reversed(range(HALVES)):
+            columns = slice(h * HALF, (h + 1) * HALF)
+            nc.scalar.activation(probs[:, columns], negated[:, columns], ACT.Exp, bias=neg_max[-1][:], scale=-1.0, accum_out=part_sum[h][:])
+            for block in range(PACK):
+                nc.tensor.transpose(p_turned[h][:, block, :], probs[:, h * HALF + block * P : h * HALF + (block + 1) * P], ident[:])
 
         nc.scalar.activation(values[:, :SCALAR_SHARE], value_pool[:].indirect(listed(0, SCALAR_SHARE)), ACT.Copy)
 
-        part_copy = sb("part_copy", [P, PIECES], F32, "value_pool")
-        total = sb("total", [P, 1], F32)
-        nc.scalar.activation(part_copy[:], part_sum[:], ACT.Copy, accum_out=total[:])
+        total = sb("total", [P, 1], F32, "value_pool")
+        nc.scalar.activation(total[:], part_sum[0][:], ACT.Identity, bias=part_sum[1][:])
         grouped = [sb(f"grouped{i}", [P, NQ + DV, PACK], BF16) for i in range(HALVES)]
         slot_codes = [sb(f"slot_codes{i}", [P, NQ + DV], U32) for i in range(HALVES)]
         slot_plane = [sb(f"slot_plane{i}", [P, NQ + DV], U8) for i in range(HALVES)]

from contextlib import ExitStack

import concourse.mybir as mybir

F32 = mybir.dt.float32
BF16 = mybir.dt.bfloat16
I32 = mybir.dt.int32
U32 = mybir.dt.uint32
U16 = mybir.dt.uint16
U8 = mybir.dt.uint8
FP8X4 = mybir.dt.float8_e4m3fn_x4
FP4X4 = mybir.dt.float4_e2m1fn_x4
ACT = mybir.ActivationFunctionType
ALU = mybir.AluOpType

P = 128
N, T, D, DV, NQ = 1024, 4096, 1024, 128, 128
CAP = 2.0
PACK = 4
HALF = P * PACK
HALVES = N // HALF
PASSES = D // HALF
QUAD = 32
PIECE = HALF // 2
PIECES = N // PIECE
SCALE_ROW = P - 1
VECTOR_ZEROES = 3 * T // 16
ZERO_PIECE = (T - VECTOR_ZEROES) // 4
SCALAR_SHARE = 224

FLOPS = 2 * NQ * N * (D + DV)
BYTES = P * T * 4 + PASSES * 16 * T + DV * T * 4 + T * 4 + PASSES * (P * NQ * 4 + 16 * NQ) + 2 * NQ * DV * 4 + P * (N // 16) * 2


def tile_attend_soft_cap_gate_topkq128n1024t4096_kernel(tc, q_words, q_scales, k_words, k_scales, vT, vs, og, offs, out):
    nc = tc.nc
    with ExitStack() as ctx:
        held = ctx.enter_context(tc.tile_pool(name="held", bufs=1))
        psum = ctx.enter_context(tc.psum_pool(name="psum", bufs=1))

        def sb(name, shape, dtype, tag=""):
            return held.tile(shape, dtype, name=name, tag=tag or name, align_bytes=64)

        def bank(name, shape, tag=""):
            return psum.tile(shape, F32, name=name, tag=tag or name)

        key_scale_pool = sb("key_scale_pool", [P, T], U8)
        nc.sync.dma_start(key_scale_pool[0:QUAD, :].bitcast(I32), k_scales.rearrange("o f t -> f o t").bitcast(I32))
        offsets = held.tile([P, N // 16], U16, name="offsets")
        nc.sync.dma_start(offsets[:], offs)

        def listed(n0, n1):
            return offsets[:, n0 // 16 : n1 // 16]

        scale_rows = sb("scale_rows", [P, N + NQ], U8)
        nc.sync.dma_start(scale_rows[0:QUAD, N:].bitcast(I32), q_scales[0].rearrange("o f q -> f o q").bitcast(I32))
        token_scale_pool = sb("token_scale_pool", [P, T], F32)
        nc.scalar.dma_start(token_scale_pool[SCALE_ROW:, :], vs[0:1, :])
        key_pool = sb("key_pool", [P, T], I32)
        nc.sync.dma_start(key_pool[:], k_words[0].rearrange("p t b -> p (t b)").bitcast(I32))
        q_codes = sb("q_codes", [P, PASSES, NQ], I32)
        nc.sync.dma_start(q_codes[:], q_words[0].rearrange("o p q r -> p o (q r)").bitcast(I32))
        gate_in = sb("gate_in", [P, DV], F32)
        nc.sync.dma_start(gate_in[:], og[0])

        ones = sb("ones", [P, QUAD], F32)
        nc.gpsimd.memset(ones[:], 1.0)
        ident = sb("ident", [P, P], F32)
        nc.gpsimd.memset(ident[:], 0.0)
        scale_words = key_scale_pool[:].bitcast(I32)
        nc.gpsimd.memset(scale_words[QUAD : 2 * QUAD, :], 0)
        for first in range(VECTOR_ZEROES, T, ZERO_PIECE):
            nc.gpsimd.memset(token_scale_pool[:SCALE_ROW, first : first + ZERO_PIECE], 0.0)
        for window in (scale_words[2 * QUAD :, :], token_scale_pool[:SCALE_ROW, :VECTOR_ZEROES]):
            odd_cut = window.shape[1] // 2 + 1
            for columns in (slice(0, odd_cut), slice(odd_cut, window.shape[1])):
                nc.vector.memset(window[:, columns], 0)
        column = sb("column", [P, QUAD], F32)
        nc.vector.tensor_tensor_scan(column[:], ones[:], ones[:], 0.0, ALU.mult, ALU.add)
        row = sb("row", [P, QUAD], F32)
        nc.vector.transpose(row[:], column[:])
        distance = sb("distance", [P, QUAD], F32)
        nc.scalar.activation(distance[:], column[:], ACT.Abs, scale=-1.0, bias=row[:, 0:1])
        for first in range(0, P, QUAD):
            rows = slice(first, first + QUAD)
            nc.scalar.activation(ident[rows, rows], distance[rows, :], ACT.Relu, scale=-1.0, bias=1.0)

        key_scale_rows = sb("key_scale_rows", [P, N], U8)
        nc.vector.tensor_copy(key_scale_rows[:], key_scale_pool[:].indirect(offsets[:]))
        nc.vector.tensor_copy(scale_rows[0:QUAD, :N].bitcast(I32), key_scale_rows[0:QUAD, :].bitcast(I32))
        planes = sb("planes", [P, PASSES, N + NQ], U8)
        for quad in (0, 2, 1, 3):
            nc.sync.dma_start(
                planes[quad * QUAD : quad * QUAD + PACK, :, :].bitcast(I32),
                scale_rows[quad * PACK * PASSES : (quad + 1) * PACK * PASSES, :].bitcast(I32),
            )
        value_pool = sb("value_pool", [P, T], F32)
        nc.sync.dma_start(value_pool[:], vT)

        token_scale = sb("token_scale", [P, N], F32)
        slot_scale = [sb(f"slot_scale{h}", [P, PACK], F32) for h in range(HALVES)]
        nc.scalar.activation(token_scale[:], token_scale_pool[:].indirect(offsets[:]), ACT.Copy)
        for h in reversed(range(HALVES)):
            nc.sync.dma_start(slot_scale[h][:], token_scale[SCALE_ROW:, h * HALF : (h + 1) * HALF].rearrange("o (p t) -> o p t", t=PACK))

        capped = [sb(f"capped{h}", [P, PACK, P], F32) for h in range(HALVES)]
        negated = sb("negated", [P, N], F32)
        value_words = sb("value_words", [P, N // 2], F32)
        values = value_words[:].bitcast(BF16)
        neg_max = [sb(f"neg_max{i}", [P, 1], F32) for i in range(HALVES)]

        def gather_keys(i):
            pairs = sb(f"key_pairs{i}", [P, PIECE], U32, f"key_pairs{i % 2}")
            nc.vector.tensor_copy(pairs[:], key_pool[:].bitcast(U32).indirect(listed(i * PIECE, (i + 1) * PIECE)))
            return pairs

        def part_keys(pairs, first, last):
            codes = sb(f"key_codes{first}", [P, PASSES, 2 * (last - first)], U8)
            words = pairs[:, first % PIECE : first % PIECE + last - first]
            nc.vector.tensor_copy(
                codes[:].bitcast(U16).rearrange("p o (h n) -> p h o n", h=2), words.bitcast(U16).rearrange("p (h n o) -> p h o n", h=2, o=PASSES)
            )
            return codes

        def multiply(scores, codes, first, last):
            for o in range(PASSES):
                nc.tensor.matmul_mx(
                    out=scores,
                    lhsT=q_codes[:, o, :].bitcast(FP8X4),
                    lhsT_scale=planes[:, o, N:],
                    rhs=codes[:, o, :].bitcast(FP4X4),
                    rhs_scale=planes[:, o, first:last],
                    start=(o == 0),
                    stop=(o == PASSES - 1),
                )

        def cap(scores, first, last):
            places = capped[first // HALF][:, :, first % HALF // PACK : (last - 1) % HALF // PACK + 1]
            nc.scalar.activation(places, scores.rearrange("q (p t) -> q t p", t=PACK), ACT.Tanh, scale=1.0 / CAP)

        gathered = [gather_keys(part) for part in range(2)]
        scores = bank("scores0", [P, PIECE])
        for first in range(0, PIECE, P):
            multiply(scores[:, first : first + P], part_keys(gathered[0], first, first + P), first, first + P)
        cap(scores[:], 0, PIECE)
        scores = bank("scores1", [P, PIECE])
        multiply(scores[:], part_keys(gathered[1], PIECE, HALF), PIECE, HALF)
        cap(scores[:], PIECE, HALF)
        gathered = [gather_keys(2 + part) for part in range(2)]
        for first in range(HALF, N, P):
            scores = bank(f"scores_from{first}", [P, P], f"scores{(first // P - 2) % 5}")
            multiply(scores[:], part_keys(gathered[first // PIECE - 2], first, first + P), first, first + P)
            cap(scores[:], first, first + P)
        gate_tanh = sb("gate_tanh", [P, DV], F32, f"key_codes{N - P}")
        nc.scalar.activation(gate_tanh[:], gate_in[:], ACT.Tanh, scale=0.5)
        gate = sb("gate", [P, DV], F32)
        nc.scalar.activation(gate[:], gate_tanh[:], ACT.Copy, scale=0.5, bias=0.5)
        for h in range(HALVES):
            nc.vector.tensor_scalar(
                negated[:, h * HALF : (h + 1) * HALF], capped[h][:].rearrange("q t p -> q (t p)"), -CAP, neg_max[h - 1][:] if h else None,
                ALU.mult, ALU.min, accum_out=neg_max[h][:],
            )

        nc.vector.tensor_copy(values[:, HALF:].rearrange("f (u p e) -> f p u e", u=2, e=2), value_pool[:].indirect(listed(HALF, N)))
        nc.vector.tensor_copy(values[:, SCALAR_SHARE:HALF], value_pool[:].indirect(listed(SCALAR_SHARE, HALF)))

        part_sum = [sb(f"part_sum{h}", [P, 1], F32) for h in range(HALVES)]
        probs = sb("probs", [P, N], F32)
        p_turned = [bank(f"p_turned{h}", [P, PACK, NQ]) for h in range(HALVES)]
        for h in reversed(range(HALVES)):
            columns = slice(h * HALF, (h + 1) * HALF)
            nc.scalar.activation(probs[:, columns], negated[:, columns], ACT.Exp, bias=neg_max[-1][:], scale=-1.0, accum_out=part_sum[h][:])
            for block in range(PACK):
                nc.tensor.transpose(p_turned[h][:, block, :], probs[:, h * HALF + block * P : h * HALF + (block + 1) * P], ident[:])

        nc.scalar.activation(values[:, :SCALAR_SHARE], value_pool[:].indirect(listed(0, SCALAR_SHARE)), ACT.Copy)

        total = sb("total", [P, 1], F32, "value_pool")
        nc.scalar.activation(total[:], part_sum[0][:], ACT.Identity, bias=part_sum[1][:])
        grouped = [sb(f"grouped{i}", [P, NQ + DV, PACK], BF16) for i in range(HALVES)]
        slot_codes = [sb(f"slot_codes{i}", [P, NQ + DV], U32) for i in range(HALVES)]
        slot_plane = [sb(f"slot_plane{i}", [P, NQ + DV], U8) for i in range(HALVES)]

        for h in reversed(range(HALVES)):
            words = values[:, h * HALF : (h + 1) * HALF].bitcast(F32)
            v_turned = bank(f"v_turned{h}", [P, 2, DV], f"scores{2 * h}")
            for u in range(2):
                nc.tensor.transpose(v_turned[:, u, :], words[:, u * P : (u + 1) * P] if h else words[:, u::2], ident[:])
            nc.scalar.copy(grouped[h][:, NQ:].bitcast(F32), v_turned[:].rearrange("p u e -> p e u"))

        for h in reversed(range(HALVES)):
            nc.vector.tensor_tensor(
                grouped[h][:, :NQ], p_turned[h][:].rearrange("p t q -> p q t"),
                slot_scale[h][:].unsqueeze(1).to_broadcast([P, NQ, PACK]), ALU.mult,
            )
        for i in reversed(range(HALVES)):
            for columns in (slice(0, NQ), slice(NQ, NQ + DV)):
                nc.vector.quantize_mx(
                    out=slot_codes[i][:, columns].bitcast(FP8X4), scales=slot_plane[i][:, columns], in_=grouped[i][:, columns].rearrange("p x t -> p (x t)")
                )
        inv_total = sb("inv_total", [P, 1], F32, "grouped0")
        nc.vector.reciprocal(inv_total[:], total[:])

        acc = bank("acc", [P, DV])
        for h in reversed(range(HALVES)):
            nc.tensor.matmul_mx(
                out=acc[:],
                lhsT=slot_codes[h][:, :NQ].bitcast(FP8X4),
                lhsT_scale=slot_plane[h][:, :NQ],
                rhs=slot_codes[h][:, NQ:].bitcast(FP8X4),
                rhs_scale=slot_plane[h][:, NQ:],
                start=(h == HALVES - 1),
                stop=(h == 0),
            )
        result = sb("result", [P, DV], F32)
        nc.vector.scalar_tensor_tensor(result[:], acc[:], inv_total[:], gate[:], ALU.mult, ALU.mult)
        nc.sync.dma_start(out[0], result[:])
